import numpy as np, ml_dtypes
CORES = [5,29,101,125,133,157,229,253]
N = 8
BF = ml_dtypes.bfloat16
def gentries(a):
    return np.ascontiguousarray(a.reshape(8, 16, -1).transpose(0, 2, 1)).reshape(8, -1)
def gtable(e):
    e = np.asarray(e); return np.ascontiguousarray(e.reshape(8, -1, 16).transpose(0, 2, 1)).reshape(128, -1).astype(np.int32)
S, C, B, U, RO, Q = 2048, 2048, 96, 32, 3, 10
L = B + U
def parts(rng):
    sk = (256 * (0.25 + 0.75 * rng.random((N, 8, 1, C))) * rng.random((N, 8, 16, C))).astype(np.int64); sk = np.minimum(sk, 255); sk[..., C - 1] = 0
    oc = np.where(rng.random((N, 8, S)) < 0.05, C - 1, rng.integers(0, C - 1, (N, 8, S)))
    cv = rng.integers(0, S, (N, 8, 16, S)); cd = np.ascontiguousarray(np.argsort(rng.random((N, 8, RO, S)), axis=-1)[..., :L * 16])
    return sk, oc, cv, cd
def fill(rng, share):
    u = rng.random((N, 8, 1, RO, B)); v = rng.random((N, 8, 1, RO, B))
    h = np.where(u < share, 9 + 31 * v, np.where(u < share + 0.1, 4 + 5 * v, np.where(u < share + 0.3, 0.0, 0.2 + 3.8 * v)))
    w = rng.random((N, 8, 16, RO, B)) * (rng.random((N, 8, 16, RO, B)) < 0.7)
    return np.minimum((80 * h * w).astype(np.int64), 4096)
def sums(sk, oc, cd):
    who = np.take_along_axis(oc, cd[:, :, 0, :B * 16], 2)
    return np.add.accumulate(np.take_along_axis(sk, who[:, :, None, :], 3).reshape(N, 8, 16, B, 16), axis=4)
def heavy(rng, sk, oc, cv, cd, nd):
    own = np.arange(S); j = np.arange(B)
    for g in rng.permutation(8)[:2]:
        left = []
        for q in range(N):
            v = rng.integers(200, 256, (16, C)); v[:, C - 1] = 0; e = rng.integers(L, C - 1, S)
            st = cd[q, g, 0].reshape(L, 16); late = st[B:].reshape(-1)
            cd[q, g, 1] = np.concatenate([rng.permutation(st[:B].reshape(-1)), rng.permutation(late)])
            cv[q, g] = rng.choice(np.setdiff1d(own, late), (16, S))
            p = rng.integers(10, 16, B); before = np.add.accumulate(v[:, e[st[:B]]], axis=2)[:, j, p - 1]
            x = 208 + (-before) % 16; want = before + x
            x[rng.integers(0, 16, B), j] -= rng.integers(0, 2, B)
            v[:, :B] = x; e[st[j, p]] = j
            big = rng.permutation(B)[:U // 2]; e[st[big[U // 8:], 8:]] = C - 1
            want[:, big] = 0; want[rng.integers(0, 16, U // 2), big] = 4096
            sk[q, g] = v; oc[q, g] = e; nd[q, g] = 0; nd[q, g, :, 0] = want
            end = np.add.reduce(v[:, e[st[:B]]], axis=2); u = np.nonzero(np.any(end < want, axis=0))[0][:U]
            left.append(np.maximum(want[:, u] - end[:, u], 0))
        for q in range(N):
            w = left[q - 1]; n = w.shape[1]; k = np.arange(n); z = np.argmax(w, axis=0); top = w[z, k]
            st = cd[q, g, 1].reshape(L, 16)[B:B + n]
            line = np.add.accumulate(sk[q, g][z[:, None], oc[q, g][st]], axis=1)
            p = np.add.reduce((line < top[:, None]).astype(np.int64), axis=1)
            before = np.where(p > 0, line[k, np.maximum(p - 1, 0)], 0)
            sk[q, g, z, B + k] = top - before - k % 2; oc[q, g, st[k, p]] = B + k
def pack(sk, oc, cv, cd, nd):
    return {"skill": np.ascontiguousarray(sk.reshape(N, 128, C)).astype(np.float32).astype(BF), "occ": oc.astype(np.int32), "cover": np.ascontiguousarray(cv.reshape(N, 128, S)).astype(np.int32),
            "cards": np.stack([gtable(a.reshape(8, -1)) for a in cd]), "need": np.ascontiguousarray(nd.reshape(N, 128, RO * B)).astype(np.float32).astype(BF)}
def setup_inputs(rng):
    sk, oc, cv, cd = parts(rng)
    return pack(sk, oc, cv, cd, fill(rng, rng.choice(np.array([0.03, 0.1, 0.2, 0.3]), (N, 8, 1, 1, 1))))
def setup_inputs_room(rng):
    sk, oc, cv, cd = parts(rng); nd = np.zeros((N, 8, 16, RO, B), np.int64); pre = sums(sk, oc, cd)
    nd[:, :, :, 0] = pre[..., 0] * (rng.random((N, 8, 1, B)) < 0.5)
    for q in range(N):
        for t in range(RO):
            size = rng.permutation(np.array([0, 1, U - 1, U, U + 1, B, U, 0]))
            for g in range(8):
                n = int(size[g]); lanes = rng.permutation(B)[:n]
                nd[q, g, :, t, lanes] = rng.integers(0, 256, (n, 16)); nd[q, g, rng.integers(0, 16, n), t, lanes] = 4096
    return pack(sk, oc, cv, cd, nd)
def setup_inputs_ties(rng):
    sk, oc, cv, cd = parts(rng)
    few = rng.integers(0, 3, sk.shape) * 16; m = np.arange(8)[None, :, None, None] % 2 == 0
    sk = np.where(m, few, sk // 16 * 16) * (rng.random((N, 8, 1, C)) > 0.1); sk[..., C - 1] = 0
    nd = fill(rng, 0.05); pre = sums(sk, oc, cd)
    p = rng.choice(np.array([0, 0, 1, 3, 7, 14, 15, 15]), (N, 8, B))
    w = np.take_along_axis(pre, p[:, :, None, :, None], 4)[..., 0]
    w = w + 16 * ((np.arange(16)[None, None, :, None] == rng.integers(0, 16, (N, 8, 1, B))) & (rng.random((N, 8, 1, B)) < 0.5))
    nd[:, :, :, 0] = w * (rng.random((N, 8, 1, B)) > 0.3)
    heavy(rng, sk, oc, cv, cd, nd)
    return pack(sk, oc, cv, cd, nd)
def setup_inputs_crowd(rng):
    sk, oc, cv, cd = parts(rng); h = B // 2; sk[..., 0] = 255; own = np.arange(S); o = rng.permutation(8)
    full = np.argsort(rng.random((N, 8, B)), axis=-1)[..., :U]
    for q in range(N):
        for g in range(8):
            card = cd[q, g, 0].reshape(L, 16)
            if g == o[0] or g == o[1]:
                k = rng.permutation(np.setdiff1d(own, card[full[q, g]].reshape(-1))); a, b = k[:L], k[L:2 * L]
                mid = rng.permutation(np.setdiff1d(own, k[:2 * L]))[:14 * L].reshape(L, 14)
                cd[q, g, 1] = np.concatenate([a[:, None], mid, b[:, None]], axis=1).reshape(-1)
                v = np.clip(sk[q, g], 16, 239); v[:, :16] = rng.integers(240, 256, (16, 16)); v[:, C - 1] = 0; sk[q, g] = v
                oc[q, g, a] = rng.integers(16, C - 1, L); oc[q, g, b] = rng.integers(0, 16, L)
                c = np.repeat(own[None, :], 16, axis=0)
                if g == o[0]: c[:, a] = b[rng.integers(0, 2, (16, L))]
                else: c[:, a] = np.where(np.arange(16)[:, None] >= rng.integers(0, 16, L)[None, :], b[None, :], a[None, :])
                cv[q, g] = c
            else:
                pool = card[h:h + 16, 15]; oc[q, g, pool[:8]] = 0
                c = pool[rng.integers(0, 16, (16, S))]; kind = rng.integers(0, 5, S)
                c[:15] = np.where(kind >= 3, own, c[:15]); c[15] = np.where(kind == 4, own, c[15]); cv[q, g] = c
    nd = fill(rng, 0.05); pre = sums(sk, oc, cd)
    nd[:, :, :, 0] = pre[..., 0] * (np.arange(B) < h); nd[:, o[:2]] = 0
    for q in range(N):
        for g in o[:2]:
            z = rng.integers(0, 16, U); l = full[q, g]; nd[q, g, z, 0, l] = pre[q, g, z, l, 15] // 16 * 16 + 16
            nd[q, g, rng.integers(0, 16, B), 1, np.arange(B)] = rng.integers(1, 17, B)
    return pack(sk, oc, cv, cd, nd)
def setup_inputs_bare(rng):
    sk, oc, cv, cd = parts(rng); h = rng.permutation(8)
    oc = np.where(rng.random((N, 8, S)) < rng.choice(np.array([0.4, 0.6, 0.8]), (N, 8, 1)), C - 1, oc); oc[:, h[0]] = C - 1
    ends = np.array([0, 1, S - 2, S - 1]); cv[:, h[2]] = rng.choice(ends, (N, 16, S)); oc[:, h[2], :2] = rng.integers(0, C - 1, (N, 2)); oc[:, h[2], S - 2:] = rng.integers(0, C - 1, (N, 2))
    nd = fill(rng, 0.05) * (rng.random((N, 8, 1, RO, B)) < 0.5); nd[::2, h[1]] = 0
    return pack(sk, oc, cv, cd, nd)
def setup_inputs_spread(rng):
    sk, oc, cv, cd = parts(rng)
    sk = np.minimum((np.exp2(8.2 * rng.random((N, 8, 1, C))) * rng.random((N, 8, 16, C))).astype(np.int64), 255); sk[..., C - 1] = 0
    oc = np.where(rng.random((N, 8, S)) < 0.1, C - 1, np.minimum(((C - 1) * rng.random((N, 8, S)) ** 3).astype(np.int64), C - 2))
    cv = np.minimum((S * rng.random((N, 8, 16, S)) ** 2).astype(np.int64), S - 1)
    nd = (np.minimum(np.exp2(12.2 * rng.random((N, 8, 1, RO, B))), 4096) * rng.choice(np.array([0.0, 0.25, 0.5, 1.0]), (N, 8, 16, RO, B))).astype(np.int64)
    return pack(sk, oc, cv, cd, nd * (rng.random((N, 8, 1, RO, B)) > 0.3))
def check_inputs(d):
    bad = []
    for k, hi in (("skill", 255), ("need", 4096), ("occ", C - 1), ("cover", S - 1), ("cards", S - 1)):
        x = np.asarray(d[k]).astype(np.float64)
        if not np.all((x >= 0) & (x <= hi) & (x == np.floor(x))): bad.append("range of " + k)
    if not np.all(np.asarray(d["skill"])[:, :, C - 1].astype(np.float32) == 0): bad.append("last column of skill")
    e = np.sort(np.asarray(d["cards"]).reshape(N, 8, 16, RO, L).transpose(0, 1, 3, 2, 4).reshape(N, 8, RO, 16 * L), axis=-1)
    if np.any(e[..., 1:] == e[..., :-1]): bad.append("equal stations on the cards of a round")
    return bad
def reference(skill, occ, cover, cards, need):
    sk = skill.astype(np.float32).astype(np.int64).reshape(N, 8, 16, C); cv = cover.astype(np.int64).reshape(N, 8, 16, S)
    cd = np.stack([gentries(a) for a in cards]).astype(np.int64).reshape(N, 8, RO, L, 16); nd = need.astype(np.float32).astype(np.int64).reshape(N, 8, 16, RO, B)
    oc = np.array(occ, dtype=np.int64); arrived = np.zeros((N, 8, 16, U), np.int64)
    for t in range(RO):
        sent = np.zeros((N, 8, 16, U), np.int64)
        for r in range(N):
            w = np.concatenate([nd[r, :, :, t], arrived[r]], axis=2)
            st = cd[r, :, t]; flat = st.reshape(8, -1)
            who = np.take_along_axis(oc[r], flat, 1)
            col = np.take_along_axis(sk[r], who[:, None, :], 2).reshape(8, 16, L, 16)
            pre = np.add.accumulate(col, axis=3)
            met = np.all(pre >= w[..., None], axis=1)
            zero = np.all(w == 0, axis=1)
            leave = ~np.concatenate([zero[..., None], met[..., :15]], axis=2)
            unmet = ~met[..., 15]; before = np.add.accumulate(unmet.astype(np.int64), axis=1) - unmet
            rest = np.maximum(w - pre[..., 15], 0); g, l = np.nonzero(unmet & (before < U))
            sent[(r + 1) % N][g, :, before[g, l]] = rest[g, :, l]
            np.put_along_axis(oc[r], flat, np.where(leave.reshape(8, -1), C - 1, who), 1)
            s = st[..., 0]; lost = leave[..., 0] & (who.reshape(8, L, 16)[..., 0] != C - 1)
            m = np.take_along_axis(cv[r], s[:, None, :], 2)
            a = np.take_along_axis(oc[r], m.reshape(8, -1), 1)
            ka = np.take_along_axis(sk[r], a[:, None, :], 2).reshape(8, 16, 16, L)
            a = a.reshape(8, 16, L); good = np.add.reduce((ka >= col[:, :, None, :, 0]).astype(np.int64), axis=1)
            fit = (a != C - 1) & (good >= Q); ok = lost & np.any(fit, axis=1)
            i = np.argmax(fit, axis=1)[:, None, :]
            src = np.take_along_axis(m, i, 1)[:, 0]; new = np.take_along_axis(a, i, 1)[:, 0]
            for g in range(8):
                lanes = np.nonzero(ok[g])[0]
                out, at = np.unique(src[g, lanes], return_index=True); lanes = lanes[at]
                oc[r, g, s[g, lanes]] = new[g, lanes]; oc[r, g, out] = C - 1
        arrived = sent
    return {"y": oc.astype(np.float32)}

@@ -1,0 +1,588 @@
+import numpy as np
+from concourse.mybir import AluOpType as A, ActivationFunctionType as F
+
+BF, FP, F16, I32, U16 = "bfloat16", "float32", "float16", "int32", "uint16"
+S, L, B, U, RO = 2048, 128, 96, 32, 3
+W = 2320
+BIG = 4096.0
+NENG = 8
+FUSED, PLAIN = [2, 3], [0, 1]
+
+SCRATCH = {}
+for _n, _w, _d in [
+        ("SK", S, BF), ("OC", 128, I32), ("CD", 384, I32), ("ND", 288, BF), ("CV", S, I32), ("JS", W, I32),
+        ("CU", 384, U16), ("OU", 128, U16), ("SGU", 128, U16), ("CH", 384, F16), ("MS", 384, F16), ("S0L", 24, U16), ("S0Y", 8, U16),
+        ("CY", 512, BF), ("M16", 384, F16), ("DM", 128, FP), ("ONES", S, BF), ("THR", 128, FP), ("D32", 128, FP), ("DR", S, BF), ("E", S, BF),
+        ("HLF", 128, FP), ("HL", 128, BF), ("LO", 16, FP), ("IO", S, FP), ("INV0", S, FP), ("INV1", S, FP), ("INV2", S, FP),
+        ("ML", 384, U16), ("MH", 384, F16), ("PN", S, BF), ("RN", S, BF),
+        ("PL0", 128, U16), ("PL1", 128, U16), ("PL2", 128, U16), ("PT0", 128, FP), ("PT1", 128, FP), ("PT2", 128, FP),
+        ("RL0", 128, U16), ("RL1", 128, U16), ("RL2", 128, U16), ("XS", S, BF), ("XG", S + 16, BF), ("XK", W, BF), ("XT", S, BF),
+        ("X15", 128, BF), ("EE", S, BF), ("D1", 1536, BF), ("D1F", 512, FP), ("NF", 128, FP), ("NZ", 384, BF), ("BS", 128, BF), ("BT", 128, BF),
+        ("BE", S, BF), ("AB", S, BF), ("CM", S, BF), ("NFM", 128, FP), ("KY", 128, FP), ("SC8", 128, FP), ("C8", 8, FP), ("ST8", 8, FP),
+        ("DG", 1024, F16), ("EQ", 1024, F16), ("LU", 8, U16), ("LS", 8, U16), ("NV", 128, BF), ("NJ", 128, FP), ("OJ", 128, FP),
+        ("ZB", 128, BF), ("ZF", 128, FP), ("DD", 128, FP), ("RD", 128, BF), ("UU", 128, FP), ("CN", 128, FP), ("WW", 128, FP), ("OF0", 128, FP),
+        ("OFF", 128, BF), ("DQ", 128, FP), ("OL", 8, U16), ("SL0", 256, FP), ("SL1", 256, FP), ("ARR0", U, FP), ("ARR1", U, FP),
+        ("RB0", U, FP), ("RB1", U, FP), ("ARB", U, BF), ("YY", W, FP)]:
+    SCRATCH[_n] = ("sbuf", [128, _w], _d)
+PARTS = {}
+for _b, _d, _l in [
+        ("GI", I32, [("TA", 128), ("TB", 128), ("TC", 128), ("W1", 128), ("W2", 128), ("W3", 128), ("W4", 128), ("T1", 128), ("T3", 128),
+                     ("T2", 8), ("CI", 8), ("PI", 8), ("SI", 8), ("IP", 8), ("IQ", 8)]),
+        ("GF", FP, [("LOF", 16), ("PO", 8), ("PV", 8), ("DCOL", 8), ("CYA", 8), ("CYB", 8), ("CYC", 8)]),
+        ("GB", BF, [("ID", 128), ("I18", 128), ("I18N", 128), ("BLKW", 128), ("BLKN", 128), ("CCON", 128), ("SELW", 8), ("SEL2", 8)]),
+        ("GH", F16, [("IH", 128), ("PM1", 128), ("PM4", 128), ("S0R", 128), ("TRI", 128), ("PH", 128), ("FS", 128), ("LOS", 128), ("LD", 128),
+                     ("FT", 128), ("FM", 128), ("B16", 16), ("ONE16", 16), ("F4K", 16)])]:
+    _o = 0
+    for _n, _w in _l:
+        PARTS[_n] = (_b, _o, {"IP": 1, "IQ": 1, "PO": 1, "PV": 1, "DCOL": 1, "CYA": 1, "CYB": 1, "CYC": 1, "B16": 8}.get(_n, _w))
+        _o += _w
+    SCRATCH[_b] = ("sbuf", [128, _o], _d)
+for _k in range(8):
+    SCRATCH["P%d" % _k] = ("psum", [128, 512], FP)
+SEMAPHORES = ["cV", "cS", "cP", "cG", "dJ"] + ["d%d" % k for k in range(10)] + ["arr0", "arr1", "rin0", "rin1", "out0", "out1"]
+
+TUNE = {"sc": 3.0, "rlat": 6.0, "hop": 0.12, "own": 0.06, "trials": 400}
+ORDER = {}
+
+
+def arrange(ops, pr):
+    m, hop = len(ops), TUNE["hop"]
+    succ = [[] for _ in range(m)]
+    for i, o in enumerate(ops):
+        for j in o["edges"]:
+            succ[j].append(i)
+    up = [0.0] * m
+    for i in range(m - 1, -1, -1):
+        o = ops[i]
+        up[i] = o["cost"] + max([up[j] + (0.0 if ops[j]["edges"][i] == 0 and ops[j]["q"] == o["q"] else hop + o["lat"]) for j in succ[i]] + [o["lat"]])
+    jit = pr["jit"] * np.random.default_rng(pr["seed"]).standard_normal(m)
+    key = [up[i] + pr["b"].get(ops[i]["tag"], 0.0) + float(jit[i]) for i in range(m)]
+    left = [len(o["edges"]) for o in ops]
+    ready = [i for i in range(m) if not left[i]]
+    slots = {k: [] for k in "VSPGY"}
+    at, end, on = [0.0] * m, [0.0] * m, [""] * m
+    while ready:
+        i = max(ready, key=lambda i: (key[i], -i))
+        ready.remove(i)
+        for j in succ[i]:
+            left[j] -= 1
+            if not left[j]:
+                ready.append(j)
+        o = ops[i]
+        best = None
+        for q in o["q"]:
+            s = 0.0
+            for j, e in o["edges"].items():
+                if on[j] == q and e == 0:
+                    s = max(s, at[j] + ops[j]["cost"])
+                else:
+                    s = max(s, end[j] + (hop if on[j] != q else TUNE["own"]))
+            for (a, b) in slots[q]:
+                if s + o["cost"] <= a:
+                    break
+                s = max(s, b)
+            pen = s + o["cost"] + (pr["pv"] if q == "V" and len(o["q"]) > 1 else 0.0)
+            if best is None or pen < best[0] - 1e-9:
+                best = (pen, s, q)
+        _, s, q = best
+        on[i], at[i], end[i] = q, s, s + o["cost"] + o["lat"]
+        slots[q].append((s, s + o["cost"]))
+        slots[q].sort()
+    return max(end), at, on
+
+
+def order_of(ops):
+    if "at" not in ORDER:
+        r = np.random.default_rng(1)
+        best, pr = None, {"pv": 1.5, "jit": 0.0, "seed": 0, "b": {}}
+        for k in range(TUNE["trials"]):
+            p = dict(pr, b=dict(pr["b"]))
+            if k:
+                c = int(r.integers(4))
+                if c == 0:
+                    p["seed"], p["jit"] = int(r.integers(1000000)), float(r.choice([0.0, 0.2, 0.5, 1.0]))
+                elif c == 1:
+                    p["pv"] = float(r.choice([0.3, 0.6, 1.0, 1.5, 2.0]))
+                else:
+                    p["b"][str(r.choice(["i0", "i1", "i2", "p0", "p1", "p2", "n0", "n1", "n2", "h0", "h1", "j0", "j1", "y"]))] = float(3 - 14 * r.random())
+            e = arrange(ops, p)
+            if best is None or e[0] < best[0]:
+                best, pr = e, p
+        ORDER["end"], ORDER["at"], ORDER["on"] = best
+    return ORDER["at"], ORDER["on"]
+
+
+def rank_program(g, core, T, topo):
+    cores = list(T.cores)
+    n = len(cores)
+
+    def relay_of(r):
+        src, dst = cores[r], cores[(r + 1) % n]
+        c = [x for x in topo.cores_of(src) if x != src and topo.may_write(x, dst)]
+        c.sort(key=lambda x: (topo.die(x) != topo.die(src), x))
+        return c[0]
+
+    def emask(a, b):
+        e = topo.engines(a, b)[:NENG]
+        return sum(1 << x for x in e), len(e)
+
+    rank = T.rank_of(core)
+    if rank is None:
+        for r in range(n):
+            if relay_of(r) == core:
+                dst = cores[(r + 1) % n]
+                _, nin = emask(cores[r], core)
+                m, k = emask(core, dst)
+                rid, pid = topo.addr(dst, core)
+                for t in range(RO - 1):
+                    g.wait_ge(T.sem["rin%d" % t], nin)
+                    g.remote_dma(T["ARR%d" % t][:, :], T["RB%d" % t][:, :], T.sem["arr%d" % t], T.sem["out%d" % t], pid, rid, m)
+                for t in range(RO - 1):
+                    g.wait_ge(T.sem["out%d" % t], k)
+        return
+
+    Q = {"V": g.vector, "S": g.scalar, "P": g.tensor, "G": g, "Y": g.sync}
+    CS = {"V": "cV", "S": "cS", "P": "cP", "G": "cG"}
+    ops, acc, tag = [], {}, [""]
+
+    def R(name, lo=0, hi=None, st=1):
+        if name in PARTS:
+            b, o, w = PARTS[name]
+            return (b, o + lo, o + (w if hi is None else hi), st)
+        return (name, lo, SCRATCH[name][1][-1] if hi is None else hi, st)
+
+    def ap(r):
+        return T[r[0]][:, r[1]:r[2]:r[3]] if r[3] != 1 else T[r[0]][:, r[1]:r[2]]
+
+    def psum(name):
+        return SCRATCH[name][0] == "psum"
+
+    def width(r):
+        return (r[2] - r[1] + r[3] - 1) // r[3]
+
+    def two(*rs):
+        return all(SCRATCH[r[0]][2] in (BF, F16, U16) for r in rs)
+
+    def overlap(a, b):
+        if psum(a[0]):
+            return True
+        if a[1] >= b[2] or b[1] >= a[2]:
+            return False
+        return not (a[3] == b[3] and a[3] > 1 and (a[1] - b[1]) % a[3])
+
+    def add(q, fn, reads, writes, cost, chain=False, kind="c", lat=0.0, extra=None):
+        me, edges = len(ops), {}
+        mine = [(r, "r") for r in reads] + [(r, "w") for r in writes]
+        for rr, k in mine:
+            for (o, ok, j) in acc.get(rr[0], []):
+                if j == me or not overlap(rr, o):
+                    continue
+                if k == "r" and ok == "r":
+                    if psum(rr[0]):
+                        edges[j] = max(edges.get(j, 0), 0)
+                    continue
+                e = 0 if k == "w" and chain else 1
+                if psum(rr[0]) and q == "P" and ops[j]["q"] == "P" and (rr[1] >= o[2] or o[1] >= rr[2]):
+                    e = 0
+                edges[j] = max(edges.get(j, 0), e)
+        for rr, k in mine:
+            keep = []
+            for e in acc.get(rr[0], []):
+                o = e[0]
+                cov = rr[1] <= o[1] and o[2] <= rr[2] and (rr[3] == 1 or (rr[3] == o[3] and (rr[1] - o[1]) % rr[3] == 0))
+                if k == "w" and e[2] != me and (cov or (psum(rr[0]) and ops[e[2]]["q"] != "P")):
+                    continue
+                keep.append(e)
+            keep.append((rr, k, me))
+            acc[rr[0]] = keep
+        ops.append({"tag": tag[0], "q": q, "fn": fn, "cost": cost, "edges": edges, "kind": kind, "lat": lat, "x": extra})
+
+    def op(q, fn, reads, writes, cyc, chain=False):
+        add(q, fn, reads, writes, (0.02 + max(cyc, 64) * 0.00083) * 1.2, chain)
+
+    def dma(q, out, in_, reads, writes, lat, group=None):
+        add(q, lambda e, z: e.dma_start(out, in_), reads, writes, 0.1, kind="d", lat=lat, extra=group)
+
+    def copy(q, o, i, scale=1.0, bias=0.0):
+        def f(e, z):
+            if z == "V":
+                if scale == 1.0 and bias == 0.0:
+                    return e.tensor_copy(ap(o), ap(i))
+                return e.tensor_scalar(ap(o), ap(i), float(scale), float(bias), A.mult, A.add)
+            return e.activation(ap(o), ap(i), F.Copy if bias == 0.0 else F.Identity, bias=float(bias), scale=float(scale))
+        op(q, f, [i], [o], width(i))
+
+    def relu(q, o, i):
+        op(q, lambda e, z: e.tensor_scalar(ap(o), ap(i), 0.0, None, A.max) if z == "V" else e.activation(ap(o), ap(i), F.Relu), [i], [o], width(i))
+
+    def ts(o, i, s1, op0, s2=None, op1=None):
+        rd, a1, a2 = [i], s1, s2
+        if isinstance(s1, tuple):
+            rd.append(s1)
+            a1 = ap(s1)
+        if isinstance(s2, tuple):
+            rd.append(s2)
+            a2 = ap(s2)
+        c = width(i) * (0.5 if two(o, i) else 1)
+        if op1 is None:
+            op("V", lambda e, z: e.tensor_scalar(ap(o), ap(i), a1, None, op0), rd, [o], c)
+        else:
+            op("V", lambda e, z: e.tensor_scalar(ap(o), ap(i), a1, a2, op0, op1), rd, [o], c)
+
+    def tt(o, a, b, o_):
+        op("V", lambda e, z: e.tensor_tensor(ap(o), ap(a), ap(b), o_), [a, b], [o], width(o) * (1 if psum(a[0]) or psum(b[0]) else 2))
+
+    def fill(o, v, q="V"):
+        if q == "G":
+            op(q, lambda e, z: e.iota(ap(o), [[0, width(o)]], int(v), 0, allow_small_or_imprecise_dtypes=True), [], [o], 150 + 2 * width(o))
+        else:
+            op(q, lambda e, z: e.memset(ap(o), v), [], [o], width(o) * (0.5 if two(o) else 1))
+
+    def scan(o, a, b, op0, op1):
+        op("V", lambda e, z: e.tensor_tensor_scan(ap(o), ap(a), ap(b), 0.0, op0, op1), [a, b], [o], width(o) * (0.5 if two(o, a, b) else 1))
+
+    def mm(o, l, r, start=True, stop=True):
+        op("P", lambda e, z: e.matmul(ap(o), ap(l), ap(r), start, stop), [l, r], [o], max(min(64, width(l)), width(r)) * 0.86, chain=not start)
+
+    def gath(q, o, win, lst):
+        op(q, lambda e, z: e.tensor_copy(ap(o), ap(win).indirect(ap(lst))) if z == "V" else
+           e.activation(ap(o), ap(win).indirect(ap(lst)), F.Copy), [win, lst], [o], 50 + 1.5 * width(o))
+
+    def scat(win, lst, i):
+        op("V", lambda e, z: e.tensor_copy(ap(win).indirect(ap(lst)), ap(i)), [lst, i], [win], 50 + TUNE["sc"] * width(i))
+
+    def place(win, lst, i):
+        op("VS", lambda e, z: e.tensor_copy(ap(win).indirect(ap(lst)), ap(i)) if z == "V" else
+           e.activation(ap(win).indirect(ap(lst)), ap(i), F.Silu), [lst, i], [win], 50 + TUNE["sc"] * width(i))
+
+    def iota(o, pat, base, cm, fl=False):
+        if fl:
+            op("G", lambda e, z: e.iota(ap(o), pat, base, cm, allow_small_or_imprecise_dtypes=True), [], [o], 150 + 2 * width(o))
+        else:
+            op("G", lambda e, z: e.iota(ap(o), pat, base, cm), [], [o], 150 + 2 * width(o))
+
+    def wrap(bank, src, k0, k1):
+        for r in range(16):
+            mm(R(bank, 0, k1 - k0), R("DR", 128 * r, 128 * r + 128), R(src, 16 * k0 + r, 16 * k1, 16), r == 0, r == 15)
+
+    h = S // 2
+    dma("Y", T.CD[:, 0:128], T.cards[:, 0:128], [], [R("CD", 0, 128)], 2.4)
+    dma("S", T.SK[:, 0:h], T.skill[:, 0:h], [], [R("SK", 0, h)], 3.5)
+    dma("Y", T.OC[:, :], T.occ[:, :], [], [R("OC")], 2.6)
+    dma("S", T.SK[:, h:S], T.skill[:, h:S], [], [R("SK", h, S)], 4.5)
+    dma("Y", T.ND[:, :], T.need[:, :], [], [R("ND")], 5.0)
+    dma("Y", T.CD[:, 128:384], T.cards[:, 128:384], [], [R("CD", 128, 384)], 5.5)
+    dma("Y", T.CV[:, :], T.cover[:, :], [], [R("CV")], 9.0)
+    for q in range(16):
+        dma("Y", T.JS[q:128:16, 0:S], T.occ[:, :], [], [R("JS", q * 128, q * 128 + 128)], 12.0, ("dJ", 256))
+
+    iota(R("IP"), [[0, 1]], 0, 1)
+    iota(R("HLF"), [[1024, 128]], 0, 0, True)
+    iota(R("LOF"), [[64, 16]], 64, 0, True)
+    iota(R("W1"), [[-16, 8], [0, 16]], 0, 1)
+    iota(R("W2"), [[-1, 128]], 0, 1)
+    iota(R("W3"), [[0, 8], [-1, 16]], 0, 1)
+    iota(R("W4"), [[-16, 8], [1, 16]], -15, 1)
+    iota(R("DCOL"), [[0, 1]], 2050, 2, True)
+    iota(R("D32"), [[1, 128]], 128, 0, True)
+    fill(R("ONES"), 1.0)
+    fill(R("DR"), 0.0, "G")
+    fill(R("D1"), 0.0, "G")
+    fill(R("D1F"), 0.0, "G")
+    op("G", lambda e, z: e.affine_select(ap(R("E")), ap(R("ONES")), [[-1, 128], [0, 16]], A.is_equal, 0.0, 0, 1), [R("ONES")], [R("E")], 200 + 2 * S)
+    ts(R("T2"), R("W1", 0, 128, 16), 1, A.arith_shift_right)
+    ts(R("SEL2"), R("T2"), 0.0, A.is_equal, 1.0 / 64, A.mult)
+    for r in range(16):
+        copy("VS", R("DR", 128 * r + r, 128 * r + 128, 16), R("SEL2"))
+    ts(R("IQ"), R("IP"), 1, A.bitwise_and)
+    copy("V", R("PO"), R("IQ"))
+    copy("V", R("PV"), R("IQ"), -1.0, 1.0)
+    ts(R("HL"), R("HLF"), R("PV"), A.mult)
+    ts(R("LO"), R("LOF"), R("PO"), A.mult)
+
+    def io_col(i):
+        o, b = R("IO", i, S, 16), R("LO", i, i + 1)
+        op("VS", lambda e, z: e.tensor_scalar(ap(o), ap(R("HL")), ap(b), None, A.add) if z == "V" else
+           e.activation(ap(o), ap(R("HL")), F.Identity, bias=ap(b)), [R("HL"), b], [o], 128)
+
+    for i in range(16):
+        io_col(i)
+    copy("V", R("CU", 0, 128), R("CD", 0, 128))
+    ts(R("TA"), R("CD", 0, 128), 127, A.bitwise_and)
+    ts(R("TB"), R("CD", 0, 128), 7, A.arith_shift_right)
+    ts(R("TC"), R("TA"), 16.0, A.mult)
+    tt(R("TA"), R("TC"), R("TB"), A.add)
+    copy("V", R("SGU"), R("TA"))
+    copy("V", R("OU"), R("OC"))
+    ts(R("ID"), R("W2"), 0.0, A.is_equal)
+    ts(R("T1"), R("W1"), 4, A.arith_shift_right)
+    ts(R("BLKW"), R("T1"), 0.0, A.is_equal, 512.0, A.mult)
+    fill(R("XG", 0, 1), BIG)
+    fill(R("XK", 0, 1), 0.0)
+    fill(R("XK", S + 1, W), 0.0)
+    ts(R("SK", 0, h), R("SK", 0, h), 1.0 / 64, A.max)
+    ts(R("SK", h, S - 1), R("SK", h, S - 1), 1.0 / 64, A.max)
+    for c in range(4):
+        gath("VS", R("XS", 512 * c, 512 * c + 512), R("SK"), R("OU", 32 * c, 32 * c + 32))
+
+    def needs(t):
+        copy("VS", R("D1", 0, 1536, 16), R("ND", B * t, B * t + B), -1.0)
+        if t < RO - 1:
+            copy("VS", R("NF", 0, B), R("ND", B * t, B * t + B))
+
+    needs(0)
+    mm(R("P7", 0, 288), R("BLKW"), R("ND"))
+    for t in range(RO):
+        ts(R("NZ", 128 * t, 128 * t + B), R("P7", B * t, B * t + B), 0.0, A.is_equal, 512.0, A.mult)
+    fill(R("NZ", B, 128), 512.0)
+    fill(R("NF", B, 128), 0.0)
+    copy("V", R("CU", 128, 384), R("CD", 128, 384))
+    copy("V", R("CH"), R("CD"))
+    ts(R("S0R"), R("W1"), 0.0, A.is_equal)
+    ts(R("B16"), R("T1", 0, 128, 16), 0.0, A.is_equal)
+    ts(R("T3"), R("W3"), 15, A.bitwise_and)
+    for t in range(RO):
+        ts(R("M16", 128 * t, 128 * t + 128), R("T3"), 0.0, A.is_equal)
+    for t in range(RO):
+        mm(R("P6", 128 * t, 128 * t + 128), R("CH", 128 * t, 128 * t + 128), R("S0R"))
+    tt(R("MS"), R("P6", 0, 384), R("M16"), A.mult)
+    for t in range(RO):
+        mm(R("P6", 8 * t, 8 * t + 8), R("MS", 128 * t, 128 * t + 128), R("B16"))
+    copy("V", R("S0L"), R("P6", 0, 24))
+    copy("V", R("S0Y"), R("P6", 16, 24), 1.0, 1.0)
+    for t in range(RO):
+        gath("V", R("ML", 128 * t, 128 * t + 128), R("CV"), R("S0L", 8 * t, 8 * t + 8))
+        copy("V", R("MH", 128 * t, 128 * t + 128), R("ML", 128 * t, 128 * t + 128))
+    ts(R("PM1"), R("W4"), 0.0, A.is_equal, -1.0, A.mult)
+    ts(R("PM4"), R("W4"), 0.0, A.is_equal, 4096.0, A.mult)
+    ts(R("SELW"), R("T1", 0, 128, 16), 0.0, A.is_equal, 67108864.0, A.mult)
+    ts(R("BLKN"), R("T1"), 0.0, A.is_equal, -262144.0, A.mult)
+    ts(R("I18"), R("W2"), 0.0, A.is_equal, 262144.0, A.mult)
+    ts(R("I18N"), R("W2"), 0.0, A.is_equal, -262144.0, A.mult)
+    ts(R("IH"), R("W2"), 0.0, A.is_equal)
+    ts(R("TRI"), R("W2"), 0.0, A.is_gt)
+    ts(R("DM"), R("T3"), 0.0, A.is_equal, R("DCOL"), A.mult)
+    ts(R("ONE16"), R("W2", 0, 16), 0.0, A.mult, 1.0, A.add)
+    ts(R("F4K"), R("W2", 0, 16), 0.0, A.mult, 4096.0, A.add)
+    fill(R("CCON"), -4980736.0)
+    fill(R("THR"), 0.0)
+    fill(R("THR", 0, 128, 16), -9.0e9)
+    fill(R("ZB"), 0.0)
+    fill(R("ZF"), 2047.0)
+    fill(R("JS", S, W), 0)
+    fill(R("YY", 0, 1), 2047.0)
+    fill(R("YY", S + 1, W), 2047.0)
+    ts(R("CYA"), R("W2", 0, 1), 0.0, A.is_equal, 2048.0, A.mult)
+    ts(R("CYB"), R("W2", 0, 1), 1.0, A.is_equal, -1.0, A.mult)
+    tt(R("CYC"), R("CYA"), R("CYB"), A.add)
+    ts(R("CY"), R("ONES", 0, 512), R("CYC"), A.mult)
+
+    def lists(t):
+        tag[0] = "i%d" % t
+        for p in range(8):
+            place(R("INV%d" % t), R("CU", 128 * t + 16 * p, 128 * t + 16 * p + 16), R("IO", 256 * p, 256 * p + 256))
+        tag[0] = "p%d" % t
+        for c in range(4):
+            gath("VS", R("PN", 512 * c, 512 * c + 512), R("INV%d" % t), R("ML", 128 * t + 32 * c, 128 * t + 32 * c + 32))
+        wrap("P7", "PN", 0, 128)
+        copy("V", R("PL%d" % t), R("P7", 0, 128))
+        if t < RO - 1:
+            copy("V", R("PH"), R("P7", 0, 128))
+            mm(R("P7", 0, 128), R("PH"), R("PM1"), True, False)
+            mm(R("P7", 0, 128), R("MH", 128 * t, 128 * t + 128), R("PM4"), False, True)
+            copy("VS", R("PT%d" % t), R("P7", 0, 128), 1.0, 2050.0)
+        else:
+            mm(R("P7", 0, 128), R("MH", 128 * t, 128 * t + 128), R("PM1"))
+            copy("VS", R("PT%d" % t), R("P7", 0, 128), 1.0, 2049.0)
+        tag[0] = "n%d" % t
+        for c in range(4):
+            if t < RO - 1:
+                gath("VS", R("RN", 512 * c, 512 * c + 512), R("INV%d" % t), R("CU", 128 * t + 128 + 32 * c, 128 * t + 160 + 32 * c))
+            else:
+                copy("VS", R("RN", 512 * c, 512 * c + 512), R("INV2", 512 * c, 512 * c + 512))
+        wrap("P7", "RN", 0, 128)
+        copy("V", R("RL%d" % t), R("P7", 0, 128))
+        tag[0] = ""
+
+    lists(0)
+
+    for t in range(RO):
+        win, lst = (R("XS"), "SGU") if t == 0 else (R("XK"), "RL%d" % (t - 1))
+        PL, last = "PL%d" % t, t == RO - 1
+        for c in range(4):
+            gath("VS", R("XG", 1 + 512 * c, 513 + 512 * c), win, R(lst, 32 * c, 32 * c + 32))
+        if t > 0:
+            a = R("ARR%d" % (t - 1))
+            copy("VS", R("ARB"), a)
+            copy("VS", R("D1F", 0, 512, 16), a, -1.0)
+            if not last:
+                copy("VS", R("NF", B, 128), a)
+            mm(R("P5", 0, U), R("BLKW"), R("ARB"))
+            ts(R("NZ", 128 * t + B, 128 * t + 128), R("P5", 0, U), 0.0, A.is_equal, 512.0, A.mult)
+        for c in range(4):
+            mm(R("P%d" % c), R("ID"), R("XG", 1 + 512 * c, 513 + 512 * c), True, False)
+        x0 = R("XG", 1, S, 16)
+        ts(R("BS"), x0, 0.0, A.is_equal, 512.0, A.mult)
+        mm(R("P6", 0, 128), x0, R("ID"))
+        copy("VS", R("BT"), R("P6", 0, 128))
+        for c in range(4):
+            x15 = R("XG", 16 + 512 * c, 513 + 512 * c, 16)
+            if not last:
+                copy("VS", R("X15", 32 * c, 32 * c + 32), x15)
+            fill(x15, BIG)
+            d1 = R("D1", 512 * c, 512 * c + 512) if c < 3 else R("D1F")
+            scan(R("EE", 512 * c, 512 * c + 512), R("XG", 512 * c, 512 * c + 512), d1, A.add, A.min)
+            mm(R("P%d" % c), R("BLKW"), R("EE", 512 * c, 512 * c + 512), False, True)
+            relu("VS", R("XK", 1 + 512 * c, 513 + 512 * c), R("P%d" % c))
+        for c in FUSED:
+            mm(R("P4"), R("BT"), R("E", 512 * c, 512 * c + 512))
+            copy("VS", R("BE", 512 * c, 512 * c + 512), R("P4"))
+        for c in PLAIN:
+            mm(R("P%d" % c), R("BT"), R("E", 512 * c, 512 * c + 512))
+
+        def fused(c):
+            m, b, p = R("CM", 512 * c, 512 * c + 512), R("BE", 512 * c, 512 * c + 512), R(PL, 32 * c, 32 * c + 32)
+            op("V", lambda e, z: e.tensor_tensor(ap(m), ap(R("XK")).indirect(ap(p)), ap(b), A.is_ge), [R("XK"), p, b], [m], 50 + 1.5 * 512)
+
+        for c in PLAIN:
+            gath("S", R("AB", 512 * c, 512 * c + 512), R("XK"), R(PL, 32 * c, 32 * c + 32))
+        for c in FUSED:
+            fused(c)
+        for c in PLAIN:
+            tt(R("CM", 512 * c, 512 * c + 512), R("AB", 512 * c, 512 * c + 512), R("P%d" % c), A.is_ge)
+        if not last:
+            tag[0] = "h%d" % t
+            for i in range(16):
+                mm(R("P5", 0, 128), R("ID"), R("XG", 1 + i, S, 16) if i < 15 else R("X15"), i == 0, i == 15)
+            tt(R("DD"), R("NF"), R("P5", 0, 128), A.subtract)
+            relu("VS", R("RD"), R("DD"))
+            mm(R("P5", 0, 128), R("BLKW"), R("RD"))
+            ts(R("UU"), R("P5", 0, 128), 0.1, A.is_gt)
+            scan(R("CN"), R("ONES", 0, 128), R("UU"), A.mult, A.add)
+            ts(R("WW"), R("UU"), -1000.0, A.mult, 999.0, A.add)
+            tt(R("OF0"), R("CN"), R("WW"), A.add)
+            tt(R("OFF"), R("OF0"), R("D32"), A.min)
+            wrap("P5", "OFF", 0, 8)
+            sl = "SL%d" % t
+            ts(R("DQ"), R("DD"), 0.0, A.max, 8388608.0, A.add)
+            fill(R(sl), 0.0)
+            copy("V", R("OL"), R("P5", 0, 8), 32.0, 0.0)
+
+            def put(e, z, sl=sl):
+                return e.tensor_scalar(ap(R(sl)).indirect(ap(R("OL"))), ap(R("DQ")), 1.0, -8388608.0, A.mult, A.add)
+            op("V", put, [R("OL"), R("DQ")], [R(sl)], 50 + TUNE["sc"] * 128)
+            rl = relay_of(rank)
+            m, k = emask(core, rl)
+            rid, pid = topo.addr(rl, core)
+            _, ka = emask(relay_of((rank - 1) % n), core)
+
+            def send(e, z, t=t, sl=sl, rid=rid, pid=pid, m=m):
+                return e.remote_dma(T["RB%d" % t][:, :], ap(R(sl, 0, U)), T.sem["rin%d" % t], T.sem["out%d" % t], pid, rid, m)
+            add("G", send, [R(sl, 0, U)], [R("ARR%d" % t)], 0.6, kind="m", lat=TUNE["rlat"], extra=("arr%d" % t, ka, "out%d" % t, k))
+            tag[0] = ""
+            needs(t + 1)
+            lists(t + 1)
+        mm(R("P6", 0, 128), R("ONES", 0, 128), R("CCON"), True, False)
+        mm(R("P6", 0, 128), R("BS"), R("BLKN"), False, False)
+        mm(R("P6", 0, 128), R("NZ", 128 * t, 128 * t + 128), R("BLKN"), False, False)
+        for i in range(16):
+            mm(R("P6", 15 - i, 128, 16), R("CM", i, S, 16), R("SELW"), False, i == 15)
+        tt(R("NFM"), R("P6", 0, 128), R("THR"), A.is_lt)
+        tt(R("KY"), R("P6", 0, 128), R("PT%d" % t), A.min)
+        scan(R("SC8"), R("NFM"), R("KY"), A.mult, A.max)
+        if last:
+            copy("V", R("C8"), R("SC8", 15, 128, 16), -1.0, 2050.0)
+        else:
+            copy("V", R("CI"), R("SC8", 15, 128, 16))
+            ts(R("PI"), R("CI"), 4095, A.bitwise_and)
+            copy("V", R("C8"), R("PI"), -1.0, 2050.0)
+        for q in range(8):
+            ts(R("DG", 128 * q, 128 * q + 128), R("IH"), R("C8", q, q + 1), A.mult)
+        for b in range(2):
+            mm(R("P%d" % (4 + b)), R("TRI"), R("DG", 512 * b, 512 * b + 512))
+        for q in range(8):
+            ts(R("EQ", 128 * q, 128 * q + 128), R("P%d" % (4 + q // 4), 128 * (q % 4), 128 * (q % 4) + 128), R("C8", q, q + 1), A.is_equal)
+        for q in range(8):
+            o = R("P6", 16 * q, 16 * q + 16)
+            mm(o, R("DG", 128 * q, 128 * q + 128), R("ONE16"), True, False)
+            mm(o, R("EQ", 128 * q, 128 * q + 128), R("F4K"), False, True)
+        tt(R("FM"), R("P6", 0, 128), R("DM"), A.min)
+        mm(R("P3", 0, 8), R("FM"), R("B16"))
+        copy("V", R("LU"), R("P3", 0, 8))
+        if not last:
+            gath("V", R("NV"), R("XK"), R("LU"))
+            tag[0] = "j%d" % t
+            mm(R("P2", 0, 128), R("I18"), R("XK", 1, S, 16))
+            gath("V", R("OJ"), R("JS"), R("S0L", 8 * t, 8 * t + 8))
+            tt(R("OJ"), R("OJ"), R("P2", 0, 128), A.min)
+            ts(R("SI"), R("CI"), 12, A.arith_shift_right)
+            copy("V", R("ST8"), R("SI"))
+            for q in range(8):
+                ts(R("FS", 16 * q, 16 * q + 16), R("M16", 0, 16), R("ST8", q, q + 1), A.mult)
+            ts(R("LOS"), R("P6", 0, 128), 2049.0, A.is_ge)
+            tt(R("LD"), R("LOS"), R("DM"), A.mult)
+            tt(R("FT"), R("FS"), R("LD"), A.max)
+            mm(R("P2", 0, 8), R("FT"), R("B16"))
+            copy("V", R("LS"), R("P2", 0, 8))
+            gath("V", R("NJ"), R("JS"), R("LS"))
+            tt(R("NJ"), R("NJ"), R("OJ"), A.max)
+            scat(R("JS"), R("S0L", 8 * t, 8 * t + 8), R("NJ"))
+            tag[0] = ""
+            scat(R("XK"), R("LU"), R("ZB"))
+            xd = R("XK", 1, S, 16)
+            tt(xd, xd, R("NV"), A.add)
+        else:
+            tag[0] = "y"
+            for c in range(4):
+                gath("VS", R("XT", 512 * c, 512 * c + 512), R("XK"), R("RL2", 32 * c, 32 * c + 32))
+            for c in range(4):
+                mm(R("P%d" % c), R("ONES", 0, 128), R("CY"), True, False)
+                mm(R("P%d" % c), R("I18N"), R("XT", 512 * c, 512 * c + 512), False, True)
+                tt(R("YY", 1 + 512 * c, 513 + 512 * c), R("JS", 512 * c, 512 * c + 512), R("P%d" % c), A.max)
+            tag[0] = ""
+            gath("V", R("NJ"), R("YY"), R("LU"))
+            scat(R("YY"), R("LU"), R("ZF"))
+            gath("V", R("OJ"), R("YY"), R("S0Y"))
+            tt(R("NJ"), R("NJ"), R("OJ"), A.min)
+            scat(R("YY"), R("S0Y"), R("NJ"))
+            for c in range(2):
+                dma("YS"[c], T.y[:, h * c:h * c + h], T.YY[0:128:16, 1 + h * c:1 + h * c + h], [R("YY", 1 + h * c, 1 + h * c + h)], [], 2.0)
+
+    at, on = order_of(ops)
+    m = len(ops)
+    cnt = {k: 0 for k in CS}
+    known = {k: {} for k in Q}
+    total = {}
+    done = [None] * m
+    nd = 0
+    for i in sorted(range(m), key=lambda i: (at[i], i)):
+        o = ops[i]
+        q = on[i]
+        need = {}
+        for j, e in o["edges"].items():
+            if e == 0 and on[j] == q and ops[j]["kind"] == "c" and o["kind"] == "c":
+                continue
+            need[done[j][0]] = max(need.get(done[j][0], 0), done[j][1])
+        for s in sorted(need):
+            if known[q].get(s, 0) < need[s]:
+                Q[q].wait_ge(T.sem[s], need[s])
+                known[q][s] = need[s]
+        ins = o["fn"](Q[q], q)
+        if o["kind"] == "c":
+            cnt[q] += 1
+            ins.then_inc(T.sem[CS[q]], 1)
+            done[i] = (CS[q], cnt[q])
+        elif o["kind"] == "d":
+            if o["x"] is None:
+                done[i] = ("d%d" % nd, 16)
+                nd += 1
+            else:
+                done[i] = o["x"]
+            ins.then_inc(T.sem[done[i][0]], 16)
+        else:
+            done[i] = (o["x"][0], o["x"][1])
+            total[o["x"][2]] = o["x"][3]
+        total[done[i][0]] = max(total.get(done[i][0], 0), done[i][1])
+    for s in sorted(total):
+        if known["G"].get(s, 0) < total[s]:
+            g.wait_ge(T.sem[s], total[s])

@@ -3,49 +3,51 @@ from concourse.mybir import AluOpType as A, ActivationFunctionType as F
 
 BF, FP, F16, I32, U16 = "bfloat16", "float32", "float16", "int32", "uint16"
 S, L, B, U, RO = 2048, 128, 96, 32, 3
-W = 2320
 BIG = 4096.0
+DUMP = 2050
+WW, WN = 4112, 2560
+KE = 8192.0
+WC = 4096.0
+MAGIC = 12582912.0
 NENG = 8
-FUSED, PLAIN = [2, 3], [0, 1]
 
 SCRATCH = {}
 for _n, _w, _d in [
-        ("SK", S, BF), ("OC", 128, I32), ("CD", 384, I32), ("ND", 288, BF), ("CV", S, I32), ("JS", W, I32),
-        ("CU", 384, U16), ("OU", 128, U16), ("SGU", 128, U16), ("CH", 384, F16), ("MS", 384, F16), ("S0L", 24, U16), ("S0Y", 8, U16),
-        ("CY", 512, BF), ("M16", 384, F16), ("DM", 128, FP), ("ONES", S, BF), ("THR", 128, FP), ("D32", 128, FP), ("DR", S, BF), ("E", S, BF),
-        ("HLF", 128, FP), ("HL", 128, BF), ("LO", 16, FP), ("IO", S, FP), ("INV0", S, FP), ("INV1", S, FP), ("INV2", S, FP),
-        ("ML", 384, U16), ("MH", 384, F16), ("PN", S, BF), ("RN", S, BF),
-        ("PL0", 128, U16), ("PL1", 128, U16), ("PL2", 128, U16), ("PT0", 128, FP), ("PT1", 128, FP), ("PT2", 128, FP),
-        ("RL0", 128, U16), ("RL1", 128, U16), ("RL2", 128, U16), ("XS", S, BF), ("XG", S + 16, BF), ("XK", W, BF), ("XT", S, BF),
-        ("X15", 128, BF), ("EE", S, BF), ("D1", 1536, BF), ("D1F", 512, FP), ("NF", 128, FP), ("NZ", 384, BF), ("BS", 128, BF), ("BT", 128, BF),
-        ("BE", S, BF), ("AB", S, BF), ("CM", S, BF), ("NFM", 128, FP), ("KY", 128, FP), ("SC8", 128, FP), ("C8", 8, FP), ("ST8", 8, FP),
-        ("DG", 1024, F16), ("EQ", 1024, F16), ("LU", 8, U16), ("LS", 8, U16), ("NV", 128, BF), ("NJ", 128, FP), ("OJ", 128, FP),
-        ("ZB", 128, BF), ("ZF", 128, FP), ("DD", 128, FP), ("RD", 128, BF), ("UU", 128, FP), ("CN", 128, FP), ("WW", 128, FP), ("OF0", 128, FP),
-        ("OFF", 128, BF), ("DQ", 128, FP), ("OL", 8, U16), ("SL0", 256, FP), ("SL1", 256, FP), ("ARR0", U, FP), ("ARR1", U, FP),
-        ("RB0", U, FP), ("RB1", U, FP), ("ARB", U, BF), ("YY", W, FP)]:
+        ("SK", S, BF), ("SKF", S, FP), ("OC", 128, I32), ("CD", 384, I32), ("ND", 288, BF), ("CV", S, I32),
+        ("W", WW, FP), ("FW", WW, BF), ("XG", S + 16, BF), ("EE", S, BF), ("D1", 1536, BF), ("D1F", 512, FP), ("CM", S, BF), ("FL", S, BF),
+        ("ZR", 1024, FP), ("MK0", 512, BF), ("MK1", 512, BF), ("MK2", 512, BF), ("TH", 512, BF), ("RI", 512, I32), ("RH", 512, F16),
+        ("OH", 128, F16), ("OT", 128, F16), ("OU", 128, U16), ("CU", 384, U16), ("CH", 384, F16), ("CT", 384, F16), ("CB", 384, FP),
+        ("SL", 48, U16), ("MH", 384, F16), ("MT", 384, F16), ("ML", 384, U16), ("PT", 384, FP), ("NZ", 384, BF), ("BS", 128, BF),
+        ("LF", 128, FP), ("LL", 128, U16), ("X15", 128, BF), ("KY", 128, FP), ("SC", 128, FP), ("DG", 1024, F16), ("EQ", 1024, F16),
+        ("FM", 256, F16), ("LU", 16, U16), ("VV", 256, FP), ("RF", 128, FP), ("ZZ", 128, BF), ("UU", 128, BF), ("CN", 128, BF),
+        ("OL", 8, U16), ("SB0", 512, FP), ("SB1", 512, FP), ("ARR0", U, FP), ("ARR1", U, FP), ("RB0", U, FP), ("RB1", U, FP),
+        ("YC", 128, FP), ("YI", 128, I32), ("YJ", 128, I32), ("YO", 128, FP),
+        ("WX", 256, FP), ("W1", 128, I32), ("T1", 128, I32), ("NI", 512, BF), ("BK2", 256, BF), ("S0R", 256, F16), ("DM", 256, FP),
+        ("I4F", 128, FP), ("BKF", 128, FP), ("CC", 256, BF), ("W3", 256, I32), ("W4", 128, I32)]:
     SCRATCH[_n] = ("sbuf", [128, _w], _d)
 PARTS = {}
 for _b, _d, _l in [
-        ("GI", I32, [("TA", 128), ("TB", 128), ("TC", 128), ("W1", 128), ("W2", 128), ("W3", 128), ("W4", 128), ("T1", 128), ("T3", 128),
-                     ("T2", 8), ("CI", 8), ("PI", 8), ("SI", 8), ("IP", 8), ("IQ", 8)]),
-        ("GF", FP, [("LOF", 16), ("PO", 8), ("PV", 8), ("DCOL", 8), ("CYA", 8), ("CYB", 8), ("CYC", 8)]),
-        ("GB", BF, [("ID", 128), ("I18", 128), ("I18N", 128), ("BLKW", 128), ("BLKN", 128), ("CCON", 128), ("SELW", 8), ("SEL2", 8)]),
-        ("GH", F16, [("IH", 128), ("PM1", 128), ("PM4", 128), ("S0R", 128), ("TRI", 128), ("PH", 128), ("FS", 128), ("LOS", 128), ("LD", 128),
-                     ("FT", 128), ("FM", 128), ("B16", 16), ("ONE16", 16), ("F4K", 16)])]:
+        ("GI", I32, [("IP", 8), ("IA", 8), ("IB", 8)]),
+        ("GF", FP, [("PR", 8), ("PX", 8), ("PY", 8), ("PU", 8), ("PM", 8), ("PN", 8), ("PD", 8), ("PE", 8), ("PZ", 8)]),
+        ("GB", BF, [("I4", 128), ("Z", 144), ("BK", 128), ("SW", 48), ("ONE", 128), ("RP", 128)]),
+        ("GH", F16, [("IH", 128), ("PV", 128), ("TRI", 128), ("Q00", 128), ("Q01", 128), ("Q10", 128), ("Q11", 128), ("B16", 16),
+                     ("O32", 32), ("K32", 32), ("C14", 128)])]:
     _o = 0
     for _n, _w in _l:
-        PARTS[_n] = (_b, _o, {"IP": 1, "IQ": 1, "PO": 1, "PV": 1, "DCOL": 1, "CYA": 1, "CYB": 1, "CYC": 1, "B16": 8}.get(_n, _w))
+        PARTS[_n] = (_b, _o, 1 if _b in ("GI", "GF") else {"B16": 8}.get(_n, _w))
         _o += _w
     SCRATCH[_b] = ("sbuf", [128, _o], _d)
 for _k in range(8):
     SCRATCH["P%d" % _k] = ("psum", [128, 512], FP)
-SEMAPHORES = ["cV", "cS", "cP", "cG", "dJ"] + ["d%d" % k for k in range(10)] + ["arr0", "arr1", "rin0", "rin1", "out0", "out1"]
+SEMAPHORES = ["cV", "cS", "cP", "cG"] + ["d%d" % k for k in range(20)] + ["arr0", "arr1", "rin0", "rin1", "out0", "out1"]
 
-TUNE = {"sc": 3.0, "rlat": 6.0, "hop": 0.12, "own": 0.06, "trials": 400}
+TUNE = {"f": 1.1, "g": 1.3, "sc": 2.5, "pe": 0.7, "rlat": 6.0, "hop": 0.12, "own": 0.08, "pv": 0.3,
+        "gath": [(0, 32, "V"), (32, 64, "S"), (64, 96, "S"), (96, 128, "S")],
+        "wrap": [(0, 64), (64, 128)], "cut": 64, "cov": 4, "b": {}}
 ORDER = {}
 
 
-def arrange(ops, pr):
+def arrange(ops):
     m, hop = len(ops), TUNE["hop"]
     succ = [[] for _ in range(m)]
     for i, o in enumerate(ops):
@@ -55,8 +57,7 @@ def arrange(ops, pr):
     for i in range(m - 1, -1, -1):
         o = ops[i]
         up[i] = o["cost"] + max([up[j] + (0.0 if ops[j]["edges"][i] == 0 and ops[j]["q"] == o["q"] else hop + o["lat"]) for j in succ[i]] + [o["lat"]])
-    jit = pr["jit"] * np.random.default_rng(pr["seed"]).standard_normal(m)
-    key = [up[i] + pr["b"].get(ops[i]["tag"], 0.0) + float(jit[i]) for i in range(m)]
+    key = [up[i] + TUNE["b"].get(ops[i]["tag"], 0.0) for i in range(m)]
     left = [len(o["edges"]) for o in ops]
     ready = [i for i in range(m) if not left[i]]
     slots = {k: [] for k in "VSPGY"}
@@ -81,7 +82,7 @@ def arrange(ops, pr):
                 if s + o["cost"] <= a:
                     break
                 s = max(s, b)
-            pen = s + o["cost"] + (pr["pv"] if q == "V" and len(o["q"]) > 1 else 0.0)
+            pen = s + o["cost"] + (TUNE["pv"] if q == "V" and len(o["q"]) > 1 else 0.0)
             if best is None or pen < best[0] - 1e-9:
                 best = (pen, s, q)
         _, s, q = best
@@ -89,27 +90,6 @@ def arrange(ops, pr):
         slots[q].append((s, s + o["cost"]))
         slots[q].sort()
     return max(end), at, on
-
-
-def order_of(ops):
-    if "at" not in ORDER:
-        r = np.random.default_rng(1)
-        best, pr = None, {"pv": 1.5, "jit": 0.0, "seed": 0, "b": {}}
-        for k in range(TUNE["trials"]):
-            p = dict(pr, b=dict(pr["b"]))
-            if k:
-                c = int(r.integers(4))
-                if c == 0:
-                    p["seed"], p["jit"] = int(r.integers(1000000)), float(r.choice([0.0, 0.2, 0.5, 1.0]))
-                elif c == 1:
-                    p["pv"] = float(r.choice([0.3, 0.6, 1.0, 1.5, 2.0]))
-                else:
-                    p["b"][str(r.choice(["i0", "i1", "i2", "p0", "p1", "p2", "n0", "n1", "n2", "h0", "h1", "j0", "j1", "y"]))] = float(3 - 14 * r.random())
-            e = arrange(ops, p)
-            if best is None or e[0] < best[0]:
-                best, pr = e, p
-        ORDER["end"], ORDER["at"], ORDER["on"] = best
-    return ORDER["at"], ORDER["on"]
 
 
 def rank_program(g, core, T, topo):
@@ -145,14 +125,14 @@ def rank_program(g, core, T, topo):
     CS = {"V": "cV", "S": "cS", "P": "cP", "G": "cG"}
     ops, acc, tag = [], {}, [""]
 
-    def R(name, lo=0, hi=None, st=1):
+    def R(name, lo=0, hi=None, st=1, rows=128):
         if name in PARTS:
             b, o, w = PARTS[name]
-            return (b, o + lo, o + (w if hi is None else hi), st)
-        return (name, lo, SCRATCH[name][1][-1] if hi is None else hi, st)
+            return (b, o + lo, o + (w if hi is None else hi), st, rows)
+        return (name, lo, SCRATCH[name][1][-1] if hi is None else hi, st, rows)
 
     def ap(r):
-        return T[r[0]][:, r[1]:r[2]:r[3]] if r[3] != 1 else T[r[0]][:, r[1]:r[2]]
+        return T[r[0]][0:r[4], r[1]:r[2]:r[3]] if r[3] != 1 else T[r[0]][0:r[4], r[1]:r[2]]
 
     def psum(name):
         return SCRATCH[name][0] == "psum"
@@ -182,7 +162,7 @@ def rank_program(g, core, T, topo):
                         edges[j] = max(edges.get(j, 0), 0)
                     continue
                 e = 0 if k == "w" and chain else 1
-                if psum(rr[0]) and q == "P" and ops[j]["q"] == "P" and (rr[1] >= o[2] or o[1] >= rr[2]):
+                if psum(rr[0]) and q == "P" and ops[j]["q"] == "P" and (rr[1] >= o[2] or o[1] >= rr[2] or (rr[3] == o[3] > 1 and (rr[1] - o[1]) % rr[3])):
                     e = 0
                 edges[j] = max(edges.get(j, 0), e)
         for rr, k in mine:
@@ -198,10 +178,10 @@ def rank_program(g, core, T, topo):
         ops.append({"tag": tag[0], "q": q, "fn": fn, "cost": cost, "edges": edges, "kind": kind, "lat": lat, "x": extra})
 
     def op(q, fn, reads, writes, cyc, chain=False):
-        add(q, fn, reads, writes, (0.02 + max(cyc, 64) * 0.00083) * 1.2, chain)
+        add(q, fn, reads, writes, 0.03 + max(cyc, 64) * 0.00083 * TUNE["f"], chain)
 
-    def dma(q, out, in_, reads, writes, lat, group=None):
-        add(q, lambda e, z: e.dma_start(out, in_), reads, writes, 0.1, kind="d", lat=lat, extra=group)
+    def dma(q, out, in_, reads, writes, lat):
+        add(q, lambda e, z: e.dma_start(out, in_), reads, writes, 0.1, kind="d", lat=lat)
 
     def copy(q, o, i, scale=1.0, bias=0.0):
         def f(e, z):
@@ -210,10 +190,10 @@ def rank_program(g, core, T, topo):
                     return e.tensor_copy(ap(o), ap(i))
                 return e.tensor_scalar(ap(o), ap(i), float(scale), float(bias), A.mult, A.add)
             return e.activation(ap(o), ap(i), F.Copy if bias == 0.0 else F.Identity, bias=float(bias), scale=float(scale))
-        op(q, f, [i], [o], width(i))
+        op(q, f, [i], [o], width(i) * (0.5 if q == "V" and two(o, i) else 1))
 
-    def relu(q, o, i):
-        op(q, lambda e, z: e.tensor_scalar(ap(o), ap(i), 0.0, None, A.max) if z == "V" else e.activation(ap(o), ap(i), F.Relu), [i], [o], width(i))
+    def act(o, i, func, scale=1.0, bias=0.0):
+        op("S", lambda e, z: e.activation(ap(o), ap(i), func, bias=float(bias), scale=float(scale)), [i], [o], width(i))
 
     def ts(o, i, s1, op0, s2=None, op1=None):
         rd, a1, a2 = [i], s1, s2
@@ -242,235 +222,204 @@ def rank_program(g, core, T, topo):
         op("V", lambda e, z: e.tensor_tensor_scan(ap(o), ap(a), ap(b), 0.0, op0, op1), [a, b], [o], width(o) * (0.5 if two(o, a, b) else 1))
 
     def mm(o, l, r, start=True, stop=True):
-        op("P", lambda e, z: e.matmul(ap(o), ap(l), ap(r), start, stop), [l, r], [o], max(min(64, width(l)), width(r)) * 0.86, chain=not start)
+        c = max(min(64, width(l)), width(r)) * (1 if two(l) else 4)
+        add("P", lambda e, z: e.matmul(ap(o), ap(l), ap(r), start, stop), [l, r], [o], c * TUNE["pe"] * 0.001 * TUNE["f"], not start)
 
     def gath(q, o, win, lst):
         op(q, lambda e, z: e.tensor_copy(ap(o), ap(win).indirect(ap(lst))) if z == "V" else
-           e.activation(ap(o), ap(win).indirect(ap(lst)), F.Copy), [win, lst], [o], 50 + 1.5 * width(o))
+           e.activation(ap(o), ap(win).indirect(ap(lst)), F.Copy), [win, lst], [o], 40 + TUNE["g"] * width(o))
 
-    def scat(win, lst, i):
-        op("V", lambda e, z: e.tensor_copy(ap(win).indirect(ap(lst)), ap(i)), [lst, i], [win], 50 + TUNE["sc"] * width(i))
+    def scat(q, win, lst, i):
+        op(q, lambda e, z: e.tensor_copy(ap(win).indirect(ap(lst)), ap(i)) if z == "V" else
+           e.activation(ap(win).indirect(ap(lst)), ap(i), F.Silu), [lst, i], [win], 40 + TUNE["sc"] * width(i))
 
-    def place(win, lst, i):
-        op("VS", lambda e, z: e.tensor_copy(ap(win).indirect(ap(lst)), ap(i)) if z == "V" else
-           e.activation(ap(win).indirect(ap(lst)), ap(i), F.Silu), [lst, i], [win], 50 + TUNE["sc"] * width(i))
-
-    def iota(o, pat, base, cm, fl=False):
-        if fl:
-            op("G", lambda e, z: e.iota(ap(o), pat, base, cm, allow_small_or_imprecise_dtypes=True), [], [o], 150 + 2 * width(o))
-        else:
+    def iota(o, pat, base, cm):
+        if SCRATCH[o[0]][2] == I32:
             op("G", lambda e, z: e.iota(ap(o), pat, base, cm), [], [o], 150 + 2 * width(o))
+        else:
+            op("G", lambda e, z: e.iota(ap(o), pat, base, cm, allow_small_or_imprecise_dtypes=True), [], [o], 150 + 2 * width(o))
 
-    def wrap(bank, src, k0, k1):
-        for r in range(16):
-            mm(R(bank, 0, k1 - k0), R("DR", 128 * r, 128 * r + 128), R(src, 16 * k0 + r, 16 * k1, 16), r == 0, r == 15)
+    def vtr(o, i):
+        op("V", lambda e, z: e.transpose(ap(o), ap(i)), [i], [o], width(o) * 0.5)
 
-    h = S // 2
-    dma("Y", T.CD[:, 0:128], T.cards[:, 0:128], [], [R("CD", 0, 128)], 2.4)
-    dma("S", T.SK[:, 0:h], T.skill[:, 0:h], [], [R("SK", 0, h)], 3.5)
-    dma("Y", T.OC[:, :], T.occ[:, :], [], [R("OC")], 2.6)
-    dma("S", T.SK[:, h:S], T.skill[:, h:S], [], [R("SK", h, S)], 4.5)
-    dma("Y", T.ND[:, :], T.need[:, :], [], [R("ND")], 5.0)
-    dma("Y", T.CD[:, 128:384], T.cards[:, 128:384], [], [R("CD", 128, 384)], 5.5)
-    dma("Y", T.CV[:, :], T.cover[:, :], [], [R("CV")], 9.0)
-    for q in range(16):
-        dma("Y", T.JS[q:128:16, 0:S], T.occ[:, :], [], [R("JS", q * 128, q * 128 + 128)], 12.0, ("dJ", 256))
+    def turn(bank, src, c0):
+        for b in range(4):
+            for x in range(2):
+                for y in range(2):
+                    mm(R(bank, 2 * b + x, 128, 8), R("Q%d%d" % (x, y)), R(src, c0 + 32 * b + 16 * y, c0 + 32 * b + 16 * y + 16), y == 0, y == 1)
+
+    def Z(i):
+        return R("Z", 15 - i, 143 - i)
+
+    dma("Y", T.OC[:, :], T.occ[:, :], [], [R("OC")], 2.0)
+    for c in range(4):
+        dma("SY"[c % 2], T.SK[:, 512 * c:512 * c + 512], T.skill[:, 512 * c:512 * c + 512], [], [R("SK", 512 * c, 512 * c + 512)], 2.4 + 0.4 * c)
+    dma("S", T.CD[:, :], T.cards[:, :], [], [R("CD")], 4.2)
+    dma("Y", T.ND[:, :], T.need[:, :], [], [R("ND")], 4.5)
+    dma("Y", T.CV[:, :], T.cover[:, :], [], [R("CV")], 7.5)
 
     iota(R("IP"), [[0, 1]], 0, 1)
-    iota(R("HLF"), [[1024, 128]], 0, 0, True)
-    iota(R("LOF"), [[64, 16]], 64, 0, True)
+    iota(R("WX"), [[1, 256]], -64, -1)
+    iota(R("RI"), [[-1, 512]], 511, 0)
     iota(R("W1"), [[-16, 8], [0, 16]], 0, 1)
-    iota(R("W2"), [[-1, 128]], 0, 1)
-    iota(R("W3"), [[0, 8], [-1, 16]], 0, 1)
     iota(R("W4"), [[-16, 8], [1, 16]], -15, 1)
-    iota(R("DCOL"), [[0, 1]], 2050, 2, True)
-    iota(R("D32"), [[1, 128]], 128, 0, True)
-    fill(R("ONES"), 1.0)
-    fill(R("DR"), 0.0, "G")
-    fill(R("D1"), 0.0, "G")
-    fill(R("D1F"), 0.0, "G")
-    op("G", lambda e, z: e.affine_select(ap(R("E")), ap(R("ONES")), [[-1, 128], [0, 16]], A.is_equal, 0.0, 0, 1), [R("ONES")], [R("E")], 200 + 2 * S)
-    ts(R("T2"), R("W1", 0, 128, 16), 1, A.arith_shift_right)
-    ts(R("SEL2"), R("T2"), 0.0, A.is_equal, 1.0 / 64, A.mult)
-    for r in range(16):
-        copy("VS", R("DR", 128 * r + r, 128 * r + 128, 16), R("SEL2"))
-    ts(R("IQ"), R("IP"), 1, A.bitwise_and)
-    copy("V", R("PO"), R("IQ"))
-    copy("V", R("PV"), R("IQ"), -1.0, 1.0)
-    ts(R("HL"), R("HLF"), R("PV"), A.mult)
-    ts(R("LO"), R("LOF"), R("PO"), A.mult)
-
-    def io_col(i):
-        o, b = R("IO", i, S, 16), R("LO", i, i + 1)
-        op("VS", lambda e, z: e.tensor_scalar(ap(o), ap(R("HL")), ap(b), None, A.add) if z == "V" else
-           e.activation(ap(o), ap(R("HL")), F.Identity, bias=ap(b)), [R("HL"), b], [o], 128)
-
-    for i in range(16):
-        io_col(i)
-    copy("V", R("CU", 0, 128), R("CD", 0, 128))
-    ts(R("TA"), R("CD", 0, 128), 127, A.bitwise_and)
-    ts(R("TB"), R("CD", 0, 128), 7, A.arith_shift_right)
-    ts(R("TC"), R("TA"), 16.0, A.mult)
-    tt(R("TA"), R("TC"), R("TB"), A.add)
-    copy("V", R("SGU"), R("TA"))
-    copy("V", R("OU"), R("OC"))
-    ts(R("ID"), R("W2"), 0.0, A.is_equal)
-    ts(R("T1"), R("W1"), 4, A.arith_shift_right)
-    ts(R("BLKW"), R("T1"), 0.0, A.is_equal, 512.0, A.mult)
-    fill(R("XG", 0, 1), BIG)
-    fill(R("XK", 0, 1), 0.0)
-    fill(R("XK", S + 1, W), 0.0)
-    ts(R("SK", 0, h), R("SK", 0, h), 1.0 / 64, A.max)
-    ts(R("SK", h, S - 1), R("SK", h, S - 1), 1.0 / 64, A.max)
+    iota(R("W3"), [[0, 8], [-1, 16], [0, 2]], 128, 1)
+    iota(R("RP"), [[1, 128]], 129, 0)
+    D0 = R("WX", 64, 192)
+    ts(R("IA"), R("IP"), 4, A.arith_shift_right, 1, A.bitwise_and)
+    copy("V", R("PX"), R("IA"))
+    copy("V", R("PY"), R("IA"), -1.0, 1.0)
+    ts(R("Q00"), D0, 0.0, A.is_equal, R("PY"), A.mult)
+    ts(R("Q11"), D0, 0.0, A.is_equal, R("PX"), A.mult)
+    ts(R("Q01"), D0, 16.0, A.is_equal, R("PY"), A.mult)
+    ts(R("Q10"), D0, -16.0, A.is_equal, R("PX"), A.mult)
+    ts(R("I4"), D0, 0.0, A.is_equal, 4.0, A.mult)
+    fill(R("C14"), 2.0 ** -14)
+    copy("V", R("RH", rows=32), R("RI", rows=32))
+    copy("V", R("OH"), R("OC"))
+    vtr(R("OT"), R("OH"))
+    turn("P7", "OT", 0)
+    copy("V", R("OU"), R("P7", 0, 128))
     for c in range(4):
-        gath("VS", R("XS", 512 * c, 512 * c + 512), R("SK"), R("OU", 32 * c, 32 * c + 32))
+        mm(R("P%d" % c), R("C14", rows=1), R("RH", rows=1), True, False)
+        mm(R("P%d" % c), R("I4"), R("SK", 512 * c, 512 * c + 512), False, True)
+        copy("VS", R("SKF", 512 * c, 512 * c + 512), R("P%d" % c), 0.25, (3 - c) / 128.0)
+    for c in range(4):
+        gath("VS", R("W", 512 * c, 512 * c + 512), R("SKF"), R("OU", 32 * c, 32 * c + 32))
+    fill(R("W", S, S + 1), BIG)
+    fill(R("W", S + 1, WN), 0.0)
+    fill(R("XG", 0, 1), BIG)
+    fill(R("ZR", 0, 512), 0.0)
+    act(R("D1F"), R("ZR", 0, 512), F.Silu)
+    copy("S", R("ZR", 512, 1024), R("ZR", 0, 512))
+    for c in range(3):
+        copy("S", R("D1", 512 * c, 512 * c + 512), R("ZR", 0, 512))
+    copy("S", R("VV", 0, 128), R("ZR", 0, 128))
+    fill(R("FW", 0, S), 0, "G")
+    for t in range(RO):
+        fill(R("MK%d" % t), t + 1, "G")
+    ts(R("IB"), R("IP"), 15, A.bitwise_and)
+    copy("V", R("PU"), R("IB"), -1.0, -49.0)
+    ts(R("Z"), R("WX", 0, 144), R("PU"), A.is_equal, KE, A.mult)
+    ts(R("PM"), R("IB"), 15.0, A.is_lt)
+    copy("V", R("PN"), R("PM"), -float(S), float(S))
+    ts(R("CU"), R("CD"), R("PM"), A.mult, R("PN"), A.add)
+    copy("V", R("CH"), R("CD"), 1.0, 1.0)
+    copy("V", R("CB"), R("CD"), 1.0, 1.0 - DUMP)
+    ts(R("IH"), D0, 0.0, A.is_equal)
+    vtr(R("CT"), R("CH"))
+    for u, i in enumerate((0, 15)):
+        for x in range(2):
+            for y in range(2):
+                mm(R("P7", 24 * u + x, 24 * u + 24, 2), R("Q%d%d" % (x, y)), R("CT", 16 * y + i, 384, 32), y == 0, y == 1)
+    copy("V", R("SL"), R("P7", 0, 48), 1.0, -1.0)
+    op("V", lambda e, z: e.tensor_scalar(ap(R("MH")), ap(R("CV")).indirect(ap(R("SL", 0, 24))), 1.0, None, A.add), [R("CV"), R("SL", 0, 24)], [R("MH")],
+       40 + TUNE["g"] * 384)
+    vtr(R("MT"), R("MH"))
+    ts(R("PV"), R("W4"), 0.0, A.is_equal)
+    for t in range(RO):
+        tag[0] = "m%d" % t
+        turn("P7", "MT", 128 * t)
+        copy("V", R("ML", 128 * t, 128 * t + 128), R("P7", 0, 128), 1.0, -1.0)
+        mm(R("P7", 0, 128), R("MH", 128 * t, 128 * t + 128), R("PV"))
+        copy("VS", R("PT", 128 * t, 128 * t + 128), R("P7", 0, 128))
+    tag[0] = ""
+    ts(R("T1"), R("W1"), 4, A.arith_shift_right)
+    ts(R("BK"), R("T1"), 0.0, A.is_equal)
+    ts(R("BKF"), R("T1"), 0.0, A.is_equal, -1024.0, A.mult)
+    ts(R("I4F"), D0, 0.0, A.is_equal, 4.0, A.mult)
+    t8 = R("T1", 0, 128, 16)
+    for k, w in enumerate((-WC, WC, -WC, 0.0, WC, 0.0)):
+        ts(R("SW", 8 * k, 8 * k + 8), t8, 0.0, A.is_equal, w, A.mult)
+    ts(R("B16"), t8, 0.0, A.is_equal)
+    ts(R("BK2", 0, 128), R("T1"), 0.0, A.is_equal, -WC, A.mult)
+    ts(R("BK2", 128, 256), R("T1"), 0.0, A.is_equal, WC, A.mult)
+    fill(R("BK2", 128, 256, 16), 0.0)
+    fill(R("ONE"), 1.0)
+    fill(R("CC", 0, 128, rows=32), -9.5 * WC)
+    fill(R("CC", 128, 256, rows=32), 9.5 * WC)
+    fill(R("CC", 128, 256, 16, rows=32), -1.0)
+    ts(R("TRI"), D0, 0.0, A.is_lt)
+    op("G", lambda e, z: e.affine_select(ap(R("NI")), ap(R("ZR", 0, 512)), [[0, 4], [-1, 128]], A.not_equal, -0.25, 0, 1), [R("ZR", 0, 512)], [R("NI")], 200 + 1024)
+    ts(R("S0R", 0, 256, 2), R("W1"), 0.0, A.mult)
+    ts(R("S0R", 1, 256, 2), R("W1"), 0.0, A.is_equal)
+    ts(R("O32", 0, 32, 2), R("W1", 0, 16), 0.0, A.mult, 1.0, A.add)
+    ts(R("O32", 1, 32, 2), R("W1", 0, 16), 0.0, A.mult)
+    ts(R("K32"), R("W1", 0, 32), 0.0, A.mult, 4096.0, A.add)
+    ts(R("W3"), R("W3"), 15, A.bitwise_and)
+    copy("V", R("PD"), R("IP"), 2.0, 2050.0)
+    copy("V", R("PE"), R("IP"), 2.0, 2306.0)
+    ts(R("DM", 0, 256, 2), R("W3", 0, 256, 2), 0.0, A.is_equal, R("PD"), A.mult)
+    ts(R("DM", 1, 256, 2), R("W3", 1, 256, 2), 0.0, A.is_equal, R("PE"), A.mult)
+    mm(R("P6", 0, 288), R("BK"), R("ND"))
+    for t in range(RO):
+        act(R("NZ", 128 * t, 128 * t + B), R("P6", B * t, B * t + B), F.Relu, -1.0, 1.0)
+    fill(R("NZ", B, 128), 1.0)
+    for t in range(RO - 1):
+        copy("S", R("SB%d" % t, 0, U), R("ZR", 0, U), 1.0, -MAGIC)
 
-    def needs(t):
+    cut = TUNE["cut"]
+    for t in range(RO):
+        last = t == RO - 1
+        WG, WS = R("W", 0, S + 1), R("W")
         copy("VS", R("D1", 0, 1536, 16), R("ND", B * t, B * t + B), -1.0)
-        if t < RO - 1:
-            copy("VS", R("NF", 0, B), R("ND", B * t, B * t + B))
-
-    needs(0)
-    mm(R("P7", 0, 288), R("BLKW"), R("ND"))
-    for t in range(RO):
-        ts(R("NZ", 128 * t, 128 * t + B), R("P7", B * t, B * t + B), 0.0, A.is_equal, 512.0, A.mult)
-    fill(R("NZ", B, 128), 512.0)
-    fill(R("NF", B, 128), 0.0)
-    copy("V", R("CU", 128, 384), R("CD", 128, 384))
-    copy("V", R("CH"), R("CD"))
-    ts(R("S0R"), R("W1"), 0.0, A.is_equal)
-    ts(R("B16"), R("T1", 0, 128, 16), 0.0, A.is_equal)
-    ts(R("T3"), R("W3"), 15, A.bitwise_and)
-    for t in range(RO):
-        ts(R("M16", 128 * t, 128 * t + 128), R("T3"), 0.0, A.is_equal)
-    for t in range(RO):
-        mm(R("P6", 128 * t, 128 * t + 128), R("CH", 128 * t, 128 * t + 128), R("S0R"))
-    tt(R("MS"), R("P6", 0, 384), R("M16"), A.mult)
-    for t in range(RO):
-        mm(R("P6", 8 * t, 8 * t + 8), R("MS", 128 * t, 128 * t + 128), R("B16"))
-    copy("V", R("S0L"), R("P6", 0, 24))
-    copy("V", R("S0Y"), R("P6", 16, 24), 1.0, 1.0)
-    for t in range(RO):
-        gath("V", R("ML", 128 * t, 128 * t + 128), R("CV"), R("S0L", 8 * t, 8 * t + 8))
-        copy("V", R("MH", 128 * t, 128 * t + 128), R("ML", 128 * t, 128 * t + 128))
-    ts(R("PM1"), R("W4"), 0.0, A.is_equal, -1.0, A.mult)
-    ts(R("PM4"), R("W4"), 0.0, A.is_equal, 4096.0, A.mult)
-    ts(R("SELW"), R("T1", 0, 128, 16), 0.0, A.is_equal, 67108864.0, A.mult)
-    ts(R("BLKN"), R("T1"), 0.0, A.is_equal, -262144.0, A.mult)
-    ts(R("I18"), R("W2"), 0.0, A.is_equal, 262144.0, A.mult)
-    ts(R("I18N"), R("W2"), 0.0, A.is_equal, -262144.0, A.mult)
-    ts(R("IH"), R("W2"), 0.0, A.is_equal)
-    ts(R("TRI"), R("W2"), 0.0, A.is_gt)
-    ts(R("DM"), R("T3"), 0.0, A.is_equal, R("DCOL"), A.mult)
-    ts(R("ONE16"), R("W2", 0, 16), 0.0, A.mult, 1.0, A.add)
-    ts(R("F4K"), R("W2", 0, 16), 0.0, A.mult, 4096.0, A.add)
-    fill(R("CCON"), -4980736.0)
-    fill(R("THR"), 0.0)
-    fill(R("THR", 0, 128, 16), -9.0e9)
-    fill(R("ZB"), 0.0)
-    fill(R("ZF"), 2047.0)
-    fill(R("JS", S, W), 0)
-    fill(R("YY", 0, 1), 2047.0)
-    fill(R("YY", S + 1, W), 2047.0)
-    ts(R("CYA"), R("W2", 0, 1), 0.0, A.is_equal, 2048.0, A.mult)
-    ts(R("CYB"), R("W2", 0, 1), 1.0, A.is_equal, -1.0, A.mult)
-    tt(R("CYC"), R("CYA"), R("CYB"), A.add)
-    ts(R("CY"), R("ONES", 0, 512), R("CYC"), A.mult)
-
-    def lists(t):
-        tag[0] = "i%d" % t
-        for p in range(8):
-            place(R("INV%d" % t), R("CU", 128 * t + 16 * p, 128 * t + 16 * p + 16), R("IO", 256 * p, 256 * p + 256))
-        tag[0] = "p%d" % t
-        for c in range(4):
-            gath("VS", R("PN", 512 * c, 512 * c + 512), R("INV%d" % t), R("ML", 128 * t + 32 * c, 128 * t + 32 * c + 32))
-        wrap("P7", "PN", 0, 128)
-        copy("V", R("PL%d" % t), R("P7", 0, 128))
-        if t < RO - 1:
-            copy("V", R("PH"), R("P7", 0, 128))
-            mm(R("P7", 0, 128), R("PH"), R("PM1"), True, False)
-            mm(R("P7", 0, 128), R("MH", 128 * t, 128 * t + 128), R("PM4"), False, True)
-            copy("VS", R("PT%d" % t), R("P7", 0, 128), 1.0, 2050.0)
-        else:
-            mm(R("P7", 0, 128), R("MH", 128 * t, 128 * t + 128), R("PM1"))
-            copy("VS", R("PT%d" % t), R("P7", 0, 128), 1.0, 2049.0)
-        tag[0] = "n%d" % t
-        for c in range(4):
-            if t < RO - 1:
-                gath("VS", R("RN", 512 * c, 512 * c + 512), R("INV%d" % t), R("CU", 128 * t + 128 + 32 * c, 128 * t + 160 + 32 * c))
-            else:
-                copy("VS", R("RN", 512 * c, 512 * c + 512), R("INV2", 512 * c, 512 * c + 512))
-        wrap("P7", "RN", 0, 128)
-        copy("V", R("RL%d" % t), R("P7", 0, 128))
-        tag[0] = ""
-
-    lists(0)
-
-    for t in range(RO):
-        win, lst = (R("XS"), "SGU") if t == 0 else (R("XK"), "RL%d" % (t - 1))
-        PL, last = "PL%d" % t, t == RO - 1
-        for c in range(4):
-            gath("VS", R("XG", 1 + 512 * c, 513 + 512 * c), win, R(lst, 32 * c, 32 * c + 32))
         if t > 0:
-            a = R("ARR%d" % (t - 1))
-            copy("VS", R("ARB"), a)
-            copy("VS", R("D1F", 0, 512, 16), a, -1.0)
-            if not last:
-                copy("VS", R("NF", B, 128), a)
-            mm(R("P5", 0, U), R("BLKW"), R("ARB"))
-            ts(R("NZ", 128 * t + B, 128 * t + 128), R("P5", 0, U), 0.0, A.is_equal, 512.0, A.mult)
-        for c in range(4):
-            mm(R("P%d" % c), R("ID"), R("XG", 1 + 512 * c, 513 + 512 * c), True, False)
+            copy("VS", R("D1F", 0, 512, 16), R("ARR%d" % (t - 1)), 1.0, MAGIC)
+            mm(R("P5", 0, U), R("BKF"), R("D1F", 0, 512, 16))
+            act(R("NZ", 128 * t + B, 128 * t + 128), R("P5", 0, U), F.Relu, -1.0, 1.0)
+        for (a, b, q) in TUNE["gath"]:
+            gath(q, R("XG", 1 + 16 * a, 1 + 16 * b), WG, R("CU", 128 * t + a, 128 * t + b))
+        if not last:
+            gath("VS", R("X15"), WG, R("SL", 24 + 8 * t, 32 + 8 * t))
+        for (a, b, q) in TUNE["gath"]:
+            d1 = R("D1", 16 * a, 16 * b) if a < B else R("D1F", 16 * (a - B), 16 * (b - B))
+            scan(R("EE", 16 * a, 16 * b), R("XG", 16 * a, 16 * b), d1, A.add, A.min)
+        for k, (a, b) in enumerate(TUNE["wrap"]):
+            p = R("P%d" % (k % 2), 0, b - a)
+            mm(p, R("IH"), R("CH", 128 * t + a, 128 * t + b), True, False)
+            for i in range(16):
+                mm(p, Z(i), R("EE", 16 * a + i, 16 * b, 16), False, i == 15)
+            tt(R("LF", a, b), p, R("CB", 128 * t + a, 128 * t + b), A.max)
+            copy("V", R("LL", a, b), R("LF", a, b), 1.0, DUMP - 1.0)
         x0 = R("XG", 1, S, 16)
-        ts(R("BS"), x0, 0.0, A.is_equal, 512.0, A.mult)
-        mm(R("P6", 0, 128), x0, R("ID"))
-        copy("VS", R("BT"), R("P6", 0, 128))
-        for c in range(4):
-            x15 = R("XG", 16 + 512 * c, 513 + 512 * c, 16)
-            if not last:
-                copy("VS", R("X15", 32 * c, 32 * c + 32), x15)
-            fill(x15, BIG)
-            d1 = R("D1", 512 * c, 512 * c + 512) if c < 3 else R("D1F")
-            scan(R("EE", 512 * c, 512 * c + 512), R("XG", 512 * c, 512 * c + 512), d1, A.add, A.min)
-            mm(R("P%d" % c), R("BLKW"), R("EE", 512 * c, 512 * c + 512), False, True)
-            relu("VS", R("XK", 1 + 512 * c, 513 + 512 * c), R("P%d" % c))
-        for c in FUSED:
-            mm(R("P4"), R("BT"), R("E", 512 * c, 512 * c + 512))
-            copy("VS", R("BE", 512 * c, 512 * c + 512), R("P4"))
-        for c in PLAIN:
-            mm(R("P%d" % c), R("BT"), R("E", 512 * c, 512 * c + 512))
-
-        def fused(c):
-            m, b, p = R("CM", 512 * c, 512 * c + 512), R("BE", 512 * c, 512 * c + 512), R(PL, 32 * c, 32 * c + 32)
-            op("V", lambda e, z: e.tensor_tensor(ap(m), ap(R("XK")).indirect(ap(p)), ap(b), A.is_ge), [R("XK"), p, b], [m], 50 + 1.5 * 512)
-
-        for c in PLAIN:
-            gath("S", R("AB", 512 * c, 512 * c + 512), R("XK"), R(PL, 32 * c, 32 * c + 32))
-        for c in FUSED:
-            fused(c)
-        for c in PLAIN:
-            tt(R("CM", 512 * c, 512 * c + 512), R("AB", 512 * c, 512 * c + 512), R("P%d" % c), A.is_ge)
+        ts(R("TH", 0, 128), x0, -1.0 / 32, A.add, 2.0 ** -16, A.max)
+        cw = S // TUNE["cov"]
+        k = 128
+        while k < cw:
+            copy("VS", R("TH", k, 2 * k), R("TH", 0, k))
+            k *= 2
+        act(R("BS"), x0, F.Relu, -65536.0, 1.0)
+        ends = sorted(set([a for (a, b) in TUNE["wrap"]] + [cut, 128]))
+        pieces = list(zip(ends[:-1], ends[1:]))
+        for (a, b) in pieces:
+            if b <= cut:
+                scat("S", WS, R("LL", a, b), R("ZR", 0, 16 * (b - a)))
+            else:
+                for a2 in range(a, b, 32):
+                    b2 = min(b, a2 + 32)
+                    scat("V", R("FW"), R("LL", a2, b2), R("MK%d" % t, 0, 16 * (b2 - a2)))
         if not last:
             tag[0] = "h%d" % t
             for i in range(16):
-                mm(R("P5", 0, 128), R("ID"), R("XG", 1 + i, S, 16) if i < 15 else R("X15"), i == 0, i == 15)
-            tt(R("DD"), R("NF"), R("P5", 0, 128), A.subtract)
-            relu("VS", R("RD"), R("DD"))
-            mm(R("P5", 0, 128), R("BLKW"), R("RD"))
-            ts(R("UU"), R("P5", 0, 128), 0.1, A.is_gt)
-            scan(R("CN"), R("ONES", 0, 128), R("UU"), A.mult, A.add)
-            ts(R("WW"), R("UU"), -1000.0, A.mult, 999.0, A.add)
-            tt(R("OF0"), R("CN"), R("WW"), A.add)
-            tt(R("OFF"), R("OF0"), R("D32"), A.min)
-            wrap("P5", "OFF", 0, 8)
-            sl = "SL%d" % t
-            ts(R("DQ"), R("DD"), 0.0, A.max, 8388608.0, A.add)
-            fill(R(sl), 0.0)
-            copy("V", R("OL"), R("P5", 0, 8), 32.0, 0.0)
+                mm(R("P5", 0, 128), R("I4"), R("XG", 1 + i, S, 16) if i < 15 else R("X15"), i == 0, False)
+            if t > 0:
+                mm(R("P5", B, 128), R("I4F"), R("D1F", 0, 512, 16), False, False)
+            mm(R("P5", 0, B), R("I4"), R("D1", 0, 1536, 16), False, True)
+            act(R("RF"), R("P5", 0, 128), F.Relu, -0.25)
+            mm(R("P5", 0, 128), R("ONE", rows=1), R("RP", rows=1), True, False)
+            mm(R("P5", 0, 128), R("BKF"), R("RF"), False, True)
+            act(R("ZZ"), R("P5", 0, 128), F.Relu)
+            act(R("UU"), R("ZZ"), F.Relu, -1.0, 1.0)
+            scan(R("CN"), R("UU"), R("UU"), A.add, A.max)
+            for k, src in enumerate(("ZZ", "CN")):
+                for r in range(16):
+                    mm(R("P5", 0, 8), Z(r), R(src, r, 128, 16), k == 0 and r == 0, k == 1 and r == 15)
+            copy("V", R("OL"), R("P5", 0, 8), 1.0 / (16 * KE), -1.0)
+            sl = "SB%d" % t
 
             def put(e, z, sl=sl):
-                return e.tensor_scalar(ap(R(sl)).indirect(ap(R("OL"))), ap(R("DQ")), 1.0, -8388608.0, A.mult, A.add)
-            op("V", put, [R("OL"), R("DQ")], [R(sl)], 50 + TUNE["sc"] * 128)
+                return e.tensor_scalar(ap(R(sl)).indirect(ap(R("OL"))), ap(R("RF")), -(1.0 + 2.0 ** -14), -MAGIC, A.mult, A.add)
+            op("V", put, [R("OL"), R("RF")], [R(sl)], 40 + TUNE["sc"] * 128)
             rl = relay_of(rank)
             m, k = emask(core, rl)
             rid, pid = topo.addr(rl, core)
@@ -480,75 +429,52 @@ def rank_program(g, core, T, topo):
                 return e.remote_dma(T["RB%d" % t][:, :], ap(R(sl, 0, U)), T.sem["rin%d" % t], T.sem["out%d" % t], pid, rid, m)
             add("G", send, [R(sl, 0, U)], [R("ARR%d" % t)], 0.6, kind="m", lat=TUNE["rlat"], extra=("arr%d" % t, ka, "out%d" % t, k))
             tag[0] = ""
-            needs(t + 1)
-            lists(t + 1)
-        mm(R("P6", 0, 128), R("ONES", 0, 128), R("CCON"), True, False)
-        mm(R("P6", 0, 128), R("BS"), R("BLKN"), False, False)
-        mm(R("P6", 0, 128), R("NZ", 128 * t, 128 * t + 128), R("BLKN"), False, False)
-        for i in range(16):
-            mm(R("P6", 15 - i, 128, 16), R("CM", i, S, 16), R("SELW"), False, i == 15)
-        tt(R("NFM"), R("P6", 0, 128), R("THR"), A.is_lt)
-        tt(R("KY"), R("P6", 0, 128), R("PT%d" % t), A.min)
-        scan(R("SC8"), R("NFM"), R("KY"), A.mult, A.max)
-        if last:
-            copy("V", R("C8"), R("SC8", 15, 128, 16), -1.0, 2050.0)
-        else:
-            copy("V", R("CI"), R("SC8", 15, 128, 16))
-            ts(R("PI"), R("CI"), 4095, A.bitwise_and)
-            copy("V", R("C8"), R("PI"), -1.0, 2050.0)
-        for q in range(8):
-            ts(R("DG", 128 * q, 128 * q + 128), R("IH"), R("C8", q, q + 1), A.mult)
-        for b in range(2):
-            mm(R("P%d" % (4 + b)), R("TRI"), R("DG", 512 * b, 512 * b + 512))
-        for q in range(8):
-            ts(R("EQ", 128 * q, 128 * q + 128), R("P%d" % (4 + q // 4), 128 * (q % 4), 128 * (q % 4) + 128), R("C8", q, q + 1), A.is_equal)
-        for q in range(8):
-            o = R("P6", 16 * q, 16 * q + 16)
-            mm(o, R("DG", 128 * q, 128 * q + 128), R("ONE16"), True, False)
-            mm(o, R("EQ", 128 * q, 128 * q + 128), R("F4K"), False, True)
-        tt(R("FM"), R("P6", 0, 128), R("DM"), A.min)
-        mm(R("P3", 0, 8), R("FM"), R("B16"))
-        copy("V", R("LU"), R("P3", 0, 8))
-        if not last:
-            gath("V", R("NV"), R("XK"), R("LU"))
-            tag[0] = "j%d" % t
-            mm(R("P2", 0, 128), R("I18"), R("XK", 1, S, 16))
-            gath("V", R("OJ"), R("JS"), R("S0L", 8 * t, 8 * t + 8))
-            tt(R("OJ"), R("OJ"), R("P2", 0, 128), A.min)
-            ts(R("SI"), R("CI"), 12, A.arith_shift_right)
-            copy("V", R("ST8"), R("SI"))
-            for q in range(8):
-                ts(R("FS", 16 * q, 16 * q + 16), R("M16", 0, 16), R("ST8", q, q + 1), A.mult)
-            ts(R("LOS"), R("P6", 0, 128), 2049.0, A.is_ge)
-            tt(R("LD"), R("LOS"), R("DM"), A.mult)
-            tt(R("FT"), R("FS"), R("LD"), A.max)
-            mm(R("P2", 0, 8), R("FT"), R("B16"))
-            copy("V", R("LS"), R("P2", 0, 8))
-            gath("V", R("NJ"), R("JS"), R("LS"))
-            tt(R("NJ"), R("NJ"), R("OJ"), A.max)
-            scat(R("JS"), R("S0L", 8 * t, 8 * t + 8), R("NJ"))
-            tag[0] = ""
-            scat(R("XK"), R("LU"), R("ZB"))
-            xd = R("XK", 1, S, 16)
-            tt(xd, xd, R("NV"), A.add)
-        else:
-            tag[0] = "y"
-            for c in range(4):
-                gath("VS", R("XT", 512 * c, 512 * c + 512), R("XK"), R("RL2", 32 * c, 32 * c + 32))
-            for c in range(4):
-                mm(R("P%d" % c), R("ONES", 0, 128), R("CY"), True, False)
-                mm(R("P%d" % c), R("I18N"), R("XT", 512 * c, 512 * c + 512), False, True)
-                tt(R("YY", 1 + 512 * c, 513 + 512 * c), R("JS", 512 * c, 512 * c + 512), R("P%d" % c), A.max)
-            tag[0] = ""
-            gath("V", R("NJ"), R("YY"), R("LU"))
-            scat(R("YY"), R("LU"), R("ZF"))
-            gath("V", R("OJ"), R("YY"), R("S0Y"))
-            tt(R("NJ"), R("NJ"), R("OJ"), A.min)
-            scat(R("YY"), R("S0Y"), R("NJ"))
-            for c in range(2):
-                dma("YS"[c], T.y[:, h * c:h * c + h], T.YY[0:128:16, 1 + h * c:1 + h * c + h], [R("YY", 1 + h * c, 1 + h * c + h)], [], 2.0)
+        mm(R("P4", 0, 256), R("ONE", rows=1), R("CC", rows=1), True, False)
+        mm(R("P4", 0, 256), R("BS"), R("BK2"), False, False)
+        mm(R("P4", 0, 256), R("NZ", 128 * t, 128 * t + 128), R("BK2"), False, False)
+        for k in range(2):
+            mm(R("P%d" % (2 + k)), R("I4"), R("NI"), True, False)
+        mm(R("P6", 0, 256), R("CH", 128 * t, 128 * t + 128), R("S0R"), True, False)
 
-    at, on = order_of(ops)
+        def cover(c, t=t, cw=cw):
+            m, b, p = R("CM", cw * c, cw * c + cw), R("TH", 0, cw), R("ML", 128 * t + cw // 16 * c, 128 * t + cw // 16 * (c + 1))
+            op("V", lambda e, z: e.tensor_tensor(ap(m), ap(WG).indirect(ap(p)), ap(b), A.is_ge), [WG, p, b], [m], 40 + TUNE["g"] * cw)
+            f, w = R("FL", cw * c, cw * c + cw), R("FW", 0, S)
+            op("S", lambda e, z: e.activation(ap(f), ap(w).indirect(ap(p)), F.Relu, bias=-float(t)), [w, p], [f], 40 + TUNE["g"] * cw)
+            for i in range(cw // 128 * c, cw // 128 * (c + 1)):
+                o = R("P4", 15 - i, 256, 16)
+                mm(o, R("CM", 128 * i, 128 * i + 128), R("SW", 8, 24) if i < 15 else R("SW", 32, 48), False, False)
+                mm(o, R("FL", 128 * i, 128 * i + 128), R("SW", 0, 16) if i < 15 else R("SW", 16, 32), False, i == 15)
+        for c in range(TUNE["cov"]):
+            cover(c)
+        scat("S", WS, R("LL", cut, 128), R("ZR", 0, 16 * (128 - cut)))
+        tt(R("KY"), R("P4", 0, 128), R("PT", 128 * t, 128 * t + 128), A.min)
+        scan(R("SC"), R("P4", 128, 256), R("KY"), A.min, A.max)
+        for q in range(8):
+            ts(R("DG", 128 * q, 128 * q + 128), R("IH"), R("SC", 16 * q + 15, 16 * q + 16), A.mult)
+        for k in range(2):
+            mm(R("P%d" % (2 + k)), R("TRI"), R("DG", 512 * k, 512 * k + 512), False, True)
+        for q in range(8):
+            mm(R("P6", 32 * q, 32 * q + 32), R("DG", 128 * q, 128 * q + 128), R("O32"), False, False)
+        for q in range(8):
+            ts(R("EQ", 128 * q, 128 * q + 128), R("P%d" % (2 + q // 4), 128 * (q % 4), 128 * (q % 4) + 128), R("SC", 16 * q + 15, 16 * q + 16), A.is_equal)
+            mm(R("P6", 32 * q, 32 * q + 32), R("EQ", 128 * q, 128 * q + 128), R("K32"), False, q == 7)
+        tt(R("FM"), R("P6", 0, 256), R("DM"), A.min)
+        for k in range(2):
+            mm(R("P4", 8 * k, 8 * k + 8), R("FM", k, 256, 2), R("B16"))
+        copy("V", R("LU"), R("P4", 0, 16), 1.0, -1.0)
+        gath("V", R("VV", 128, 256), R("W", 0, WN), R("LU", 0, 8))
+        scat("V", R("W", 0, WN), R("LU"), R("VV"))
+
+    dma("Y", T.YC[:, :], T.W[0:128:16, 0:S], [R("W", 0, S)], [R("YC")], 2.0)
+    copy("V", R("YI"), R("YC"), 65536.0)
+    ts(R("YJ"), R("YI"), 2047, A.bitwise_and)
+    copy("V", R("YO"), R("YJ"), -1.0, 2047.0)
+    dma("Y", T.y[:, :], T.YO[:, :], [R("YO")], [], 2.0)
+
+    if "at" not in ORDER:
+        ORDER["end"], ORDER["at"], ORDER["on"] = arrange(ops)
+    at, on = ORDER["at"], ORDER["on"]
     m = len(ops)
     cnt = {k: 0 for k in CS}
     known = {k: {} for k in Q}
@@ -573,11 +499,8 @@ def rank_program(g, core, T, topo):
             ins.then_inc(T.sem[CS[q]], 1)
             done[i] = (CS[q], cnt[q])
         elif o["kind"] == "d":
-            if o["x"] is None:
-                done[i] = ("d%d" % nd, 16)
-                nd += 1
-            else:
-                done[i] = o["x"]
+            done[i] = ("d%d" % nd, 16)
+            nd += 1
             ins.then_inc(T.sem[done[i][0]], 16)
         else:
             done[i] = (o["x"][0], o["x"][1])

@@ -1,10 +1,9 @@
-import numpy as np
 from concourse.mybir import AluOpType as A, ActivationFunctionType as F
 
 BF, FP, F16, I32, U16 = "bfloat16", "float32", "float16", "int32", "uint16"
 S, L, B, U, RO = 2048, 128, 96, 32, 3
 BIG = 4096.0
-DUMP = 2050
+DUMP = 2064
 WW, WN = 4112, 2560
 KE = 8192.0
 WC = 4096.0
@@ -15,23 +14,24 @@ SCRATCH = {}
 for _n, _w, _d in [
         ("SK", S, BF), ("SKF", S, FP), ("OC", 128, I32), ("CD", 384, I32), ("ND", 288, BF), ("CV", S, I32),
         ("W", WW, FP), ("FW", WW, BF), ("XG", S + 16, BF), ("EE", S, BF), ("D1", 1536, BF), ("D1F", 512, FP), ("CM", S, BF), ("FL", S, BF),
-        ("ZR", 1024, FP), ("MK0", 512, BF), ("MK1", 512, BF), ("MK2", 512, BF), ("TH", 512, BF), ("RI", 512, I32), ("RH", 512, F16),
-        ("OH", 128, F16), ("OT", 128, F16), ("OU", 128, U16), ("CU", 384, U16), ("CH", 384, F16), ("CT", 384, F16), ("CB", 384, FP),
-        ("SL", 48, U16), ("MH", 384, F16), ("MT", 384, F16), ("ML", 384, U16), ("PT", 384, FP), ("NZ", 384, BF), ("BS", 128, BF),
-        ("LF", 128, FP), ("LL", 128, U16), ("X15", 128, BF), ("KY", 128, FP), ("SC", 128, FP), ("DG", 1024, F16), ("EQ", 1024, F16),
-        ("FM", 256, F16), ("LU", 16, U16), ("VV", 256, FP), ("RF", 128, FP), ("ZZ", 128, BF), ("UU", 128, BF), ("CN", 128, BF),
+        ("ZR", 512, FP), ("MK0", 512, BF), ("MK1", 512, BF), ("MK2", 512, BF), ("TH", 512, BF), ("RH", 1024, F16),
+        ("OH", 128, F16), ("OT", 128, F16), ("OU", 128, U16), ("CU", 384, U16), ("CH", 384, F16), ("CT", 384, F16),
+        ("SL", 48, U16), ("MH", 128, F16), ("MT", 128, F16), ("ML", 256, U16), ("PT", 256, FP), ("NZ", 384, BF), ("BS", 128, BF),
+        ("SO0", U, FP), ("SO1", U, FP),
+        ("LF", 128, FP), ("LL", 128, U16), ("X15", 128, BF), ("KY", 128, FP), ("SC", 128, FP), ("DG", 1024, F16), ("EQ", 1024, BF),
+        ("FM", 256, F16), ("LU", 16, U16), ("VV", 256, FP), ("RF", 128, FP), ("ZC", 256, BF), ("ZT", 256, BF), ("UU", 128, BF),
         ("OL", 8, U16), ("SB0", 512, FP), ("SB1", 512, FP), ("ARR0", U, FP), ("ARR1", U, FP), ("RB0", U, FP), ("RB1", U, FP),
         ("YC", 128, FP), ("YI", 128, I32), ("YJ", 128, I32), ("YO", 128, FP),
-        ("WX", 256, FP), ("W1", 128, I32), ("T1", 128, I32), ("NI", 512, BF), ("BK2", 256, BF), ("S0R", 256, F16), ("DM", 256, FP),
-        ("I4F", 128, FP), ("BKF", 128, FP), ("CC", 256, BF), ("W3", 256, I32), ("W4", 128, I32)]:
+        ("WX", 256, FP), ("NI", 512, BF), ("BK2", 256, BF), ("S0R", 256, BF), ("DM", 256, FP),
+        ("I1F", 128, FP), ("BKF", 128, FP), ("CC", 256, BF), ("ONE", 256, BF), ("E3", 256, BF)]:
     SCRATCH[_n] = ("sbuf", [128, _w], _d)
 PARTS = {}
 for _b, _d, _l in [
         ("GI", I32, [("IP", 8), ("IA", 8), ("IB", 8)]),
-        ("GF", FP, [("PR", 8), ("PX", 8), ("PY", 8), ("PU", 8), ("PM", 8), ("PN", 8), ("PD", 8), ("PE", 8), ("PZ", 8)]),
-        ("GB", BF, [("I4", 128), ("Z", 144), ("BK", 128), ("SW", 48), ("ONE", 128), ("RP", 128)]),
-        ("GH", F16, [("IH", 128), ("PV", 128), ("TRI", 128), ("Q00", 128), ("Q01", 128), ("Q10", 128), ("Q11", 128), ("B16", 16),
-                     ("O32", 32), ("K32", 32), ("C14", 128)])]:
+        ("GF", FP, [("PX", 8), ("PY", 8), ("PM", 8), ("PN", 8), ("PD", 8), ("PE", 8)]),
+        ("GB", BF, [("I1", 128), ("Z", 144), ("BK", 128), ("SW", 48), ("RP", 128), ("PV", 128), ("TRI", 128), ("Q00", 128), ("Q01", 128),
+                    ("Q10", 128), ("Q11", 128), ("B16", 16), ("O32", 32), ("K32", 32), ("C16", 128), ("E1", 128), ("E2", 128), ("E4", 144),
+                    ("CK", 64)])]:
     _o = 0
     for _n, _w in _l:
         PARTS[_n] = (_b, _o, 1 if _b in ("GI", "GF") else {"B16": 8}.get(_n, _w))
@@ -39,57 +39,8 @@ for _b, _d, _l in [
     SCRATCH[_b] = ("sbuf", [128, _o], _d)
 for _k in range(8):
     SCRATCH["P%d" % _k] = ("psum", [128, 512], FP)
-SEMAPHORES = ["cV", "cS", "cP", "cG"] + ["d%d" % k for k in range(20)] + ["arr0", "arr1", "rin0", "rin1", "out0", "out1"]
-
-TUNE = {"f": 1.1, "g": 1.3, "sc": 2.5, "pe": 0.7, "rlat": 6.0, "hop": 0.12, "own": 0.08, "pv": 0.3,
-        "gath": [(0, 32, "V"), (32, 64, "S"), (64, 96, "S"), (96, 128, "S")],
-        "wrap": [(0, 64), (64, 128)], "cut": 64, "cov": 4, "b": {}}
-ORDER = {}
-
-
-def arrange(ops):
-    m, hop = len(ops), TUNE["hop"]
-    succ = [[] for _ in range(m)]
-    for i, o in enumerate(ops):
-        for j in o["edges"]:
-            succ[j].append(i)
-    up = [0.0] * m
-    for i in range(m - 1, -1, -1):
-        o = ops[i]
-        up[i] = o["cost"] + max([up[j] + (0.0 if ops[j]["edges"][i] == 0 and ops[j]["q"] == o["q"] else hop + o["lat"]) for j in succ[i]] + [o["lat"]])
-    key = [up[i] + TUNE["b"].get(ops[i]["tag"], 0.0) for i in range(m)]
-    left = [len(o["edges"]) for o in ops]
-    ready = [i for i in range(m) if not left[i]]
-    slots = {k: [] for k in "VSPGY"}
-    at, end, on = [0.0] * m, [0.0] * m, [""] * m
-    while ready:
-        i = max(ready, key=lambda i: (key[i], -i))
-        ready.remove(i)
-        for j in succ[i]:
-            left[j] -= 1
-            if not left[j]:
-                ready.append(j)
-        o = ops[i]
-        best = None
-        for q in o["q"]:
-            s = 0.0
-            for j, e in o["edges"].items():
-                if on[j] == q and e == 0:
-                    s = max(s, at[j] + ops[j]["cost"])
-                else:
-                    s = max(s, end[j] + (hop if on[j] != q else TUNE["own"]))
-            for (a, b) in slots[q]:
-                if s + o["cost"] <= a:
-                    break
-                s = max(s, b)
-            pen = s + o["cost"] + (TUNE["pv"] if q == "V" and len(o["q"]) > 1 else 0.0)
-            if best is None or pen < best[0] - 1e-9:
-                best = (pen, s, q)
-        _, s, q = best
-        on[i], at[i], end[i] = q, s, s + o["cost"] + o["lat"]
-        slots[q].append((s, s + o["cost"]))
-        slots[q].sort()
-    return max(end), at, on
+SEMAPHORES = ["cV", "cS", "cP", "cG"] + ["d%d" % k for k in range(12)] + ["arr0", "arr1", "rin0", "rin1", "out0", "out1"]
+TUNE = {"cov": [0, 4, 8, 12, 16], "cut": 112}
 
 
 def rank_program(g, core, T, topo):
@@ -123,7 +74,8 @@ def rank_program(g, core, T, topo):
 
     Q = {"V": g.vector, "S": g.scalar, "P": g.tensor, "G": g, "Y": g.sync}
     CS = {"V": "cV", "S": "cS", "P": "cP", "G": "cG"}
-    ops, acc, tag = [], {}, [""]
+    acc, done, on = {}, [], []
+    cnt, known, total, nd = {k: 0 for k in CS}, {k: {} for k in Q}, {}, [0]
 
     def R(name, lo=0, hi=None, st=1, rows=128):
         if name in PARTS:
@@ -140,107 +92,115 @@ def rank_program(g, core, T, topo):
     def width(r):
         return (r[2] - r[1] + r[3] - 1) // r[3]
 
-    def two(*rs):
-        return all(SCRATCH[r[0]][2] in (BF, F16, U16) for r in rs)
+    def apart(a, b):
+        return a[1] >= b[2] or b[1] >= a[2] or (a[3] == b[3] and a[3] > 1 and (a[1] - b[1]) % a[3] != 0)
 
-    def overlap(a, b):
-        if psum(a[0]):
-            return True
-        if a[1] >= b[2] or b[1] >= a[2]:
-            return False
-        return not (a[3] == b[3] and a[3] > 1 and (a[1] - b[1]) % a[3])
-
-    def add(q, fn, reads, writes, cost, chain=False, kind="c", lat=0.0, extra=None):
-        me, edges = len(ops), {}
+    def issue(q, fn, reads, writes, chain=False, sem=None):
+        me, need = len(done), {}
         mine = [(r, "r") for r in reads] + [(r, "w") for r in writes]
         for rr, k in mine:
             for (o, ok, j) in acc.get(rr[0], []):
-                if j == me or not overlap(rr, o):
+                same = on[j] == q
+                if psum(rr[0]):
+                    if same and ((k == "r" and ok == "r") or (q == "P" and (chain or apart(rr, o)))):
+                        continue
+                elif apart(rr, o) or (k == "r" and ok == "r"):
                     continue
-                if k == "r" and ok == "r":
-                    if psum(rr[0]):
-                        edges[j] = max(edges.get(j, 0), 0)
-                    continue
-                e = 0 if k == "w" and chain else 1
-                if psum(rr[0]) and q == "P" and ops[j]["q"] == "P" and (rr[1] >= o[2] or o[1] >= rr[2] or (rr[3] == o[3] > 1 and (rr[1] - o[1]) % rr[3])):
-                    e = 0
-                edges[j] = max(edges.get(j, 0), e)
+                need[done[j][0]] = max(need.get(done[j][0], 0), done[j][1])
         for rr, k in mine:
             keep = []
             for e in acc.get(rr[0], []):
                 o = e[0]
-                cov = rr[1] <= o[1] and o[2] <= rr[2] and (rr[3] == 1 or (rr[3] == o[3] and (rr[1] - o[1]) % rr[3] == 0))
-                if k == "w" and e[2] != me and (cov or (psum(rr[0]) and ops[e[2]]["q"] != "P")):
+                cov = rr[1] <= o[1] and o[2] <= rr[2] and rr[4] >= o[4] and (rr[3] == 1 or (rr[3] == o[3] and (rr[1] - o[1]) % rr[3] == 0))
+                if k == "w" and e[2] != me and (cov or (psum(rr[0]) and on[e[2]] != "P")):
                     continue
                 keep.append(e)
             keep.append((rr, k, me))
             acc[rr[0]] = keep
-        ops.append({"tag": tag[0], "q": q, "fn": fn, "cost": cost, "edges": edges, "kind": kind, "lat": lat, "x": extra})
+        for s in sorted(need):
+            if known[q].get(s, 0) < need[s]:
+                Q[q].wait_ge(T.sem[s], need[s])
+                known[q][s] = need[s]
+        ins = fn(Q[q])
+        if sem is None:
+            cnt[q] += 1
+            sem = (CS[q], cnt[q])
+            ins.then_inc(T.sem[CS[q]], 1)
+            on.append(q)
+        elif sem == "dma":
+            sem = ("d%d" % nd[0], 16)
+            nd[0] += 1
+            ins.then_inc(T.sem[sem[0]], 16)
+            on.append("")
+        else:
+            on.append("")
+        done.append(sem)
+        total[sem[0]] = max(total.get(sem[0], 0), sem[1])
 
-    def op(q, fn, reads, writes, cyc, chain=False):
-        add(q, fn, reads, writes, 0.03 + max(cyc, 64) * 0.00083 * TUNE["f"], chain)
-
-    def dma(q, out, in_, reads, writes, lat):
-        add(q, lambda e, z: e.dma_start(out, in_), reads, writes, 0.1, kind="d", lat=lat)
+    def dma(q, out, in_, reads, writes):
+        issue(q, lambda e: e.dma_start(out, in_), reads, writes, sem="dma")
 
     def copy(q, o, i, scale=1.0, bias=0.0):
-        def f(e, z):
-            if z == "V":
-                if scale == 1.0 and bias == 0.0:
-                    return e.tensor_copy(ap(o), ap(i))
-                return e.tensor_scalar(ap(o), ap(i), float(scale), float(bias), A.mult, A.add)
-            return e.activation(ap(o), ap(i), F.Copy if bias == 0.0 else F.Identity, bias=float(bias), scale=float(scale))
-        op(q, f, [i], [o], width(i) * (0.5 if q == "V" and two(o, i) else 1))
+        if q == "S":
+            act(o, i, F.Copy if bias == 0.0 else F.Identity, scale, bias)
+        elif q == "G":
+            issue(q, lambda e: e.affine_select(ap(o), ap(i), [[0, width(o)]], A.is_ge, 0.0, 0, 0), [i], [o])
+        elif scale == 1.0 and bias == 0.0:
+            issue(q, lambda e: e.tensor_copy(ap(o), ap(i)), [i], [o])
+        else:
+            ts(o, i, float(scale), A.mult, float(bias), A.add)
 
     def act(o, i, func, scale=1.0, bias=0.0):
-        op("S", lambda e, z: e.activation(ap(o), ap(i), func, bias=float(bias), scale=float(scale)), [i], [o], width(i))
+        if isinstance(scale, tuple):
+            issue("S", lambda e: e.activation(ap(o), ap(i), func, scale=ap(scale)), [i, scale], [o])
+        else:
+            issue("S", lambda e: e.activation(ap(o), ap(i), func, bias=float(bias), scale=float(scale)), [i], [o])
 
     def ts(o, i, s1, op0, s2=None, op1=None):
-        rd, a1, a2 = [i], s1, s2
-        if isinstance(s1, tuple):
-            rd.append(s1)
-            a1 = ap(s1)
-        if isinstance(s2, tuple):
-            rd.append(s2)
-            a2 = ap(s2)
-        c = width(i) * (0.5 if two(o, i) else 1)
+        rd = [i] + [s for s in (s1, s2) if isinstance(s, tuple)]
+        a1, a2 = [ap(s) if isinstance(s, tuple) else s for s in (s1, s2)]
         if op1 is None:
-            op("V", lambda e, z: e.tensor_scalar(ap(o), ap(i), a1, None, op0), rd, [o], c)
+            issue("V", lambda e: e.tensor_scalar(ap(o), ap(i), a1, None, op0), rd, [o])
         else:
-            op("V", lambda e, z: e.tensor_scalar(ap(o), ap(i), a1, a2, op0, op1), rd, [o], c)
+            issue("V", lambda e: e.tensor_scalar(ap(o), ap(i), a1, a2, op0, op1), rd, [o])
 
     def tt(o, a, b, o_):
-        op("V", lambda e, z: e.tensor_tensor(ap(o), ap(a), ap(b), o_), [a, b], [o], width(o) * (1 if psum(a[0]) or psum(b[0]) else 2))
+        issue("V", lambda e: e.tensor_tensor(ap(o), ap(a), ap(b), o_), [a, b], [o])
 
-    def fill(o, v, q="V"):
-        if q == "G":
-            op(q, lambda e, z: e.iota(ap(o), [[0, width(o)]], int(v), 0, allow_small_or_imprecise_dtypes=True), [], [o], 150 + 2 * width(o))
+    def fill(q, o, v):
+        if q == "V":
+            issue(q, lambda e: e.memset(ap(o), v), [], [o])
+        elif q == "S":
+            copy(q, o, R("ZR", 0, width(o), rows=o[4]), 1.0, v)
         else:
-            op(q, lambda e, z: e.memset(ap(o), v), [], [o], width(o) * (0.5 if two(o) else 1))
+            iota(o, [[0, width(o)]], int(v), 0)
 
     def scan(o, a, b, op0, op1):
-        op("V", lambda e, z: e.tensor_tensor_scan(ap(o), ap(a), ap(b), 0.0, op0, op1), [a, b], [o], width(o) * (0.5 if two(o, a, b) else 1))
+        issue("V", lambda e: e.tensor_tensor_scan(ap(o), ap(a), ap(b), 0.0, op0, op1), [a, b], [o])
 
     def mm(o, l, r, start=True, stop=True):
-        c = max(min(64, width(l)), width(r)) * (1 if two(l) else 4)
-        add("P", lambda e, z: e.matmul(ap(o), ap(l), ap(r), start, stop), [l, r], [o], c * TUNE["pe"] * 0.001 * TUNE["f"], not start)
+        issue("P", lambda e: e.matmul(ap(o), ap(l), ap(r), start, stop), [l, r], [o], chain=not start)
 
     def gath(q, o, win, lst):
-        op(q, lambda e, z: e.tensor_copy(ap(o), ap(win).indirect(ap(lst))) if z == "V" else
-           e.activation(ap(o), ap(win).indirect(ap(lst)), F.Copy), [win, lst], [o], 40 + TUNE["g"] * width(o))
+        issue(q, lambda e: e.tensor_copy(ap(o), ap(win).indirect(ap(lst))) if q == "V" else
+              e.activation(ap(o), ap(win).indirect(ap(lst)), F.Copy), [win, lst], [o])
 
     def scat(q, win, lst, i):
-        op(q, lambda e, z: e.tensor_copy(ap(win).indirect(ap(lst)), ap(i)) if z == "V" else
-           e.activation(ap(win).indirect(ap(lst)), ap(i), F.Silu), [lst, i], [win], 40 + TUNE["sc"] * width(i))
+        issue(q, lambda e: e.tensor_copy(ap(win).indirect(ap(lst)), ap(i)) if q == "V" else
+              e.activation(ap(win).indirect(ap(lst)), ap(i), F.Silu), [lst, i], [win])
 
     def iota(o, pat, base, cm):
         if SCRATCH[o[0]][2] == I32:
-            op("G", lambda e, z: e.iota(ap(o), pat, base, cm), [], [o], 150 + 2 * width(o))
+            issue("G", lambda e: e.iota(ap(o), pat, base, cm), [], [o])
         else:
-            op("G", lambda e, z: e.iota(ap(o), pat, base, cm, allow_small_or_imprecise_dtypes=True), [], [o], 150 + 2 * width(o))
+            issue("G", lambda e: e.iota(ap(o), pat, base, cm, allow_small_or_imprecise_dtypes=True), [], [o])
+
+    def ones_where(o, pat, base, cm):
+        i = R("ONE", 0, width(o), rows=o[4])
+        issue("G", lambda e: e.affine_select(ap(o), ap(i), pat, A.is_equal, 0.0, base, cm), [i], [o])
 
     def vtr(o, i):
-        op("V", lambda e, z: e.transpose(ap(o), ap(i)), [i], [o], width(o) * 0.5)
+        issue("V", lambda e: e.transpose(ap(o), ap(i)), [i], [o])
 
     def turn(bank, src, c0):
         for b in range(4):
@@ -251,261 +211,316 @@ def rank_program(g, core, T, topo):
     def Z(i):
         return R("Z", 15 - i, 143 - i)
 
-    dma("Y", T.OC[:, :], T.occ[:, :], [], [R("OC")], 2.0)
+    WG, WS, D0 = R("W", 0, S + 1), R("W"), R("WX", 64, 192)
+
+    dma("Y", T.OC[:, :], T.occ[:, :], [], [R("OC")])
     for c in range(4):
-        dma("SY"[c % 2], T.SK[:, 512 * c:512 * c + 512], T.skill[:, 512 * c:512 * c + 512], [], [R("SK", 512 * c, 512 * c + 512)], 2.4 + 0.4 * c)
-    dma("S", T.CD[:, :], T.cards[:, :], [], [R("CD")], 4.2)
-    dma("Y", T.ND[:, :], T.need[:, :], [], [R("ND")], 4.5)
-    dma("Y", T.CV[:, :], T.cover[:, :], [], [R("CV")], 7.5)
+        dma("SY"[c % 2], T.SK[:, 512 * c:512 * c + 512], T.skill[:, 512 * c:512 * c + 512], [], [R("SK", 512 * c, 512 * c + 512)])
+        if c == 1:
+            dma("Y", T.CD[:, 0:128], T.cards[:, 0:128], [], [R("CD", 0, 128)])
+    dma("Y", T.ND[:, :], T.need[:, :], [], [R("ND")])
+    dma("Y", T.CD[:, 128:384], T.cards[:, 128:384], [], [R("CD", 128, 384)])
+    dma("Y", T.CV[:, :], T.cover[:, :], [], [R("CV")])
 
     iota(R("IP"), [[0, 1]], 0, 1)
     iota(R("WX"), [[1, 256]], -64, -1)
-    iota(R("RI"), [[-1, 512]], 511, 0)
-    iota(R("W1"), [[-16, 8], [0, 16]], 0, 1)
-    iota(R("W4"), [[-16, 8], [1, 16]], -15, 1)
-    iota(R("W3"), [[0, 8], [-1, 16], [0, 2]], 128, 1)
-    iota(R("RP"), [[1, 128]], 129, 0)
-    D0 = R("WX", 64, 192)
+    fill("V", R("ONE"), 1.0)
+    fill("V", R("ZR"), 0.0)
+    fill("V", R("C16", rows=32), 2.0 ** -16)
+    act(R("D1F"), R("ZR"), F.Silu)
+    ones_where(R("E1", rows=8), [[-1, 8], [0, 16]], 0, 1)
+    ones_where(R("E4", rows=8), [[1, 144]], -15, -16)
+    fill("G", R("FW", 0, S), 0)
+    fill("G", R("MK0"), 1)
     ts(R("IA"), R("IP"), 4, A.arith_shift_right, 1, A.bitwise_and)
+    copy("V", R("RH", 0, 256, rows=1), R("WX", rows=1), -1.0, 959.0)
     copy("V", R("PX"), R("IA"))
+    copy("V", R("RH", 256, 512, rows=1), R("RH", 0, 256, rows=1), 1.0, -256.0)
     copy("V", R("PY"), R("IA"), -1.0, 1.0)
-    ts(R("Q00"), D0, 0.0, A.is_equal, R("PY"), A.mult)
+    ts(R("I1"), D0, 0.0, A.is_equal)
+    copy("V", R("RH", 512, 1024, rows=1), R("RH", 0, 512, rows=1), 1.0, -512.0)
     ts(R("Q11"), D0, 0.0, A.is_equal, R("PX"), A.mult)
-    ts(R("Q01"), D0, 16.0, A.is_equal, R("PY"), A.mult)
     ts(R("Q10"), D0, -16.0, A.is_equal, R("PX"), A.mult)
-    ts(R("I4"), D0, 0.0, A.is_equal, 4.0, A.mult)
-    fill(R("C14"), 2.0 ** -14)
-    copy("V", R("RH", rows=32), R("RI", rows=32))
+    ts(R("Q00"), D0, 0.0, A.is_equal, R("PY"), A.mult)
+    ts(R("Q01"), D0, 16.0, A.is_equal, R("PY"), A.mult)
     copy("V", R("OH"), R("OC"))
     vtr(R("OT"), R("OH"))
+    for c in (0, 2, 1, 3):
+        mm(R("P%d" % c), R("C16", rows=1), R("RH", 512 * (c % 2), 512 * (c % 2) + 512, rows=1), True, c > 1)
+        if c == 2:
+            mm(R("P6", 0, 144), R("E1", rows=8), R("E4", rows=8))
+            mm(R("P6", 256, 384), R("E1", rows=8), R("E1", rows=8))
     turn("P7", "OT", 0)
-    copy("V", R("OU"), R("P7", 0, 128))
-    for c in range(4):
-        mm(R("P%d" % c), R("C14", rows=1), R("RH", rows=1), True, False)
-        mm(R("P%d" % c), R("I4"), R("SK", 512 * c, 512 * c + 512), False, True)
-        copy("VS", R("SKF", 512 * c, 512 * c + 512), R("P%d" % c), 0.25, (3 - c) / 128.0)
-    for c in range(4):
-        gath("VS", R("W", 512 * c, 512 * c + 512), R("SKF"), R("OU", 32 * c, 32 * c + 32))
-    fill(R("W", S, S + 1), BIG)
-    fill(R("W", S + 1, WN), 0.0)
-    fill(R("XG", 0, 1), BIG)
-    fill(R("ZR", 0, 512), 0.0)
-    act(R("D1F"), R("ZR", 0, 512), F.Silu)
-    copy("S", R("ZR", 512, 1024), R("ZR", 0, 512))
-    for c in range(3):
-        copy("S", R("D1", 512 * c, 512 * c + 512), R("ZR", 0, 512))
-    copy("S", R("VV", 0, 128), R("ZR", 0, 128))
-    fill(R("FW", 0, S), 0, "G")
-    for t in range(RO):
-        fill(R("MK%d" % t), t + 1, "G")
     ts(R("IB"), R("IP"), 15, A.bitwise_and)
-    copy("V", R("PU"), R("IB"), -1.0, -49.0)
-    ts(R("Z"), R("WX", 0, 144), R("PU"), A.is_equal, KE, A.mult)
+    fill("V", R("W", S, S + 1), BIG)
     ts(R("PM"), R("IB"), 15.0, A.is_lt)
-    copy("V", R("PN"), R("PM"), -float(S), float(S))
-    ts(R("CU"), R("CD"), R("PM"), A.mult, R("PN"), A.add)
-    copy("V", R("CH"), R("CD"), 1.0, 1.0)
-    copy("V", R("CB"), R("CD"), 1.0, 1.0 - DUMP)
-    ts(R("IH"), D0, 0.0, A.is_equal)
-    vtr(R("CT"), R("CH"))
-    for u, i in enumerate((0, 15)):
-        for x in range(2):
-            for y in range(2):
-                mm(R("P7", 24 * u + x, 24 * u + 24, 2), R("Q%d%d" % (x, y)), R("CT", 16 * y + i, 384, 32), y == 0, y == 1)
-    copy("V", R("SL"), R("P7", 0, 48), 1.0, -1.0)
-    op("V", lambda e, z: e.tensor_scalar(ap(R("MH")), ap(R("CV")).indirect(ap(R("SL", 0, 24))), 1.0, None, A.add), [R("CV"), R("SL", 0, 24)], [R("MH")],
-       40 + TUNE["g"] * 384)
-    vtr(R("MT"), R("MH"))
-    ts(R("PV"), R("W4"), 0.0, A.is_equal)
-    for t in range(RO):
-        tag[0] = "m%d" % t
-        turn("P7", "MT", 128 * t)
-        copy("V", R("ML", 128 * t, 128 * t + 128), R("P7", 0, 128), 1.0, -1.0)
-        mm(R("P7", 0, 128), R("MH", 128 * t, 128 * t + 128), R("PV"))
-        copy("VS", R("PT", 128 * t, 128 * t + 128), R("P7", 0, 128))
-    tag[0] = ""
-    ts(R("T1"), R("W1"), 4, A.arith_shift_right)
-    ts(R("BK"), R("T1"), 0.0, A.is_equal)
-    ts(R("BKF"), R("T1"), 0.0, A.is_equal, -1024.0, A.mult)
-    ts(R("I4F"), D0, 0.0, A.is_equal, 4.0, A.mult)
-    t8 = R("T1", 0, 128, 16)
-    for k, w in enumerate((-WC, WC, -WC, 0.0, WC, 0.0)):
-        ts(R("SW", 8 * k, 8 * k + 8), t8, 0.0, A.is_equal, w, A.mult)
-    ts(R("B16"), t8, 0.0, A.is_equal)
-    ts(R("BK2", 0, 128), R("T1"), 0.0, A.is_equal, -WC, A.mult)
-    ts(R("BK2", 128, 256), R("T1"), 0.0, A.is_equal, WC, A.mult)
-    fill(R("BK2", 128, 256, 16), 0.0)
-    fill(R("ONE"), 1.0)
-    fill(R("CC", 0, 128, rows=32), -9.5 * WC)
-    fill(R("CC", 128, 256, rows=32), 9.5 * WC)
-    fill(R("CC", 128, 256, 16, rows=32), -1.0)
-    ts(R("TRI"), D0, 0.0, A.is_lt)
-    op("G", lambda e, z: e.affine_select(ap(R("NI")), ap(R("ZR", 0, 512)), [[0, 4], [-1, 128]], A.not_equal, -0.25, 0, 1), [R("ZR", 0, 512)], [R("NI")], 200 + 1024)
-    ts(R("S0R", 0, 256, 2), R("W1"), 0.0, A.mult)
-    ts(R("S0R", 1, 256, 2), R("W1"), 0.0, A.is_equal)
-    ts(R("O32", 0, 32, 2), R("W1", 0, 16), 0.0, A.mult, 1.0, A.add)
-    ts(R("O32", 1, 32, 2), R("W1", 0, 16), 0.0, A.mult)
-    ts(R("K32"), R("W1", 0, 32), 0.0, A.mult, 4096.0, A.add)
-    ts(R("W3"), R("W3"), 15, A.bitwise_and)
-    copy("V", R("PD"), R("IP"), 2.0, 2050.0)
-    copy("V", R("PE"), R("IP"), 2.0, 2306.0)
-    ts(R("DM", 0, 256, 2), R("W3", 0, 256, 2), 0.0, A.is_equal, R("PD"), A.mult)
-    ts(R("DM", 1, 256, 2), R("W3", 1, 256, 2), 0.0, A.is_equal, R("PE"), A.mult)
-    mm(R("P6", 0, 288), R("BK"), R("ND"))
-    for t in range(RO):
-        act(R("NZ", 128 * t, 128 * t + B), R("P6", B * t, B * t + B), F.Relu, -1.0, 1.0)
-    fill(R("NZ", B, 128), 1.0)
+    fill("V", R("XG", 0, 1), BIG)
+    copy("V", R("PN"), R("PM"), -float(S + 1), float(S))
+    fill("V", R("CK", rows=32), float(DUMP))
+    fill("V", R("D1"), 0.0)
+    fill("S", R("W", S + 1, WN), 0.0)
+    fill("S", R("VV", 0, 128), 0.0)
+    fill("S", R("NZ", B, 128), 1.0)
     for t in range(RO - 1):
-        copy("S", R("SB%d" % t, 0, U), R("ZR", 0, U), 1.0, -MAGIC)
+        fill("S", R("SB%d" % t, 0, U), -MAGIC)
+    bk = R("P6", 256, 384)
+    copy("S", R("Z"), R("P6", 0, 144), KE)
+    copy("S", R("BK"), bk)
+    copy("S", R("BKF"), bk, -1024.0)
+    copy("S", R("BK2", 0, 128), bk, -WC)
+    copy("S", R("BK2", 128, 256), bk, WC)
+    for k, w in enumerate((-WC, WC, -WC, 0.0, WC, 0.0)):
+        copy("S", R("SW", 8 * k, 8 * k + 8), R("P6", 256, 384, 16), w)
+    copy("S", R("B16"), R("P6", 256, 384, 16))
+    fill("S", R("BK2", 128, 256, 16), 0.0)
+    for c in range(4):
+        sk, o = R("SK", 512 * c, 512 * c + 512), R("SKF", 512 * c, 512 * c + 512)
+        if c < 2:
+            mm(R("P%d" % c), R("I1"), sk, False, True)
+            copy("S", o, R("P%d" % c), 1.0, 1.0 / 64)
+        else:
+            tt(o, sk, R("P%d" % c), A.add)
+        if c == 2:
+            copy("V", R("OU"), R("P7", 0, 128))
 
-    cut = TUNE["cut"]
+    def lists(a, b):
+        copy("V", R("CH", 128 * a, 128 * b), R("CD", 128 * a, 128 * b), 1.0, 1.0)
+        vtr(R("CT", 128 * a, 128 * b), R("CH", 128 * a, 128 * b))
+        ts(R("CU", 128 * a, 128 * b), R("CH", 128 * a, 128 * b), R("PM"), A.mult, R("PN"), A.add)
+        w = 8 * (b - a)
+        for u, i in enumerate((15, 0)):
+            for x in range(2):
+                for y in range(2):
+                    mm(R("P7", w * u + x, w * u + w, 2), R("Q%d%d" % (x, y)), R("CT", 128 * a + 16 * y + i, 128 * b, 32), y == 0, y == 1)
+
+    def ends(a, b):
+        copy("V", R("SL", 16 * a, 16 * b), R("P7", 0, 16 * (b - a)), 1.0, -1.0)
+
+    def SL(u, t):
+        return R("SL", 8 * u, 8 * u + 8) if t == 0 else R("SL", 8 + 16 * u + 8 * t, 16 + 16 * u + 8 * t)
+
+    def covers(t, now=True):
+        issue("V", lambda e: e.tensor_scalar(ap(R("MH")), ap(R("CV")).indirect(ap(SL(1, t))), 1.0, None, A.add), [R("CV"), SL(1, t)], [R("MH")])
+        vtr(R("MT"), R("MH"))
+        if now:
+            turn("P7", "MT", 0)
+
+    def coverlist(t):
+        copy("V", R("ML", 128 * (t % 2), 128 * (t % 2) + 128), R("P7", 0, 128), 1.0, -1.0)
+
+    def keys(t):
+        mm(R("P5" if t else "P1", 0, 128), R("MH"), R("PV"))
+        copy("S", R("PT", 128 * (t % 2), 128 * (t % 2) + 128), R("P5" if t else "P1", 0, 128))
+
+    def needs(q, t):
+        copy(q, R("D1", 0, 1536, 16), R("ND", B * t, B * t + B), -1.0)
+
+    lists(0, 1)
+    mm(R("P6", 0, 288), R("BK"), R("ND"))
+    for c in range(4):
+        gath("SV"[c % 2], R("W", 512 * c, 512 * c + 512), R("SKF"), R("OU", 32 * c, 32 * c + 32))
+        if c == 1:
+            ends(0, 1)
+    needs("V", 0)
+
+    def consts2():
+        iota(R("RP", rows=32), [[1, 128]], 129, 0)
+        ones_where(R("I1F"), [[-1, 128]], 0, 1)
+        issue("G", lambda e: e.affine_select(ap(R("TRI")), ap(R("ONE", 0, 128)), [[-1, 128]], A.is_gt, 0.0, 0, 1), [R("ONE")], [R("TRI")])
+        iota(R("CC", 0, 128, rows=32), [[0, 128]], int(-9.5 * WC), 0)
+        iota(R("CC", 128, 256, rows=32), [[0, 128]], int(9.5 * WC), 0)
+        iota(R("CC", 128, 256, 16, rows=32), [[0, 8]], -1, 0)
+        ones_where(R("PV"), [[-16, 8], [1, 16]], -15, 1)
+        issue("G", lambda e: e.affine_select(ap(R("NI")), ap(R("ZR")), [[0, 4], [-1, 128]], A.not_equal, -1.0, 0, 1), [R("ZR")], [R("NI")])
+        ones_where(R("S0R"), [[-16, 8], [0, 16], [-1000, 2]], 1000, 1)
+        ones_where(R("E2", rows=16), [[0, 8], [-1, 16]], 0, 1)
+        ones_where(R("E3", rows=16), [[0, 8], [-1, 16], [0, 2]], 0, 1)
+        iota(R("PD"), [[0, 1]], 2050, 2)
+        iota(R("PE"), [[0, 1]], 2306, 2)
+        iota(R("O32"), [[0, 16], [-1, 2]], 1, 0)
+        iota(R("K32"), [[0, 32]], 4096, 0)
+
+    def consts3():
+        act(R("DM", 0, 256, 2), R("P0", 0, 256, 2), F.Copy, R("PD"))
+        act(R("DM", 1, 256, 2), R("P0", 1, 256, 2), F.Copy, R("PE"))
+
+    consts2()
+
+    cut, cov = TUNE["cut"], TUNE["cov"]
     for t in range(RO):
-        last = t == RO - 1
-        WG, WS = R("W", 0, S + 1), R("W")
-        copy("VS", R("D1", 0, 1536, 16), R("ND", B * t, B * t + B), -1.0)
-        if t > 0:
-            copy("VS", R("D1F", 0, 512, 16), R("ARR%d" % (t - 1)), 1.0, MAGIC)
-            mm(R("P5", 0, U), R("BKF"), R("D1F", 0, 512, 16))
-            act(R("NZ", 128 * t + B, 128 * t + 128), R("P5", 0, U), F.Relu, -1.0, 1.0)
-        for (a, b, q) in TUNE["gath"]:
-            gath(q, R("XG", 1 + 16 * a, 1 + 16 * b), WG, R("CU", 128 * t + a, 128 * t + b))
-        if not last:
-            gath("VS", R("X15"), WG, R("SL", 24 + 8 * t, 32 + 8 * t))
-        for (a, b, q) in TUNE["gath"]:
-            d1 = R("D1", 16 * a, 16 * b) if a < B else R("D1F", 16 * (a - B), 16 * (b - B))
-            scan(R("EE", 16 * a, 16 * b), R("XG", 16 * a, 16 * b), d1, A.add, A.min)
-        for k, (a, b) in enumerate(TUNE["wrap"]):
-            p = R("P%d" % (k % 2), 0, b - a)
-            mm(p, R("IH"), R("CH", 128 * t + a, 128 * t + b), True, False)
+        last, c0, c1 = t == RO - 1, 128 * t, 128 * (t % 2)
+        x0 = R("XG", 1, S, 16)
+
+        def openings():
+            for k in range(2):
+                mm(R("P%d" % (2 + k)), R("I1"), R("NI"), True, False)
+            mm(R("P6", 0, 256), R("CH", c0, c0 + 128), R("S0R"), True, False)
+            if t == 0:
+                mm(R("P0", 0, 256), R("E2", rows=16), R("E3", rows=16))
+            else:
+                mm(R("P4", 0, 256), R("ONE", 0, 128, rows=1), R("CC", rows=1), True, False)
+
+        def cards(q, a):
+            gath(q, R("XG", 1 + 16 * a, 513 + 16 * a), WG, R("CU", c0 + a, c0 + a + 32))
+
+        def sums(a):
+            scan(R("EE", 16 * a, 16 * a + 512), R("XG", 16 * a, 16 * a + 512), R("D1", 16 * a, 16 * a + 512) if a < B else R("D1F"), A.add, A.min)
+
+        def wrap(k, a, b):
+            p = R("P%d" % k, 0, b - a)
+            mm(p, R("I1"), R("CH", c0 + a, c0 + b), True, False)
+            mm(p, R("ONE", 0, 128, rows=1), R("CK", 0, b - a, rows=1), False, False)
             for i in range(16):
                 mm(p, Z(i), R("EE", 16 * a + i, 16 * b, 16), False, i == 15)
-            tt(R("LF", a, b), p, R("CB", 128 * t + a, 128 * t + b), A.max)
-            copy("V", R("LL", a, b), R("LF", a, b), 1.0, DUMP - 1.0)
-        x0 = R("XG", 1, S, 16)
-        ts(R("TH", 0, 128), x0, -1.0 / 32, A.add, 2.0 ** -16, A.max)
-        cw = S // TUNE["cov"]
-        k = 128
-        while k < cw:
-            copy("VS", R("TH", k, 2 * k), R("TH", 0, k))
-            k *= 2
-        act(R("BS"), x0, F.Relu, -65536.0, 1.0)
-        ends = sorted(set([a for (a, b) in TUNE["wrap"]] + [cut, 128]))
-        pieces = list(zip(ends[:-1], ends[1:]))
-        for (a, b) in pieces:
-            if b <= cut:
-                scat("S", WS, R("LL", a, b), R("ZR", 0, 16 * (b - a)))
-            else:
-                for a2 in range(a, b, 32):
-                    b2 = min(b, a2 + 32)
-                    scat("V", R("FW"), R("LL", a2, b2), R("MK%d" % t, 0, 16 * (b2 - a2)))
-        if not last:
-            tag[0] = "h%d" % t
-            for i in range(16):
-                mm(R("P5", 0, 128), R("I4"), R("XG", 1 + i, S, 16) if i < 15 else R("X15"), i == 0, False)
-            if t > 0:
-                mm(R("P5", B, 128), R("I4F"), R("D1F", 0, 512, 16), False, False)
-            mm(R("P5", 0, B), R("I4"), R("D1", 0, 1536, 16), False, True)
-            act(R("RF"), R("P5", 0, 128), F.Relu, -0.25)
-            mm(R("P5", 0, 128), R("ONE", rows=1), R("RP", rows=1), True, False)
-            mm(R("P5", 0, 128), R("BKF"), R("RF"), False, True)
-            act(R("ZZ"), R("P5", 0, 128), F.Relu)
-            act(R("UU"), R("ZZ"), F.Relu, -1.0, 1.0)
-            scan(R("CN"), R("UU"), R("UU"), A.add, A.max)
-            for k, src in enumerate(("ZZ", "CN")):
-                for r in range(16):
-                    mm(R("P5", 0, 8), Z(r), R(src, r, 128, 16), k == 0 and r == 0, k == 1 and r == 15)
-            copy("V", R("OL"), R("P5", 0, 8), 1.0 / (16 * KE), -1.0)
-            sl = "SB%d" % t
 
-            def put(e, z, sl=sl):
-                return e.tensor_scalar(ap(R(sl)).indirect(ap(R("OL"))), ap(R("RF")), -(1.0 + 2.0 ** -14), -MAGIC, A.mult, A.add)
-            op("V", put, [R("OL"), R("RF")], [R(sl)], 40 + TUNE["sc"] * 128)
+        def leave(k, a, b):
+            tt(R("LF", a, b), R("P%d" % k, 0, b - a), R("CH", c0 + a, c0 + b), A.max)
+            copy("V", R("LL", a, b), R("LF", a, b), 1.0, -1.0)
+
+        def zero(a, b):
+            scat("S", WS, R("LL", a, b), R("ZR", 0, 16 * (b - a)))
+
+        def mark(a, b):
+            scat("V", R("FW"), R("LL", a, b), R("MK%d" % t, 0, 16 * (b - a)))
+
+        if t > 0:
+            copy("G", R("D1F", 0, 512, 16), R("ARR%d" % (t - 1)))
+        cards("V", 0)
+        cards("S", 32)
+        cards("S", 64)
+        cards("S", 96)
+        if t > 0:
+            openings()
+        sums(0)
+        wrap(0, 0, 32)
+        sums(32)
+        if not last:
+            gath("S", R("X15"), WG, SL(0, t))
+        sums(64)
+        wrap(1, 32, 96)
+        leave(0, 0, 32)
+        act(R("TH", 0, 128), x0, F.Relu, 1.0, -1.0 / 32)
+        zero(0, 32)
+        copy("G", R("TH", 128, 256), R("TH", 0, 128))
+        copy("G", R("TH", 256, 512), R("TH", 0, 256))
+        sums(96)
+        wrap(0, 96, 128)
+        if t == 0:
+            covers(t)
+        leave(1, 32, 96)
+        zero(32, 64)
+        mark(64, 96)
+        leave(0, 96, 128)
+        if t == 0:
+            coverlist(t)
+        if cut < 128:
+            zero(cut, 128)
+        if cut > 96:
+            mark(96, cut)
+        if not last:
+            for i in range(16):
+                mm(R("P5", 0, 128), R("I1"), R("XG", 1 + i, S, 16) if i < 15 else R("X15"), i == 0, False)
+            if t > 0:
+                mm(R("P5", B, 128), R("I1F"), R("D1F", 0, 512, 16), False, False)
+            mm(R("P5", 0, B), R("I1"), R("D1", 0, 1536, 16), False, True)
+            act(R("RF"), R("P5", 0, 128), F.Relu, -1.0)
+            mm(R("P5", 0, 128), R("ONE", 0, 128, rows=1), R("RP", rows=1), True, False)
+            mm(R("P5", 0, 128), R("BKF"), R("RF"), False, True)
+        if t == 0:
+            mm(R("P4", 0, 256), R("ONE", 0, 128, rows=1), R("CC", rows=1), True, False)
+        else:
+            mm(R("P1", 0, U), R("BKF"), R("D1F", 0, 512, 16))
+
+        def cover(a, b):
+            m, th, p = R("CM", 128 * a, 128 * b), R("TH", 0, 128 * (b - a)), R("ML", c1 + 8 * a, c1 + 8 * b)
+            issue("V", lambda e: e.tensor_tensor(ap(m), ap(WG).indirect(ap(p)), ap(th), A.is_gt), [WG, p, th], [m])
+            f, w = R("FL", 128 * a, 128 * b), R("FW", 0, S)
+            issue("S", lambda e: e.activation(ap(f), ap(w).indirect(ap(p)), F.Relu, bias=-float(t)), [w, p], [f])
+            for i in range(a, b):
+                mm(R("P4", 15 - i, 256, 16), R("CM", 128 * i, 128 * i + 128), R("SW", 8, 24) if i < 15 else R("SW", 32, 48), False, False)
+            for i in range(a, b):
+                mm(R("P4", 15 - i, 256, 16), R("FL", 128 * i, 128 * i + 128), R("SW", 0, 16) if i < 15 else R("SW", 16, 32), False, i == 15)
+
+        sl = "SB%d" % t
+        for k in range(len(cov) - 1):
+            cover(cov[k], cov[k + 1])
+            if k == 0 and not last:
+                act(R("ZC", 0, 128), R("P5", 0, 128), F.Relu)
+                act(R("UU"), R("ZC", 0, 128), F.Relu, -1.0, 1.0)
+            if k == 1:
+                act(R("BS"), x0, F.Relu, -65536.0, 1.0)
+                if t > 0:
+                    act(R("NZ", c0 + B, c0 + 128), R("P1", 0, U), F.Relu, -1.0, 1.0)
+                else:
+                    for u in range(RO):
+                        act(R("NZ", 128 * u, 128 * u + B), R("P6", B * u, B * u + B), F.Relu, -1.0, 1.0)
+                    keys(t)
+                mm(R("P4", 0, 256), R("BS"), R("BK2"), False, False)
+                mm(R("P4", 0, 256), R("NZ", c0, c0 + 128), R("BK2"), False, False)
+            if k == 2 and t == 0:
+                openings()
+            if k == 1 and not last:
+                scan(R("ZC", 128, 256), R("UU"), R("UU"), A.add, A.max)
+                vtr(R("ZT"), R("ZC"))
+                for x in range(2):
+                    for y in range(2):
+                        for u in range(2):
+                            mm(R("P5", x, 8, 2), R("Q%d%d" % (x, y)), R("ZT", 128 * u + 16 * y, 128 * u + 128, 32), y + u == 0, y + u == 2)
+            if k == 2 and not last:
+                copy("V", R("OL"), R("P5", 0, 8), 1.0, -1.0)
+        if not last:
+            issue("V", lambda e: e.tensor_scalar(ap(R(sl)).indirect(ap(R("OL"))), ap(R("RF")), -(1.0 + 2.0 ** -14), -MAGIC, A.mult, A.add),
+                  [R("OL"), R("RF")], [R(sl)])
+            so = R("SO%d" % t)
+            copy("S", so, R(sl, 0, U), 1.0, MAGIC)
             rl = relay_of(rank)
             m, k = emask(core, rl)
             rid, pid = topo.addr(rl, core)
             _, ka = emask(relay_of((rank - 1) % n), core)
-
-            def send(e, z, t=t, sl=sl, rid=rid, pid=pid, m=m):
-                return e.remote_dma(T["RB%d" % t][:, :], ap(R(sl, 0, U)), T.sem["rin%d" % t], T.sem["out%d" % t], pid, rid, m)
-            add("G", send, [R(sl, 0, U)], [R("ARR%d" % t)], 0.6, kind="m", lat=TUNE["rlat"], extra=("arr%d" % t, ka, "out%d" % t, k))
-            tag[0] = ""
-        mm(R("P4", 0, 256), R("ONE", rows=1), R("CC", rows=1), True, False)
-        mm(R("P4", 0, 256), R("BS"), R("BK2"), False, False)
-        mm(R("P4", 0, 256), R("NZ", 128 * t, 128 * t + 128), R("BK2"), False, False)
-        for k in range(2):
-            mm(R("P%d" % (2 + k)), R("I4"), R("NI"), True, False)
-        mm(R("P6", 0, 256), R("CH", 128 * t, 128 * t + 128), R("S0R"), True, False)
-
-        def cover(c, t=t, cw=cw):
-            m, b, p = R("CM", cw * c, cw * c + cw), R("TH", 0, cw), R("ML", 128 * t + cw // 16 * c, 128 * t + cw // 16 * (c + 1))
-            op("V", lambda e, z: e.tensor_tensor(ap(m), ap(WG).indirect(ap(p)), ap(b), A.is_ge), [WG, p, b], [m], 40 + TUNE["g"] * cw)
-            f, w = R("FL", cw * c, cw * c + cw), R("FW", 0, S)
-            op("S", lambda e, z: e.activation(ap(f), ap(w).indirect(ap(p)), F.Relu, bias=-float(t)), [w, p], [f], 40 + TUNE["g"] * cw)
-            for i in range(cw // 128 * c, cw // 128 * (c + 1)):
-                o = R("P4", 15 - i, 256, 16)
-                mm(o, R("CM", 128 * i, 128 * i + 128), R("SW", 8, 24) if i < 15 else R("SW", 32, 48), False, False)
-                mm(o, R("FL", 128 * i, 128 * i + 128), R("SW", 0, 16) if i < 15 else R("SW", 16, 32), False, i == 15)
-        for c in range(TUNE["cov"]):
-            cover(c)
-        scat("S", WS, R("LL", cut, 128), R("ZR", 0, 16 * (128 - cut)))
-        tt(R("KY"), R("P4", 0, 128), R("PT", 128 * t, 128 * t + 128), A.min)
+            issue("G", lambda e: e.remote_dma(T["RB%d" % t][:, :], ap(so), T.sem["rin%d" % t], T.sem["out%d" % t], pid, rid, m),
+                  [so], [R("ARR%d" % t)], sem=("arr%d" % t, ka))
+            total["out%d" % t] = k
+            fill("G", R("MK%d" % (t + 1)), t + 2)
+        zero(64, 96)
+        if cut > 96:
+            zero(96, cut)
+        if t == 0:
+            lists(1, 3)
+        tt(R("KY"), R("P4", 0, 128), R("PT", c1, c1 + 128), A.min)
         scan(R("SC"), R("P4", 128, 256), R("KY"), A.min, A.max)
-        for q in range(8):
-            ts(R("DG", 128 * q, 128 * q + 128), R("IH"), R("SC", 16 * q + 15, 16 * q + 16), A.mult)
+        if t == 0:
+            ends(1, 3)
+            consts3()
         for k in range(2):
+            for q in range(4 * k, 4 * k + 4):
+                ts(R("DG", 128 * q, 128 * q + 128), R("I1"), R("SC", 16 * q + 15, 16 * q + 16), A.mult)
             mm(R("P%d" % (2 + k)), R("TRI"), R("DG", 512 * k, 512 * k + 512), False, True)
         for q in range(8):
             mm(R("P6", 32 * q, 32 * q + 32), R("DG", 128 * q, 128 * q + 128), R("O32"), False, False)
+        if not last:
+            covers(t + 1, False)
         for q in range(8):
             ts(R("EQ", 128 * q, 128 * q + 128), R("P%d" % (2 + q // 4), 128 * (q % 4), 128 * (q % 4) + 128), R("SC", 16 * q + 15, 16 * q + 16), A.is_equal)
             mm(R("P6", 32 * q, 32 * q + 32), R("EQ", 128 * q, 128 * q + 128), R("K32"), False, q == 7)
+        if not last:
+            needs("S", t + 1)
         tt(R("FM"), R("P6", 0, 256), R("DM"), A.min)
         for k in range(2):
             mm(R("P4", 8 * k, 8 * k + 8), R("FM", k, 256, 2), R("B16"))
+        if not last:
+            turn("P7", "MT", 0)
         copy("V", R("LU"), R("P4", 0, 16), 1.0, -1.0)
         gath("V", R("VV", 128, 256), R("W", 0, WN), R("LU", 0, 8))
         scat("V", R("W", 0, WN), R("LU"), R("VV"))
+        if not last:
+            coverlist(t + 1)
+            keys(t + 1)
 
-    dma("Y", T.YC[:, :], T.W[0:128:16, 0:S], [R("W", 0, S)], [R("YC")], 2.0)
+    dma("Y", T.YC[:, :], T.W[0:128:16, 0:S], [R("W", 0, S)], [R("YC")])
     copy("V", R("YI"), R("YC"), 65536.0)
     ts(R("YJ"), R("YI"), 2047, A.bitwise_and)
     copy("V", R("YO"), R("YJ"), -1.0, 2047.0)
-    dma("Y", T.y[:, :], T.YO[:, :], [R("YO")], [], 2.0)
-
-    if "at" not in ORDER:
-        ORDER["end"], ORDER["at"], ORDER["on"] = arrange(ops)
-    at, on = ORDER["at"], ORDER["on"]
-    m = len(ops)
-    cnt = {k: 0 for k in CS}
-    known = {k: {} for k in Q}
-    total = {}
-    done = [None] * m
-    nd = 0
-    for i in sorted(range(m), key=lambda i: (at[i], i)):
-        o = ops[i]
-        q = on[i]
-        need = {}
-        for j, e in o["edges"].items():
-            if e == 0 and on[j] == q and ops[j]["kind"] == "c" and o["kind"] == "c":
-                continue
-            need[done[j][0]] = max(need.get(done[j][0], 0), done[j][1])
-        for s in sorted(need):
-            if known[q].get(s, 0) < need[s]:
-                Q[q].wait_ge(T.sem[s], need[s])
-                known[q][s] = need[s]
-        ins = o["fn"](Q[q], q)
-        if o["kind"] == "c":
-            cnt[q] += 1
-            ins.then_inc(T.sem[CS[q]], 1)
-            done[i] = (CS[q], cnt[q])
-        elif o["kind"] == "d":
-            done[i] = ("d%d" % nd, 16)
-            nd += 1
-            ins.then_inc(T.sem[done[i][0]], 16)
-        else:
-            done[i] = (o["x"][0], o["x"][1])
-            total[o["x"][2]] = o["x"][3]
-        total[done[i][0]] = max(total.get(done[i][0], 0), done[i][1])
+    dma("Y", T.y[:, :], T.YO[:, :], [R("YO")], [])
     for s in sorted(total):
         if known["G"].get(s, 0) < total[s]:
             g.wait_ge(T.sem[s], total[s])

@@ -8,7 +8,7 @@ WW, WN = 4112, 2560
 KE = 8192.0
 WC = 4096.0
 MAGIC = 12582912.0
-NENG = 8
+NENG = 4
 
 SCRATCH = {}
 for _n, _w, _d in [
@@ -16,8 +16,8 @@ for _n, _w, _d in [
         ("W", WW, FP), ("FW", WW, BF), ("XG", S + 16, BF), ("EE", S, BF), ("D1", 1536, BF), ("D1F", 512, FP), ("CM", S, BF), ("FL", S, BF),
         ("ZR", 512, FP), ("MK0", 512, BF), ("MK1", 512, BF), ("MK2", 512, BF), ("TH", 512, BF), ("RH", 1024, F16),
         ("OH", 128, F16), ("OT", 128, F16), ("OU", 128, U16), ("CU", 384, U16), ("CH", 384, F16), ("CT", 384, F16),
-        ("SL", 48, U16), ("MH", 128, F16), ("MT", 128, F16), ("ML", 256, U16), ("PT", 256, FP), ("NZ", 384, BF), ("BS", 128, BF),
-        ("SO0", U, FP), ("SO1", U, FP),
+        ("SL", 48, U16), ("MH", 128, F16), ("MT", 128, F16), ("ML", 128, U16), ("PT", 128, FP), ("NZ", 384, BF), ("BS", 128, BF),
+        ("SO0", U, FP), ("SO1", U, FP), ("SN", U, FP), ("RS", 128, FP),
         ("LF", 128, FP), ("LL", 128, U16), ("X15", 128, BF), ("KY", 128, FP), ("SC", 128, FP), ("DG", 1024, F16), ("EQ", 1024, BF),
         ("FM", 256, F16), ("LU", 16, U16), ("VV", 256, FP), ("RF", 128, FP), ("ZC", 256, BF), ("ZT", 256, BF), ("UU", 128, BF),
         ("OL", 8, U16), ("SB0", 512, FP), ("SB1", 512, FP), ("ARR0", U, FP), ("ARR1", U, FP), ("RB0", U, FP), ("RB1", U, FP),
@@ -31,7 +31,7 @@ for _b, _d, _l in [
         ("GF", FP, [("PX", 8), ("PY", 8), ("PM", 8), ("PN", 8), ("PD", 8), ("PE", 8)]),
         ("GB", BF, [("I1", 128), ("Z", 144), ("BK", 128), ("SW", 48), ("RP", 128), ("PV", 128), ("TRI", 128), ("Q00", 128), ("Q01", 128),
                     ("Q10", 128), ("Q11", 128), ("B16", 16), ("O32", 32), ("K32", 32), ("C16", 128), ("E1", 128), ("E2", 128), ("E4", 144),
-                    ("CK", 64)])]:
+                    ("CK", 64), ("NEG", 128)])]:
     _o = 0
     for _n, _w in _l:
         PARTS[_n] = (_b, _o, 1 if _b in ("GI", "GF") else {"B16": 8}.get(_n, _w))
@@ -40,7 +40,13 @@ for _b, _d, _l in [
 for _k in range(8):
     SCRATCH["P%d" % _k] = ("psum", [128, 512], FP)
 SEMAPHORES = ["cV", "cS", "cP", "cG"] + ["d%d" % k for k in range(12)] + ["arr0", "arr1", "rin0", "rin1", "out0", "out1"]
-TUNE = {"cov": [0, 4, 8, 12, 16], "cut": 112}
+TUNE = {"cov": [[0, 4, 8, 12, 16], [0, 4, 8, 12, 16], [0, 4, 8, 12, 15, 16]], "cut": [112, 116, 114], "gs": 128}
+ON = {"x15": "V", "th": "V", "bs": "V", "nz": "V", "rf": "S", "uu": "S", "zc": "S", "so": "V", "take": "V", "eq": "V",
+      "f0": "S", "f1": "S", "f2": "S", "f3": "S", "f4": "S"}
+ORDER = """g0 b16 g1 g2 g4 arr ends0 g3 s0 x15 s1 s2 w0 nz0 l0 ch ml L0 s3 w1 oc0 l1 th cov0 L1 bs vm0 m1 w2 pt l2 nzm z0 turn0 z1 tot0 tot1
+nz th2 ml0 sb L2 z2 th4 pt0 m2 c0 f0 rf c1 knz kbs nf0 short nc0 c2 nz1 f1 uu num zc consts nc1 vz2 f2 c3 c4 nf1 nc2 f3 turnz dmm nz2 f4
+nf2 Z1 ol nc3 dm0 nf3 Z2 dm1 endt put op0 nc4 nf4 key wz so pick ends pairs ol0 e0 choices e1 cov win0 win1 u0 vz olist u1 send take cu
+move needs op vm oc turn""".split()
 
 
 def rank_program(g, core, T, topo):
@@ -195,18 +201,23 @@ def rank_program(g, core, T, topo):
         else:
             issue("G", lambda e: e.iota(ap(o), pat, base, cm, allow_small_or_imprecise_dtypes=True), [], [o])
 
+    def select(o, i, pat, op, other, base, cm):
+        issue("G", lambda e: e.affine_select(ap(o), ap(i), pat, op, other, base, cm), [i], [o])
+
     def ones_where(o, pat, base, cm):
-        i = R("ONE", 0, width(o), rows=o[4])
-        issue("G", lambda e: e.affine_select(ap(o), ap(i), pat, A.is_equal, 0.0, base, cm), [i], [o])
+        select(o, R("ONE", 0, width(o), rows=o[4]), pat, A.is_equal, 0.0, base, cm)
 
     def vtr(o, i):
         issue("V", lambda e: e.transpose(ap(o), ap(i)), [i], [o])
 
-    def turn(bank, src, c0):
+    def Qm(x, y):
+        return R("Q%d%d" % (x, y))
+
+    def turn(bank, src):
         for b in range(4):
             for x in range(2):
                 for y in range(2):
-                    mm(R(bank, 2 * b + x, 128, 8), R("Q%d%d" % (x, y)), R(src, c0 + 32 * b + 16 * y, c0 + 32 * b + 16 * y + 16), y == 0, y == 1)
+                    mm(R(bank, 2 * b + x, 128, 8), Qm(x, y), R(src, 32 * b + 16 * y, 32 * b + 16 * y + 16), y == 0, y == 1)
 
     def Z(i):
         return R("Z", 15 - i, 143 - i)
@@ -222,76 +233,19 @@ def rank_program(g, core, T, topo):
     dma("Y", T.CD[:, 128:384], T.cards[:, 128:384], [], [R("CD", 128, 384)])
     dma("Y", T.CV[:, :], T.cover[:, :], [], [R("CV")])
 
-    iota(R("IP"), [[0, 1]], 0, 1)
-    iota(R("WX"), [[1, 256]], -64, -1)
-    fill("V", R("ONE"), 1.0)
-    fill("V", R("ZR"), 0.0)
-    fill("V", R("C16", rows=32), 2.0 ** -16)
-    act(R("D1F"), R("ZR"), F.Silu)
-    ones_where(R("E1", rows=8), [[-1, 8], [0, 16]], 0, 1)
-    ones_where(R("E4", rows=8), [[1, 144]], -15, -16)
-    fill("G", R("FW", 0, S), 0)
-    fill("G", R("MK0"), 1)
-    ts(R("IA"), R("IP"), 4, A.arith_shift_right, 1, A.bitwise_and)
-    copy("V", R("RH", 0, 256, rows=1), R("WX", rows=1), -1.0, 959.0)
-    copy("V", R("PX"), R("IA"))
-    copy("V", R("RH", 256, 512, rows=1), R("RH", 0, 256, rows=1), 1.0, -256.0)
-    copy("V", R("PY"), R("IA"), -1.0, 1.0)
-    ts(R("I1"), D0, 0.0, A.is_equal)
-    copy("V", R("RH", 512, 1024, rows=1), R("RH", 0, 512, rows=1), 1.0, -512.0)
-    ts(R("Q11"), D0, 0.0, A.is_equal, R("PX"), A.mult)
-    ts(R("Q10"), D0, -16.0, A.is_equal, R("PX"), A.mult)
-    ts(R("Q00"), D0, 0.0, A.is_equal, R("PY"), A.mult)
-    ts(R("Q01"), D0, 16.0, A.is_equal, R("PY"), A.mult)
-    copy("V", R("OH"), R("OC"))
-    vtr(R("OT"), R("OH"))
-    for c in (0, 2, 1, 3):
-        mm(R("P%d" % c), R("C16", rows=1), R("RH", 512 * (c % 2), 512 * (c % 2) + 512, rows=1), True, c > 1)
-        if c == 2:
-            mm(R("P6", 0, 144), R("E1", rows=8), R("E4", rows=8))
-            mm(R("P6", 256, 384), R("E1", rows=8), R("E1", rows=8))
-    turn("P7", "OT", 0)
-    ts(R("IB"), R("IP"), 15, A.bitwise_and)
-    fill("V", R("W", S, S + 1), BIG)
-    ts(R("PM"), R("IB"), 15.0, A.is_lt)
-    fill("V", R("XG", 0, 1), BIG)
-    copy("V", R("PN"), R("PM"), -float(S + 1), float(S))
-    fill("V", R("CK", rows=32), float(DUMP))
-    fill("V", R("D1"), 0.0)
-    fill("S", R("W", S + 1, WN), 0.0)
-    fill("S", R("VV", 0, 128), 0.0)
-    fill("S", R("NZ", B, 128), 1.0)
-    for t in range(RO - 1):
-        fill("S", R("SB%d" % t, 0, U), -MAGIC)
-    bk = R("P6", 256, 384)
-    copy("S", R("Z"), R("P6", 0, 144), KE)
-    copy("S", R("BK"), bk)
-    copy("S", R("BKF"), bk, -1024.0)
-    copy("S", R("BK2", 0, 128), bk, -WC)
-    copy("S", R("BK2", 128, 256), bk, WC)
-    for k, w in enumerate((-WC, WC, -WC, 0.0, WC, 0.0)):
-        copy("S", R("SW", 8 * k, 8 * k + 8), R("P6", 256, 384, 16), w)
-    copy("S", R("B16"), R("P6", 256, 384, 16))
-    fill("S", R("BK2", 128, 256, 16), 0.0)
-    for c in range(4):
-        sk, o = R("SK", 512 * c, 512 * c + 512), R("SKF", 512 * c, 512 * c + 512)
-        if c < 2:
-            mm(R("P%d" % c), R("I1"), sk, False, True)
-            copy("S", o, R("P%d" % c), 1.0, 1.0 / 64)
-        else:
-            tt(o, sk, R("P%d" % c), A.add)
-        if c == 2:
-            copy("V", R("OU"), R("P7", 0, 128))
-
-    def lists(a, b):
+    def cards16(a, b):
         copy("V", R("CH", 128 * a, 128 * b), R("CD", 128 * a, 128 * b), 1.0, 1.0)
-        vtr(R("CT", 128 * a, 128 * b), R("CH", 128 * a, 128 * b))
+
+    def cardlist(a, b):
         ts(R("CU", 128 * a, 128 * b), R("CH", 128 * a, 128 * b), R("PM"), A.mult, R("PN"), A.add)
+
+    def ends_turn(a, b):
+        vtr(R("CT", 128 * a, 128 * b), R("CH", 128 * a, 128 * b))
         w = 8 * (b - a)
         for u, i in enumerate((15, 0)):
             for x in range(2):
                 for y in range(2):
-                    mm(R("P7", w * u + x, w * u + w, 2), R("Q%d%d" % (x, y)), R("CT", 128 * a + 16 * y + i, 128 * b, 32), y == 0, y == 1)
+                    mm(R("P7", w * u + x, w * u + w, 2), Qm(x, y), R("CT", 128 * a + 16 * y + i, 128 * b, 32), y == 0, y == 1)
 
     def ends(a, b):
         copy("V", R("SL", 16 * a, 16 * b), R("P7", 0, 16 * (b - a)), 1.0, -1.0)
@@ -299,69 +253,113 @@ def rank_program(g, core, T, topo):
     def SL(u, t):
         return R("SL", 8 * u, 8 * u + 8) if t == 0 else R("SL", 8 + 16 * u + 8 * t, 16 + 16 * u + 8 * t)
 
-    def covers(t, now=True):
+    def covers(t):
         issue("V", lambda e: e.tensor_scalar(ap(R("MH")), ap(R("CV")).indirect(ap(SL(1, t))), 1.0, None, A.add), [R("CV"), SL(1, t)], [R("MH")])
-        vtr(R("MT"), R("MH"))
-        if now:
-            turn("P7", "MT", 0)
 
-    def coverlist(t):
-        copy("V", R("ML", 128 * (t % 2), 128 * (t % 2) + 128), R("P7", 0, 128), 1.0, -1.0)
+    def covers_turn(bank):
+        turn("P7", "MT")
+        mm(R(bank, 128, 256), R("MH"), R("PV"))
 
-    def keys(t):
-        mm(R("P5" if t else "P1", 0, 128), R("MH"), R("PV"))
-        copy("S", R("PT", 128 * (t % 2), 128 * (t % 2) + 128), R("P5" if t else "P1", 0, 128))
+    def coverlist():
+        copy("V", R("ML"), R("P7", 0, 128), 1.0, -1.0)
+
+    def keys(bank):
+        copy("S", R("PT"), R(bank, 128, 256))
 
     def needs(q, t):
         copy(q, R("D1", 0, 1536, 16), R("ND", B * t, B * t + B), -1.0)
 
-    lists(0, 1)
-    mm(R("P6", 0, 288), R("BK"), R("ND"))
+    def noneed(t):
+        act(R("NZ", 128 * t, 128 * t + B), R("P7", 128 + B * t, 128 + B * t + B), F.Relu, -1.0, 1.0)
+
+    def open_pairs():
+        for k in range(2):
+            mm(R("P%d" % (2 + k)), R("I1"), R("NI"), True, False)
+
+    def open_lists(t):
+        mm(R("P6", 0, 256), R("CH", 128 * t, 128 * t + 128), R("S0R"), True, False)
+
+    def open_counts():
+        mm(R("P4", 0, 256), R("ONE", 0, 128, rows=1), R("CC", rows=1), True, False)
+
+    iota(R("WX"), [[1, 256]], -64, -1)
+    iota(R("IP"), [[0, 1]], 0, 1)
+    fill("V", R("ONE"), 1.0)
+    fill("V", R("C16", rows=32), 2.0 ** -16)
+    fill("V", R("ZR"), 0.0)
+    act(R("D1F"), R("ZR"), F.Silu)
+    ones_where(R("E1", rows=8), [[-1, 8], [0, 16]], 0, 1)
+    ones_where(R("E4", rows=8), [[1, 144]], -15, -16)
+    fill("G", R("FW", 0, S), 0)
+    fill("G", R("MK0"), 1)
+    copy("V", R("RH", 0, 256, rows=1), R("WX", rows=1), -1.0, 959.0)
+    ts(R("IA"), R("IP"), 4, A.arith_shift_right, 1, A.bitwise_and)
+    copy("V", R("RH", 256, 512, rows=1), R("RH", 0, 256, rows=1), 1.0, -256.0)
+    copy("V", R("PX"), R("IA"))
+    copy("V", R("PY"), R("IA"), -1.0, 1.0)
+    copy("V", R("RH", 512, 1024, rows=1), R("RH", 0, 512, rows=1), 1.0, -512.0)
+    ts(R("Q11"), D0, 0.0, A.is_equal, R("PX"), A.mult)
+    ts(R("Q10"), D0, -16.0, A.is_equal, R("PX"), A.mult)
+    ts(R("Q00"), D0, 0.0, A.is_equal, R("PY"), A.mult)
+    ts(R("Q01"), D0, 16.0, A.is_equal, R("PY"), A.mult)
+    copy("V", R("OH"), R("OC"))
+    ts(R("I1"), D0, 0.0, A.is_equal)
+    vtr(R("OT"), R("OH"))
+    for c in (0, 2, 1, 3):
+        mm(R("P%d" % c), R("C16", rows=1), R("RH", 512 * (c % 2), 512 * (c % 2) + 512, rows=1), True, c > 1)
+        if c == 2:
+            mm(R("P6", 0, 144), R("E1", rows=8), R("E4", rows=8))
+            mm(R("P6", 256, 384), R("E1", rows=8), R("E1", rows=8))
+    fill("V", R("D1"), 0.0)
+    ts(R("IB"), R("IP"), 15, A.bitwise_and)
+    fill("V", R("W", S, S + 1), BIG)
+    ts(R("PM"), R("IB"), 15.0, A.is_lt)
+    fill("V", R("XG", 0, 1), BIG)
+    copy("V", R("PN"), R("PM"), -float(S + 1), float(S))
+    fill("V", R("CK", rows=32), float(DUMP))
+    bk = R("P6", 256, 384)
+    copy("S", R("Z"), R("P6", 0, 144), KE)
+    copy("S", R("BK"), bk)
+    copy("S", R("BKF"), bk, -2048.0)
+    copy("S", R("BK2", 0, 128), bk, -WC)
+    copy("S", R("BK2", 128, 256), bk, WC)
+    for k, w in enumerate((-WC, WC, -WC, 0.0, WC, 0.0)):
+        copy("S", R("SW", 8 * k, 8 * k + 8), R("P6", 256, 384, 16), w)
+    fill("S", R("BK2", 128, 256, 16), 0.0)
+    fill("V", R("NZ", B, 128), 1.0)
     for c in range(4):
-        gath("SV"[c % 2], R("W", 512 * c, 512 * c + 512), R("SKF"), R("OU", 32 * c, 32 * c + 32))
-        if c == 1:
-            ends(0, 1)
+        sk, o = R("SK", 512 * c, 512 * c + 512), R("SKF", 512 * c, 512 * c + 512)
+        if c < 2:
+            mm(R("P%d" % c), R("I1"), sk, False, True)
+            copy("S", o, R("P%d" % c), 1.0, 1.0 / 64)
+        else:
+            tt(o, sk, R("P%d" % c), A.add)
+        if c == 0:
+            turn("P7", "OT")
+        if c == 2:
+            cards16(0, 1)
+            copy("V", R("OU"), R("P7", 0, 128))
+    cardlist(0, 1)
+    for a, b, q in ((0, 66, "S"), (66, 96, "V"), (96, 128, "V")):
+        gath(q, R("W", 16 * a, 16 * b), R("SKF"), R("OU", a, b))
+        if a == 66:
+            ends_turn(0, 1)
+            mm(R("P7", 128, 416), R("BK"), R("ND"))
     needs("V", 0)
+    iota(R("RP", rows=32), [[2, 128]], 258, 0)
+    iota(R("CC", 0, 128, rows=32), [[0, 128]], int(-9.5 * WC), 0)
+    iota(R("CC", 128, 256, rows=32), [[0, 128]], int(9.5 * WC), 0)
+    ones_where(R("PV"), [[-16, 8], [1, 16]], -15, 1)
+    iota(R("CC", 128, 256, 16, rows=32), [[0, 8]], -1, 0)
+    select(R("NI"), R("ZR"), [[0, 4], [-1, 128]], A.not_equal, -1.0, 0, 1)
 
-    def consts2():
-        iota(R("RP", rows=32), [[1, 128]], 129, 0)
-        ones_where(R("I1F"), [[-1, 128]], 0, 1)
-        issue("G", lambda e: e.affine_select(ap(R("TRI")), ap(R("ONE", 0, 128)), [[-1, 128]], A.is_gt, 0.0, 0, 1), [R("ONE")], [R("TRI")])
-        iota(R("CC", 0, 128, rows=32), [[0, 128]], int(-9.5 * WC), 0)
-        iota(R("CC", 128, 256, rows=32), [[0, 128]], int(9.5 * WC), 0)
-        iota(R("CC", 128, 256, 16, rows=32), [[0, 8]], -1, 0)
-        ones_where(R("PV"), [[-16, 8], [1, 16]], -15, 1)
-        issue("G", lambda e: e.affine_select(ap(R("NI")), ap(R("ZR")), [[0, 4], [-1, 128]], A.not_equal, -1.0, 0, 1), [R("ZR")], [R("NI")])
-        ones_where(R("S0R"), [[-16, 8], [0, 16], [-1000, 2]], 1000, 1)
-        ones_where(R("E2", rows=16), [[0, 8], [-1, 16]], 0, 1)
-        ones_where(R("E3", rows=16), [[0, 8], [-1, 16], [0, 2]], 0, 1)
-        iota(R("PD"), [[0, 1]], 2050, 2)
-        iota(R("PE"), [[0, 1]], 2306, 2)
-        iota(R("O32"), [[0, 16], [-1, 2]], 1, 0)
-        iota(R("K32"), [[0, 32]], 4096, 0)
-
-    def consts3():
-        act(R("DM", 0, 256, 2), R("P0", 0, 256, 2), F.Copy, R("PD"))
-        act(R("DM", 1, 256, 2), R("P0", 1, 256, 2), F.Copy, R("PE"))
-
-    consts2()
-
-    cut, cov = TUNE["cut"], TUNE["cov"]
     for t in range(RO):
-        last, c0, c1 = t == RO - 1, 128 * t, 128 * (t % 2)
+        cov = TUNE["cov"][t]
+        first, last, c0, cut = t == 0, t == RO - 1, 128 * t, TUNE["cut"][t]
         x0 = R("XG", 1, S, 16)
 
-        def openings():
-            for k in range(2):
-                mm(R("P%d" % (2 + k)), R("I1"), R("NI"), True, False)
-            mm(R("P6", 0, 256), R("CH", c0, c0 + 128), R("S0R"), True, False)
-            if t == 0:
-                mm(R("P0", 0, 256), R("E2", rows=16), R("E3", rows=16))
-            else:
-                mm(R("P4", 0, 256), R("ONE", 0, 128, rows=1), R("CC", rows=1), True, False)
-
-        def cards(q, a):
-            gath(q, R("XG", 1 + 16 * a, 513 + 16 * a), WG, R("CU", c0 + a, c0 + a + 32))
+        def cards(q, a, b):
+            gath(q, R("XG", 1 + 16 * a, 1 + 16 * b), WG, R("CU", c0 + a, c0 + b))
 
         def sums(a):
             scan(R("EE", 16 * a, 16 * a + 512), R("XG", 16 * a, 16 * a + 512), R("D1", 16 * a, 16 * a + 512) if a < B else R("D1F"), A.add, A.min)
@@ -375,6 +373,8 @@ def rank_program(g, core, T, topo):
 
         def leave(k, a, b):
             tt(R("LF", a, b), R("P%d" % k, 0, b - a), R("CH", c0 + a, c0 + b), A.max)
+
+        def leavelist(a, b):
             copy("V", R("LL", a, b), R("LF", a, b), 1.0, -1.0)
 
         def zero(a, b):
@@ -383,96 +383,84 @@ def rank_program(g, core, T, topo):
         def mark(a, b):
             scat("V", R("FW"), R("LL", a, b), R("MK%d" % t, 0, 16 * (b - a)))
 
-        if t > 0:
-            copy("G", R("D1F", 0, 512, 16), R("ARR%d" % (t - 1)))
-        cards("V", 0)
-        cards("S", 32)
-        cards("S", 64)
-        cards("S", 96)
-        if t > 0:
-            openings()
-        sums(0)
-        wrap(0, 0, 32)
-        sums(32)
-        if not last:
-            gath("S", R("X15"), WG, SL(0, t))
-        sums(64)
-        wrap(1, 32, 96)
-        leave(0, 0, 32)
-        act(R("TH", 0, 128), x0, F.Relu, 1.0, -1.0 / 32)
-        zero(0, 32)
-        copy("G", R("TH", 128, 256), R("TH", 0, 128))
-        copy("G", R("TH", 256, 512), R("TH", 0, 256))
-        sums(96)
-        wrap(0, 96, 128)
-        if t == 0:
-            covers(t)
-        leave(1, 32, 96)
-        zero(32, 64)
-        mark(64, 96)
-        leave(0, 96, 128)
-        if t == 0:
-            coverlist(t)
-        if cut < 128:
-            zero(cut, 128)
-        if cut > 96:
-            mark(96, cut)
-        if not last:
-            for i in range(16):
+        def compare(k):
+            a, b = cov[k], cov[k + 1]
+            m, th, p = R("CM", 128 * a, 128 * b), R("TH", 0, 128 * (b - a)), R("ML", 8 * a, 8 * b)
+            issue("V", lambda e: e.tensor_tensor(ap(m), ap(WG).indirect(ap(p)), ap(th), A.is_gt), [WG, p, th], [m])
+
+        def marked(k):
+            a, b = cov[k], cov[k + 1]
+            f, w, p = R("FL", 128 * a, 128 * b), R("FW", 0, S), R("ML", 8 * a, 8 * b)
+            if ON["f%d" % k] == "S":
+                issue("S", lambda e: e.activation(ap(f), ap(w).indirect(ap(p)), F.Relu, bias=-float(t)), [w, p], [f])
+            else:
+                issue("V", lambda e: e.tensor_scalar(ap(f), ap(w).indirect(ap(p)), -float(t), 0.0, A.add, A.max), [w, p], [f])
+
+        def count(src, k):
+            u = 8 if src == "CM" else 0
+            for i in range(cov[k], cov[k + 1]):
+                w = R("SW", u, u + 16) if i < 15 else R("SW", 16 + 2 * u, 32 + 2 * u)
+                mm(R("P4", 15 - i, 256, 16), R(src, 128 * i, 128 * i + 128), w, False, src == "FL" and i == 15)
+
+        def relu(name, o, i, scale, bias):
+            if ON[name] == "S":
+                act(o, i, F.Relu, scale, bias)
+            elif bias == 1.0:
+                ts(o, i, 0.0, A.is_equal)
+            elif scale == 1.0:
+                ts(o, i, bias, A.add, 0.0, A.max)
+            else:
+                ts(o, i, scale, A.mult, 0.0, A.max)
+
+        def consts():
+            ones_where(R("S0R"), [[-16, 8], [0, 16], [-1000, 2]], 1000, 1)
+            ones_where(R("E2", rows=16), [[0, 8], [-1, 16]], 0, 1)
+            ones_where(R("E3", rows=16), [[0, 8], [-1, 16], [0, 2]], 0, 1)
+            select(R("TRI"), R("ONE", 0, 128), [[-1, 128]], A.is_gt, 0.0, 0, 1)
+            fill("G", R("NEG"), -1)
+            iota(R("PD"), [[0, 1]], 2050, 2)
+            iota(R("PE"), [[0, 1]], 2306, 2)
+            iota(R("O32"), [[0, 16], [-1, 2]], 1, 0)
+            iota(R("K32"), [[0, 32]], 4096, 0)
+            ones_where(R("I1F"), [[-1, 128]], 0, 1)
+
+        def totals(a, b):
+            for i in range(a, b):
                 mm(R("P5", 0, 128), R("I1"), R("XG", 1 + i, S, 16) if i < 15 else R("X15"), i == 0, False)
-            if t > 0:
-                mm(R("P5", B, 128), R("I1F"), R("D1F", 0, 512, 16), False, False)
-            mm(R("P5", 0, B), R("I1"), R("D1", 0, 1536, 16), False, True)
-            act(R("RF"), R("P5", 0, 128), F.Relu, -1.0)
+            if b == 16:
+                if not first:
+                    mm(R("P5", B, 128), R("I1F"), R("D1F", 0, 512, 16), False, False)
+                mm(R("P5", 0, B), R("I1"), R("D1", 0, 1536, 16), False, True)
+
+        sl, so = "SB%d" % t, R("SO%d" % min(t, 1))
+
+        def short():
             mm(R("P5", 0, 128), R("ONE", 0, 128, rows=1), R("RP", rows=1), True, False)
             mm(R("P5", 0, 128), R("BKF"), R("RF"), False, True)
-        if t == 0:
-            mm(R("P4", 0, 256), R("ONE", 0, 128, rows=1), R("CC", rows=1), True, False)
-        else:
-            mm(R("P1", 0, U), R("BKF"), R("D1F", 0, 512, 16))
 
-        def cover(a, b):
-            m, th, p = R("CM", 128 * a, 128 * b), R("TH", 0, 128 * (b - a)), R("ML", c1 + 8 * a, c1 + 8 * b)
-            issue("V", lambda e: e.tensor_tensor(ap(m), ap(WG).indirect(ap(p)), ap(th), A.is_gt), [WG, p, th], [m])
-            f, w = R("FL", 128 * a, 128 * b), R("FW", 0, S)
-            issue("S", lambda e: e.activation(ap(f), ap(w).indirect(ap(p)), F.Relu, bias=-float(t)), [w, p], [f])
-            for i in range(a, b):
-                mm(R("P4", 15 - i, 256, 16), R("CM", 128 * i, 128 * i + 128), R("SW", 8, 24) if i < 15 else R("SW", 32, 48), False, False)
-            for i in range(a, b):
-                mm(R("P4", 15 - i, 256, 16), R("FL", 128 * i, 128 * i + 128), R("SW", 0, 16) if i < 15 else R("SW", 16, 32), False, i == 15)
+        def unmet():
+            if ON["uu"] == "S":
+                act(R("UU"), R("P5", 0, 128), F.Sign, -1.0)
+            else:
+                ts(R("UU"), R("P5", 0, 128), 0.0, A.is_lt, 2.0, A.mult)
 
-        sl = "SB%d" % t
-        for k in range(len(cov) - 1):
-            cover(cov[k], cov[k + 1])
-            if k == 0 and not last:
-                act(R("ZC", 0, 128), R("P5", 0, 128), F.Relu)
-                act(R("UU"), R("ZC", 0, 128), F.Relu, -1.0, 1.0)
-            if k == 1:
-                act(R("BS"), x0, F.Relu, -65536.0, 1.0)
-                if t > 0:
-                    act(R("NZ", c0 + B, c0 + 128), R("P1", 0, U), F.Relu, -1.0, 1.0)
-                else:
-                    for u in range(RO):
-                        act(R("NZ", 128 * u, 128 * u + B), R("P6", B * u, B * u + B), F.Relu, -1.0, 1.0)
-                    keys(t)
-                mm(R("P4", 0, 256), R("BS"), R("BK2"), False, False)
-                mm(R("P4", 0, 256), R("NZ", c0, c0 + 128), R("BK2"), False, False)
-            if k == 2 and t == 0:
-                openings()
-            if k == 1 and not last:
+        def number():
+            if ON["uu"] == "S":
+                scan(R("ZC", 128, 256), R("UU"), R("ONE", 0, 128), A.add, A.add)
+            else:
                 scan(R("ZC", 128, 256), R("UU"), R("UU"), A.add, A.max)
-                vtr(R("ZT"), R("ZC"))
-                for x in range(2):
-                    for y in range(2):
-                        for u in range(2):
-                            mm(R("P5", x, 8, 2), R("Q%d%d" % (x, y)), R("ZT", 128 * u + 16 * y, 128 * u + 128, 32), y + u == 0, y + u == 2)
-            if k == 2 and not last:
-                copy("V", R("OL"), R("P5", 0, 8), 1.0, -1.0)
-        if not last:
+
+        def slots_turn():
+            for x in range(2):
+                for y in range(2):
+                    for u in range(2):
+                        mm(R("P5", x, 8, 2), Qm(x, y), R("ZT", 128 * u + 16 * y, 128 * u + 128, 32), y + u == 0, y + u == 2)
+
+        def put():
             issue("V", lambda e: e.tensor_scalar(ap(R(sl)).indirect(ap(R("OL"))), ap(R("RF")), -(1.0 + 2.0 ** -14), -MAGIC, A.mult, A.add),
                   [R("OL"), R("RF")], [R(sl)])
-            so = R("SO%d" % t)
-            copy("S", so, R(sl, 0, U), 1.0, MAGIC)
+
+        def send():
             rl = relay_of(rank)
             m, k = emask(core, rl)
             rid, pid = topo.addr(rl, core)
@@ -481,40 +469,84 @@ def rank_program(g, core, T, topo):
                   [so], [R("ARR%d" % t)], sem=("arr%d" % t, ka))
             total["out%d" % t] = k
             fill("G", R("MK%d" % (t + 1)), t + 2)
-        zero(64, 96)
-        if cut > 96:
-            zero(96, cut)
-        if t == 0:
-            lists(1, 3)
-        tt(R("KY"), R("P4", 0, 128), R("PT", c1, c1 + 128), A.min)
-        scan(R("SC"), R("P4", 128, 256), R("KY"), A.min, A.max)
-        if t == 0:
-            ends(1, 3)
-            consts3()
-        for k in range(2):
+
+        def pairs():
+            for q in range(8):
+                d, p = R("DG", 128 * q, 128 * q + 128), R("P%d" % (2 + q // 4), 128 * (q % 4), 128 * (q % 4) + 128)
+                ts(d, R("I1"), R("SC", 16 * q + 15, 16 * q + 16), A.mult)
+                mm(p, R("TRI"), d, False, q % 4 == 3 and ON["eq"] == "V")
+                if ON["eq"] == "P":
+                    mm(p, d, R("NEG"), False, q % 4 == 3)
+
+        def choices():
+            for q in range(8):
+                mm(R("P6", 32 * q, 32 * q + 32), R("DG", 128 * q, 128 * q + 128), R("O32"), False, False)
+
+        def equal(k):
+            if ON["eq"] == "P":
+                ts(R("EQ", 512 * k, 512 * k + 512), R("P%d" % (2 + k)), 0.0, A.is_equal)
             for q in range(4 * k, 4 * k + 4):
-                ts(R("DG", 128 * q, 128 * q + 128), R("I1"), R("SC", 16 * q + 15, 16 * q + 16), A.mult)
-            mm(R("P%d" % (2 + k)), R("TRI"), R("DG", 512 * k, 512 * k + 512), False, True)
-        for q in range(8):
-            mm(R("P6", 32 * q, 32 * q + 32), R("DG", 128 * q, 128 * q + 128), R("O32"), False, False)
+                if ON["eq"] == "V":
+                    ts(R("EQ", 128 * q, 128 * q + 128), R("P%d" % (2 + k), 128 * (q % 4), 128 * (q % 4) + 128), R("SC", 16 * q + 15, 16 * q + 16), A.is_equal)
+                mm(R("P6", 32 * q, 32 * q + 32), R("EQ", 128 * q, 128 * q + 128), R("K32"), False, q == 7)
+
+        def winners(k):
+            tt(R("FM", 128 * k, 128 * k + 128), R("P6", k, 256, 2), R("DM", k, 256, 2), A.min)
+            mm(R("P%d" % k, 0, 8), R("FM", 128 * k, 128 * k + 128), R("B16"))
+
+        gs = TUNE["gs"]
+        every = {
+            "g0": lambda: cards("V", 0, 32), "g1": lambda: cards("S", 32, 64), "g2": lambda: cards("S", 64, 96),
+            "g3": lambda: cards("S", 96, gs), "g4": lambda: cards("V", gs, 128) if gs < 128 else None,
+            "s0": lambda: sums(0), "s1": lambda: sums(32), "s2": lambda: sums(64), "s3": lambda: sums(96),
+            "w0": lambda: wrap(0, 0, 32), "w1": lambda: wrap(1, 32, 96), "w2": lambda: wrap(0, 96, 128),
+            "l0": lambda: leave(0, 0, 32), "l1": lambda: leave(1, 32, 96), "l2": lambda: leave(0, 96, 128),
+            "L0": lambda: leavelist(0, 32), "L1": lambda: leavelist(32, 96), "L2": lambda: leavelist(96, 128),
+            "z0": lambda: zero(0, 32), "z1": lambda: zero(32, 64), "z2": lambda: zero(cut, 128),
+            "m1": lambda: mark(64, 96), "m2": lambda: mark(96, cut), "Z1": lambda: zero(64, 96), "Z2": lambda: zero(96, cut),
+            "th": lambda: relu("th", R("TH", 0, 128), x0, 1.0, -1.0 / 32), "bs": lambda: relu("bs", R("BS"), x0, -65536.0, 1.0),
+            "th2": lambda: copy("G", R("TH", 128, 256), R("TH", 0, 128)), "th4": lambda: copy("G", R("TH", 256, 512), R("TH", 0, 256)),
+            "knz": lambda: mm(R("P4", 0, 256), R("NZ", c0, c0 + 128), R("BK2"), False, False),
+            "kbs": lambda: mm(R("P4", 0, 256), R("BS"), R("BK2"), False, False),
+            "key": lambda: tt(R("KY"), R("P4", 0, 128), R("PT"), A.min),
+            "pick": lambda: scan(R("SC"), R("P4", 128, 256), R("KY"), A.min, A.max),
+            "pairs": pairs, "choices": choices, "e0": lambda: equal(0), "e1": lambda: equal(1),
+            "win0": lambda: winners(0), "win1": lambda: winners(1),
+            "u0": lambda: copy("V", R("LU", 0, 8), R("P0", 0, 8), 1.0, -1.0), "u1": lambda: copy("V", R("LU", 8, 16), R("P1", 0, 8), 1.0, -1.0),
+            "take": lambda: gath(ON["take"], R("VV", 128, 256), R("W", 0, WN), R("LU", 0, 8)),
+            "move": lambda: scat("V", R("W", 0, WN), R("LU"), R("VV"))}
+        for k in range(len(cov) - 1):
+            every.update({"c%d" % k: lambda k=k: compare(k), "f%d" % k: lambda k=k: marked(k),
+                          "nc%d" % k: lambda k=k: count("CM", k), "nf%d" % k: lambda k=k: count("FL", k)})
+        if first:
+            every.update({
+                "ends0": lambda: ends(0, 1), "nz0": lambda: noneed(0), "nz1": lambda: noneed(1), "nz2": lambda: noneed(2), "consts": consts,
+                "cov0": lambda: covers(0), "vm0": lambda: vtr(R("MT"), R("MH")), "turn0": lambda: covers_turn("P6"), "ml0": coverlist,
+                "pt0": lambda: keys("P6"), "oc0": open_counts, "op0": open_pairs, "ol0": lambda: open_lists(0),
+                "ch": lambda: cards16(1, 3), "endt": lambda: ends_turn(1, 3), "ends": lambda: ends(1, 3), "cu": lambda: cardlist(1, 3),
+                "dmm": lambda: mm(R("P0", 0, 256), R("E2", rows=16), R("E3", rows=16)),
+                "dm0": lambda: act(R("DM", 0, 256, 2), R("P0", 0, 256, 2), F.Copy, R("PD")),
+                "dm1": lambda: act(R("DM", 1, 256, 2), R("P0", 1, 256, 2), F.Copy, R("PE")),
+                "b16": lambda: copy("S", R("B16"), R("BK", 0, 128, 16)),
+                "wz": lambda: fill("S", R("W", S + 1, WN), 0.0), "vz": lambda: fill("S", R("VV", 0, 128), 0.0)})
+        else:
+            every.update({
+                "arr": lambda: copy("G", R("D1F", 0, 512, 16), R("ARR%d" % (t - 1))), "ml": coverlist, "pt": lambda: keys("P5"),
+                "nzm": lambda: mm(R("P7", 0, U), R("BKF"), R("D1F", 0, 512, 16)),
+                "nz": lambda: relu("nz", R("NZ", c0 + B, c0 + 128), R("P7", 0, U), -1.0, 1.0)})
         if not last:
-            covers(t + 1, False)
-        for q in range(8):
-            ts(R("EQ", 128 * q, 128 * q + 128), R("P%d" % (2 + q // 4), 128 * (q % 4), 128 * (q % 4) + 128), R("SC", 16 * q + 15, 16 * q + 16), A.is_equal)
-            mm(R("P6", 32 * q, 32 * q + 32), R("EQ", 128 * q, 128 * q + 128), R("K32"), False, q == 7)
-        if not last:
-            needs("S", t + 1)
-        tt(R("FM"), R("P6", 0, 256), R("DM"), A.min)
-        for k in range(2):
-            mm(R("P4", 8 * k, 8 * k + 8), R("FM", k, 256, 2), R("B16"))
-        if not last:
-            turn("P7", "MT", 0)
-        copy("V", R("LU"), R("P4", 0, 16), 1.0, -1.0)
-        gath("V", R("VV", 128, 256), R("W", 0, WN), R("LU", 0, 8))
-        scat("V", R("W", 0, WN), R("LU"), R("VV"))
-        if not last:
-            coverlist(t + 1)
-            keys(t + 1)
+            every.update({
+                "x15": lambda: gath(ON["x15"], R("X15"), WG, SL(0, t)), "tot0": lambda: totals(0, 8), "tot1": lambda: totals(8, 16),
+                "rf": lambda: relu("rf", R("RF"), R("P5", 0, 128), -1.0, 0.0), "short": short, "uu": unmet,
+                "zc": lambda: relu("zc", R("ZC", 0, 128), R("P5", 0, 128), 1.0, 0.0),
+                "num": number, "vz2": lambda: vtr(R("ZT"), R("ZC")), "turnz": slots_turn,
+                "ol": lambda: copy("V", R("OL"), R("P5", 0, 8), 0.5, -1.0), "sb": lambda: fill("S", R(sl, 0, U), -MAGIC), "put": put,
+                "so": lambda: copy(ON["so"], so, R(sl, 0, U), 1.0, MAGIC), "send": send, "needs": lambda: needs("S", t + 1),
+                "cov": lambda: covers(t + 1), "vm": lambda: vtr(R("MT"), R("MH")), "turn": lambda: covers_turn("P5"),
+                "op": open_pairs, "oc": open_counts, "olist": lambda: open_lists(t + 1)})
+        for name in ORDER:
+            if name in every:
+                every[name]()
 
     dma("Y", T.YC[:, :], T.W[0:128:16, 0:S], [R("W", 0, S)], [R("YC")])
     copy("V", R("YI"), R("YC"), 65536.0)

@@ -4,7 +4,7 @@ BF, FP, F16, I32, U16 = "bfloat16", "float32", "float16", "int32", "uint16"
 S, L, B, U, RO = 2048, 128, 96, 32, 3
 BIG = 4096.0
 DUMP = 2064
-WW, WN = 4112, 2560
+WW, WN = 4128, 2560
 KE = 8192.0
 WC = 4096.0
 MAGIC = 12582912.0
@@ -17,21 +17,19 @@ for _n, _w, _d in [
         ("ZR", 512, FP), ("MK0", 512, BF), ("MK1", 512, BF), ("MK2", 512, BF), ("TH", 512, BF), ("RH", 1024, F16),
         ("OH", 128, F16), ("OT", 128, F16), ("OU", 128, U16), ("CU", 384, U16), ("CH", 384, F16), ("CT", 384, F16),
         ("SL", 48, U16), ("MH", 128, F16), ("MT", 128, F16), ("ML", 128, U16), ("PT", 128, FP), ("NZ", 384, BF), ("BS", 128, BF),
-        ("SO0", U, FP), ("SO1", U, FP), ("SN", U, FP), ("RS", 128, FP),
-        ("LF", 128, FP), ("LL", 128, U16), ("X15", 128, BF), ("KY", 128, FP), ("SC", 128, FP), ("DG", 1024, F16), ("EQ", 1024, BF),
-        ("FM", 256, F16), ("LU", 16, U16), ("VV", 256, FP), ("RF", 128, FP), ("ZC", 256, BF), ("ZT", 256, BF), ("UU", 128, BF),
-        ("OL", 8, U16), ("SB0", 512, FP), ("SB1", 512, FP), ("ARR0", U, FP), ("ARR1", U, FP), ("RB0", U, FP), ("RB1", U, FP),
-        ("YC", 128, FP), ("YI", 128, I32), ("YJ", 128, I32), ("YO", 128, FP),
-        ("WX", 256, FP), ("NI", 512, BF), ("BK2", 256, BF), ("S0R", 256, BF), ("DM", 256, FP),
-        ("I1F", 128, FP), ("BKF", 128, FP), ("CC", 256, BF), ("ONE", 256, BF), ("E3", 256, BF)]:
+        ("LL", 128, U16), ("X15", 128, BF), ("KY", 128, FP), ("SC", 128, FP), ("DG", 1024, F16), ("EQ", 1024, BF),
+        ("FM", 256, F16), ("LU", 16, U16), ("VV", 256, FP), ("RF", 128, FP), ("RB", 128, BF), ("ZC", 256, BF), ("ZT", 256, BF), ("UU", 128, BF),
+        ("OL", 8, U16), ("SB0", 512, FP), ("SB1", 512, FP), ("SO0", U, FP), ("SO1", U, FP), ("RB0", U, FP), ("RB1", U, FP),
+        ("ARR0", U, FP), ("ARR1", U, FP), ("AB", U, BF), ("YC", 128, FP), ("YI", 128, I32), ("YJ", 128, I32), ("YO", 128, FP),
+        ("WX", 256, FP), ("BK2", 256, BF), ("S0R", 256, BF), ("DM", 256, FP), ("I1F", 128, FP), ("ONE", 256, BF), ("E3", 256, BF)]:
     SCRATCH[_n] = ("sbuf", [128, _w], _d)
 PARTS = {}
 for _b, _d, _l in [
         ("GI", I32, [("IP", 8), ("IA", 8), ("IB", 8)]),
         ("GF", FP, [("PX", 8), ("PY", 8), ("PM", 8), ("PN", 8), ("PD", 8), ("PE", 8)]),
-        ("GB", BF, [("I1", 128), ("Z", 144), ("BK", 128), ("SW", 48), ("RP", 128), ("PV", 128), ("TRI", 128), ("Q00", 128), ("Q01", 128),
-                    ("Q10", 128), ("Q11", 128), ("B16", 16), ("O32", 32), ("K32", 32), ("C16", 128), ("E1", 128), ("E2", 128), ("E4", 144),
-                    ("CK", 64), ("NEG", 128)])]:
+        ("GB", BF, [("I1", 128), ("Z", 144), ("BK", 128), ("BKF", 128), ("SW", 48), ("RP", 128), ("PV", 128), ("TRI", 128), ("Q00", 128),
+                    ("Q01", 128), ("Q10", 128), ("Q11", 128), ("B16", 16), ("O32", 32), ("K32", 32), ("C16", 128), ("E1", 128), ("E2", 128),
+                    ("E4", 144), ("CK", 64)])]:
     _o = 0
     for _n, _w in _l:
         PARTS[_n] = (_b, _o, 1 if _b in ("GI", "GF") else {"B16": 8}.get(_n, _w))
@@ -40,13 +38,21 @@ for _b, _d, _l in [
 for _k in range(8):
     SCRATCH["P%d" % _k] = ("psum", [128, 512], FP)
 SEMAPHORES = ["cV", "cS", "cP", "cG"] + ["d%d" % k for k in range(12)] + ["arr0", "arr1", "rin0", "rin1", "out0", "out1"]
-TUNE = {"cov": [[0, 4, 8, 12, 16], [0, 4, 8, 12, 16], [0, 4, 8, 12, 15, 16]], "cut": [112, 116, 114], "gs": 128}
-ON = {"x15": "V", "th": "V", "bs": "V", "nz": "V", "rf": "S", "uu": "S", "zc": "S", "so": "V", "take": "V", "eq": "V",
-      "f0": "S", "f1": "S", "f2": "S", "f3": "S", "f4": "S"}
-ORDER = """g0 b16 g1 g2 g4 arr ends0 g3 s0 x15 s1 s2 w0 nz0 l0 ch ml L0 s3 w1 oc0 l1 th cov0 L1 bs vm0 m1 w2 pt l2 nzm z0 turn0 z1 tot0 tot1
-nz th2 ml0 sb L2 z2 th4 pt0 m2 c0 f0 rf c1 knz kbs nf0 short nc0 c2 nz1 f1 uu num zc consts nc1 vz2 f2 c3 c4 nf1 nc2 f3 turnz dmm nz2 f4
-nf2 Z1 ol nc3 dm0 nf3 Z2 dm1 endt put op0 nc4 nf4 key wz so pick ends pairs ol0 e0 choices e1 cov win0 win1 u0 vz olist u1 send take cu
-move needs op vm oc turn""".split()
+
+TUNE = {"state": [("S", 0, 72), ("V", 72, 100), ("V", 100, 128)],
+        "gath": [{0: ("V", 0, 16), 1: ("S", 16, 32), 2: ("S", 32, 64), 3: ("S", 64, 76), 4: ("V", 76, 96)},
+                 {0: ("V", 0, 16), 1: ("S", 16, 32), 2: ("S", 32, 64), 3: ("S", 64, 96), 4: ("V", 96, 128)}],
+        "cov": [[0, 4, 8, 12, 16], [0, 4, 8, 12, 16], [0, 4, 8, 12, 15, 16]], "marks": [(58, 96), (64, 116), (64, 114)]}
+ON = {"big": "V", "needs0": "V", "d10": "V", "d11": "V", "d12": "V", "x15": "V", "th": "V", "nz": "V", "rf": "S", "zc": "S", "so": "V",
+      "rb": "G"}
+ORDER = """wx zr one ip d10 rh0 ia E1 c16 rh1 wbig py E4 ramp0 rh2 E3 px d12 ramp2 E2 blocks q11 ib oh i1 q00 ot d1f sw1 pm ramp3 pv sw0
+bk2b q10 bkf q01 ramp1 pn Z sk0 turno d11 xbig tab2 ou tab0 bk tab3 ck sk1 fw ch0 s0r bk2c bk2a tab1 mk b16 W0 W1 ow01 ow00 endt0 nd
+needs0 arr W2 rff cu0
+g1 g2 ends0 g3 g0 nz0 scf x15 s0 g4 pt w0 s1 l0 s2 w1 ml th arb z0 s3 cov0 sb l1 bs tot0 z1 th2 w2 vm0 m1 l2 rp tot2 turn0 th4 tot1
+ml0 nzm tot3 nz kbs m2 z2 pt0
+rf f1 ol0 f0 c1 dmm rb f2 c0 c2 c3 ch c4 short knz consts nf0 nf1 f3 nc0 nc2 uu nc1 f4 nf2 nz1 nc3 zc nf3 nz2 nc4 Z1 dm0 endt nf4
+num wz key vz2 pick turnz cu pairs ol e0 ow0 choices e1 dm1 put win0 so ends win1 send cov olist needs u0 Z2 u1 take vm vz move ow1 ow2
+turn""".split()
 
 
 def rank_program(g, core, T, topo):
@@ -150,7 +156,7 @@ def rank_program(g, core, T, topo):
         if q == "S":
             act(o, i, F.Copy if bias == 0.0 else F.Identity, scale, bias)
         elif q == "G":
-            issue(q, lambda e: e.affine_select(ap(o), ap(i), [[0, width(o)]], A.is_ge, 0.0, 0, 0), [i], [o])
+            select(o, i, [[0, width(o)]], A.is_ge, 0.0, 0, 0)
         elif scale == 1.0 and bias == 0.0:
             issue(q, lambda e: e.tensor_copy(ap(o), ap(i)), [i], [o])
         else:
@@ -180,6 +186,16 @@ def rank_program(g, core, T, topo):
             copy(q, o, R("ZR", 0, width(o), rows=o[4]), 1.0, v)
         else:
             iota(o, [[0, width(o)]], int(v), 0)
+
+    def relu(q, o, i, scale, bias):
+        if q == "S":
+            act(o, i, F.Relu, scale, bias)
+        elif bias == 1.0:
+            ts(o, i, 0.0, A.is_equal)
+        elif scale == 1.0:
+            ts(o, i, bias, A.add, 0.0, A.max)
+        else:
+            ts(o, i, scale, A.mult, 0.0, A.max)
 
     def scan(o, a, b, op0, op1):
         issue("V", lambda e: e.tensor_tensor_scan(ap(o), ap(a), ap(b), 0.0, op0, op1), [a, b], [o])
@@ -213,25 +229,25 @@ def rank_program(g, core, T, topo):
     def Qm(x, y):
         return R("Q%d%d" % (x, y))
 
-    def turn(bank, src):
-        for b in range(4):
+    def turn(bank, src, nb=4):
+        for b in range(nb):
             for x in range(2):
                 for y in range(2):
-                    mm(R(bank, 2 * b + x, 128, 8), Qm(x, y), R(src, 32 * b + 16 * y, 32 * b + 16 * y + 16), y == 0, y == 1)
+                    mm(R(bank, 2 * b + x, 32 * nb, 2 * nb), Qm(x, y), R(src, 32 * b + 16 * y, 32 * b + 16 * y + 16), y == 0, y == 1)
 
     def Z(i):
         return R("Z", 15 - i, 143 - i)
 
     WG, WS, D0 = R("W", 0, S + 1), R("W"), R("WX", 64, 192)
+    WRAPS = ((2, 0, 32), (3, 32, 96), (1, 96, 128))
 
     dma("Y", T.OC[:, :], T.occ[:, :], [], [R("OC")])
-    for c in range(4):
-        dma("SY"[c % 2], T.SK[:, 512 * c:512 * c + 512], T.skill[:, 512 * c:512 * c + 512], [], [R("SK", 512 * c, 512 * c + 512)])
-        if c == 1:
-            dma("Y", T.CD[:, 0:128], T.cards[:, 0:128], [], [R("CD", 0, 128)])
+    for q, a, b in (("S", 0, 1024), ("Y", 1024, 1536), ("Y", 1536, S)):
+        dma(q, T.SK[:, a:b], T.skill[:, a:b], [], [R("SK", a, b)])
+    dma("Y", T.CD[:, 0:128], T.cards[:, 0:128], [], [R("CD", 0, 128)])
     dma("Y", T.ND[:, :], T.need[:, :], [], [R("ND")])
-    dma("Y", T.CD[:, 128:384], T.cards[:, 128:384], [], [R("CD", 128, 384)])
     dma("Y", T.CV[:, :], T.cover[:, :], [], [R("CV")])
+    dma("Y", T.CD[:, 128:384], T.cards[:, 128:384], [], [R("CD", 128, 384)])
 
     def cards16(a, b):
         copy("V", R("CH", 128 * a, 128 * b), R("CD", 128 * a, 128 * b), 1.0, 1.0)
@@ -256,12 +272,12 @@ def rank_program(g, core, T, topo):
     def covers(t):
         issue("V", lambda e: e.tensor_scalar(ap(R("MH")), ap(R("CV")).indirect(ap(SL(1, t))), 1.0, None, A.add), [R("CV"), SL(1, t)], [R("MH")])
 
-    def covers_turn(bank):
-        turn("P7", "MT")
+    def covers_turn(bank, nb=4):
+        turn("P7", "MT", nb)
         mm(R(bank, 128, 256), R("MH"), R("PV"))
 
-    def coverlist():
-        copy("V", R("ML"), R("P7", 0, 128), 1.0, -1.0)
+    def coverlist(nl=L):
+        copy("V", R("ML", 0, nl), R("P7", 0, nl), 1.0, -1.0)
 
     def keys(bank):
         copy("S", R("PT"), R(bank, 128, 256))
@@ -272,91 +288,98 @@ def rank_program(g, core, T, topo):
     def noneed(t):
         act(R("NZ", 128 * t, 128 * t + B), R("P7", 128 + B * t, 128 + B * t + B), F.Relu, -1.0, 1.0)
 
-    def open_pairs():
-        for k in range(2):
-            mm(R("P%d" % (2 + k)), R("I1"), R("NI"), True, False)
+    def open_wrap(t, k, a, b):
+        p = R("P%d" % k, 0, b - a)
+        mm(p, R("I1"), R("CH", 128 * t + a, 128 * t + b), True, False)
+        mm(p, R("ONE", 0, 128, rows=1), R("CK", 0, b - a, rows=1), False, False)
 
     def open_lists(t):
         mm(R("P6", 0, 256), R("CH", 128 * t, 128 * t + 128), R("S0R"), True, False)
 
-    def open_counts():
-        mm(R("P4", 0, 256), R("ONE", 0, 128, rows=1), R("CC", rows=1), True, False)
-
-    iota(R("WX"), [[1, 256]], -64, -1)
-    iota(R("IP"), [[0, 1]], 0, 1)
-    fill("V", R("ONE"), 1.0)
-    fill("V", R("C16", rows=32), 2.0 ** -16)
-    fill("V", R("ZR"), 0.0)
-    act(R("D1F"), R("ZR"), F.Silu)
-    ones_where(R("E1", rows=8), [[-1, 8], [0, 16]], 0, 1)
-    ones_where(R("E4", rows=8), [[1, 144]], -15, -16)
-    fill("G", R("FW", 0, S), 0)
-    fill("G", R("MK0"), 1)
-    copy("V", R("RH", 0, 256, rows=1), R("WX", rows=1), -1.0, 959.0)
-    ts(R("IA"), R("IP"), 4, A.arith_shift_right, 1, A.bitwise_and)
-    copy("V", R("RH", 256, 512, rows=1), R("RH", 0, 256, rows=1), 1.0, -256.0)
-    copy("V", R("PX"), R("IA"))
-    copy("V", R("PY"), R("IA"), -1.0, 1.0)
-    copy("V", R("RH", 512, 1024, rows=1), R("RH", 0, 512, rows=1), 1.0, -512.0)
-    ts(R("Q11"), D0, 0.0, A.is_equal, R("PX"), A.mult)
-    ts(R("Q10"), D0, -16.0, A.is_equal, R("PX"), A.mult)
-    ts(R("Q00"), D0, 0.0, A.is_equal, R("PY"), A.mult)
-    ts(R("Q01"), D0, 16.0, A.is_equal, R("PY"), A.mult)
-    copy("V", R("OH"), R("OC"))
-    ts(R("I1"), D0, 0.0, A.is_equal)
-    vtr(R("OT"), R("OH"))
-    for c in (0, 2, 1, 3):
-        mm(R("P%d" % c), R("C16", rows=1), R("RH", 512 * (c % 2), 512 * (c % 2) + 512, rows=1), True, c > 1)
-        if c == 2:
-            mm(R("P6", 0, 144), R("E1", rows=8), R("E4", rows=8))
-            mm(R("P6", 256, 384), R("E1", rows=8), R("E1", rows=8))
-    fill("V", R("D1"), 0.0)
-    ts(R("IB"), R("IP"), 15, A.bitwise_and)
-    fill("V", R("W", S, S + 1), BIG)
-    ts(R("PM"), R("IB"), 15.0, A.is_lt)
-    fill("V", R("XG", 0, 1), BIG)
-    copy("V", R("PN"), R("PM"), -float(S + 1), float(S))
-    fill("V", R("CK", rows=32), float(DUMP))
     bk = R("P6", 256, 384)
-    copy("S", R("Z"), R("P6", 0, 144), KE)
-    copy("S", R("BK"), bk)
-    copy("S", R("BKF"), bk, -2048.0)
-    copy("S", R("BK2", 0, 128), bk, -WC)
-    copy("S", R("BK2", 128, 256), bk, WC)
-    for k, w in enumerate((-WC, WC, -WC, 0.0, WC, 0.0)):
-        copy("S", R("SW", 8 * k, 8 * k + 8), R("P6", 256, 384, 16), w)
-    fill("S", R("BK2", 128, 256, 16), 0.0)
-    fill("V", R("NZ", B, 128), 1.0)
-    for c in range(4):
+
+    def ramp(c):
+        mm(R("P%d" % c), R("C16", rows=1), R("RH", 512 * (c % 2), 512 * (c % 2) + 512, rows=1), True, c > 1)
+
+    def table(c):
         sk, o = R("SK", 512 * c, 512 * c + 512), R("SKF", 512 * c, 512 * c + 512)
         if c < 2:
-            mm(R("P%d" % c), R("I1"), sk, False, True)
             copy("S", o, R("P%d" % c), 1.0, 1.0 / 64)
         else:
             tt(o, sk, R("P%d" % c), A.add)
-        if c == 0:
-            turn("P7", "OT")
-        if c == 2:
-            cards16(0, 1)
-            copy("V", R("OU"), R("P7", 0, 128))
-    cardlist(0, 1)
-    for a, b, q in ((0, 66, "S"), (66, 96, "V"), (96, 128, "V")):
-        gath(q, R("W", 16 * a, 16 * b), R("SKF"), R("OU", a, b))
-        if a == 66:
-            ends_turn(0, 1)
-            mm(R("P7", 128, 416), R("BK"), R("ND"))
-    needs("V", 0)
-    iota(R("RP", rows=32), [[2, 128]], 258, 0)
-    iota(R("CC", 0, 128, rows=32), [[0, 128]], int(-9.5 * WC), 0)
-    iota(R("CC", 128, 256, rows=32), [[0, 128]], int(9.5 * WC), 0)
-    ones_where(R("PV"), [[-16, 8], [1, 16]], -15, 1)
-    iota(R("CC", 128, 256, 16, rows=32), [[0, 8]], -1, 0)
-    select(R("NI"), R("ZR"), [[0, 4], [-1, 128]], A.not_equal, -1.0, 0, 1)
+
+    def blocks():
+        mm(R("P6", 0, 144), R("E1", rows=8), R("E4", rows=8))
+        mm(bk, R("E1", rows=8), R("E1", rows=8))
+
+    def signs(a, b):
+        for k in range(a, b):
+            copy("S", R("SW", 8 * k, 8 * k + 8), R("P6", 256, 384, 16), (-WC, WC, -WC, 0.0, WC, 0.0)[k])
+
+    def sel(x, y):
+        ts(Qm(x, y), D0, 16.0 * (y - x), A.is_equal, R("PX" if x else "PY"), A.mult)
+
+    def consts():
+        select(R("TRI"), R("ONE", 0, 128), [[-1, 128]], A.is_gt, -1.0, 0, 1)
+        iota(R("PD"), [[0, 1]], 2050, 2)
+        iota(R("PE"), [[0, 1]], 2306, 2)
+        iota(R("O32"), [[0, 16], [-1, 2]], 1, 0)
+        iota(R("K32"), [[0, 32]], 4096, 0)
+        ones_where(R("I1F"), [[-1, 128]], 0, 1)
+
+    begin = {
+        "wx": lambda: iota(R("WX"), [[1, 256]], -64, -1),
+        "ip": lambda: iota(R("IP"), [[0, 1]], 0, 1), "one": lambda: fill("V", R("ONE"), 1.0),
+        "c16": lambda: fill("V", R("C16", rows=32), 2.0 ** -16), "zr": lambda: fill("V", R("ZR"), 0.0),
+        "d1f": lambda: act(R("D1F"), R("ZR"), F.Silu),
+        "E1": lambda: ones_where(R("E1", rows=8), [[-1, 8], [0, 16]], 0, 1), "E4": lambda: ones_where(R("E4", rows=8), [[1, 144]], -15, -16),
+        "fw": lambda: fill("G", R("FW", 0, S), 0), "mk": lambda: fill("G", R("MK0"), 1),
+        "rh0": lambda: copy("V", R("RH", 0, 256, rows=1), R("WX", rows=1), -1.0, 959.0),
+        "rh1": lambda: copy("V", R("RH", 256, 512, rows=1), R("RH", 0, 256, rows=1), 1.0, -256.0),
+        "rh2": lambda: copy("V", R("RH", 512, 1024, rows=1), R("RH", 0, 512, rows=1), 1.0, -512.0),
+        "ia": lambda: ts(R("IA"), R("IP"), 4, A.arith_shift_right, 1, A.bitwise_and),
+        "px": lambda: copy("V", R("PX"), R("IA")), "py": lambda: copy("V", R("PY"), R("IA"), -1.0, 1.0),
+        "q11": lambda: sel(1, 1), "q10": lambda: sel(1, 0), "q00": lambda: sel(0, 0), "q01": lambda: sel(0, 1),
+        "oh": lambda: copy("V", R("OH"), R("OC")), "i1": lambda: ts(R("I1"), D0, 0.0, A.is_equal), "ot": lambda: vtr(R("OT"), R("OH")),
+        "blocks": blocks, "turno": lambda: turn("P7", "OT"), "ou": lambda: copy("V", R("OU"), R("P7", 0, 128)),
+        "ib": lambda: ts(R("IB"), R("IP"), 15, A.bitwise_and), "pm": lambda: ts(R("PM"), R("IB"), 15.0, A.is_lt),
+        "pn": lambda: copy("V", R("PN"), R("PM"), -float(S + 1), float(S)),
+        "wbig": lambda: fill(ON["big"], R("W", S, S + 1), BIG), "xbig": lambda: fill(ON["big"], R("XG", 0, 1), BIG),
+        "ck": lambda: fill(ON["big"], R("CK", rows=32), float(DUMP)),
+        "Z": lambda: copy("S", R("Z"), R("P6", 0, 144), KE), "bk": lambda: copy("S", R("BK"), bk),
+        "bkf": lambda: copy("S", R("BKF"), bk, -2048.0), "bk2a": lambda: copy("S", R("BK2", 0, 128), bk, -WC),
+        "bk2b": lambda: copy("S", R("BK2", 128, 256), bk, WC), "bk2c": lambda: fill("S", R("BK2", 128, 256, 16), 0.0),
+        "sw0": lambda: signs(0, 3), "sw1": lambda: signs(3, 6),
+        "ch0": lambda: cards16(0, 1), "needs0": lambda: needs(ON["needs0"], 0), "cu0": lambda: cardlist(0, 1), "endt0": lambda: ends_turn(0, 1),
+        "nd": lambda: mm(R("P7", 128, 416), R("BK"), R("ND")),
+        "rp": lambda: iota(R("RP", rows=32), [[2, 128]], 258, 0), "pv": lambda: ones_where(R("PV"), [[-16, 8], [1, 16]], -15, 1),
+        "s0r": lambda: ones_where(R("S0R"), [[-16, 8], [0, 16], [-1000, 2]], 1000, 1),
+        "E2": lambda: ones_where(R("E2", rows=16), [[0, 8], [-1, 16]], 0, 1),
+        "E3": lambda: ones_where(R("E3", rows=16), [[0, 8], [-1, 16], [0, 2]], 0, 1),
+        "ends0": lambda: ends(0, 1), "nz0": lambda: noneed(0), "nz1": lambda: noneed(1), "nz2": lambda: noneed(2), "consts": consts,
+        "cov0": lambda: covers(0), "vm0": lambda: vtr(R("MT"), R("MH")), "turn0": lambda: covers_turn("P6", 3), "ml0": lambda: coverlist(B),
+        "scf": lambda: fill("S", R("SC"), 0.0), "rff": lambda: fill("S", R("RF", B, 128), 0.0),
+        "pt0": lambda: keys("P6"), "ol0": lambda: open_lists(0),
+        "ch": lambda: cards16(1, 3), "endt": lambda: ends_turn(1, 3), "ends": lambda: ends(1, 3), "cu": lambda: cardlist(1, 3),
+        "dmm": lambda: mm(R("P0", 0, 256), R("E2", rows=16), R("E3", rows=16)),
+        "dm0": lambda: act(R("DM", 0, 256, 2), R("P0", 0, 256, 2), F.Copy, R("PD")),
+        "dm1": lambda: act(R("DM", 1, 256, 2), R("P0", 1, 256, 2), F.Copy, R("PE")),
+        "b16": lambda: copy("S", R("B16"), R("BK", 0, 128, 16)),
+        "wz": lambda: fill("S", R("W", S + 1, WN), 0.0), "vz": lambda: fill("S", R("VV", 0, 128), 0.0)}
+    for c in range(4):
+        begin.update({"ramp%d" % c: lambda c=c: ramp(c), "tab%d" % c: lambda c=c: table(c)})
+    for c in range(3):
+        begin.update({"d1%d" % c: lambda c=c: fill(ON["d1%d" % c], R("D1", 512 * c, 512 * c + 512), 0.0),
+                      "W%d" % c: lambda p=TUNE["state"][c]: gath(p[0], R("W", 16 * p[1], 16 * p[2]), R("SKF"), R("OU", p[1], p[2]))})
+    for c in range(2):
+        begin["ow0%d" % c] = lambda c=c: open_wrap(0, *WRAPS[c])
+        begin["sk%d" % c] = lambda c=c: mm(R("P%d" % c), R("I1"), R("SK", 512 * c, 512 * c + 512), False, True)
 
     for t in range(RO):
-        cov = TUNE["cov"][t]
-        first, last, c0, cut = t == 0, t == RO - 1, 128 * t, TUNE["cut"][t]
-        x0 = R("XG", 1, S, 16)
+        first, last, c0, cov = t == 0, t == RO - 1, 128 * t, TUNE["cov"][t]
+        nl = B if first else L
+        ma, cut = TUNE["marks"][t]
+        x0, sl, so = R("XG", 1, 16 * nl, 16), "SB%d" % t, R("SO%d" % min(t, 1))
 
         def cards(q, a, b):
             gath(q, R("XG", 1 + 16 * a, 1 + 16 * b), WG, R("CU", c0 + a, c0 + b))
@@ -366,16 +389,11 @@ def rank_program(g, core, T, topo):
 
         def wrap(k, a, b):
             p = R("P%d" % k, 0, b - a)
-            mm(p, R("I1"), R("CH", c0 + a, c0 + b), True, False)
-            mm(p, R("ONE", 0, 128, rows=1), R("CK", 0, b - a, rows=1), False, False)
             for i in range(16):
                 mm(p, Z(i), R("EE", 16 * a + i, 16 * b, 16), False, i == 15)
 
         def leave(k, a, b):
-            tt(R("LF", a, b), R("P%d" % k, 0, b - a), R("CH", c0 + a, c0 + b), A.max)
-
-        def leavelist(a, b):
-            copy("V", R("LL", a, b), R("LF", a, b), 1.0, -1.0)
+            tt(R("LL", a, b), R("P%d" % k, 0, b - a), R("CD", c0 + a, c0 + b), A.max)
 
         def zero(a, b):
             scat("S", WS, R("LL", a, b), R("ZR", 0, 16 * (b - a)))
@@ -385,70 +403,31 @@ def rank_program(g, core, T, topo):
 
         def compare(k):
             a, b = cov[k], cov[k + 1]
-            m, th, p = R("CM", 128 * a, 128 * b), R("TH", 0, 128 * (b - a)), R("ML", 8 * a, 8 * b)
+            m, th, p = R("CM", nl * a, nl * b), R("TH", 0, nl * (b - a)), R("ML", nl // 16 * a, nl // 16 * b)
             issue("V", lambda e: e.tensor_tensor(ap(m), ap(WG).indirect(ap(p)), ap(th), A.is_gt), [WG, p, th], [m])
 
         def marked(k):
             a, b = cov[k], cov[k + 1]
-            f, w, p = R("FL", 128 * a, 128 * b), R("FW", 0, S), R("ML", 8 * a, 8 * b)
-            if ON["f%d" % k] == "S":
-                issue("S", lambda e: e.activation(ap(f), ap(w).indirect(ap(p)), F.Relu, bias=-float(t)), [w, p], [f])
-            else:
-                issue("V", lambda e: e.tensor_scalar(ap(f), ap(w).indirect(ap(p)), -float(t), 0.0, A.add, A.max), [w, p], [f])
+            f, w, p = R("FL", nl * a, nl * b), R("FW", 0, S), R("ML", nl // 16 * a, nl // 16 * b)
+            issue("S", lambda e: e.activation(ap(f), ap(w).indirect(ap(p)), F.Relu, bias=-float(t)), [w, p], [f])
 
         def count(src, k):
             u = 8 if src == "CM" else 0
             for i in range(cov[k], cov[k + 1]):
                 w = R("SW", u, u + 16) if i < 15 else R("SW", 16 + 2 * u, 32 + 2 * u)
-                mm(R("P4", 15 - i, 256, 16), R(src, 128 * i, 128 * i + 128), w, False, src == "FL" and i == 15)
-
-        def relu(name, o, i, scale, bias):
-            if ON[name] == "S":
-                act(o, i, F.Relu, scale, bias)
-            elif bias == 1.0:
-                ts(o, i, 0.0, A.is_equal)
-            elif scale == 1.0:
-                ts(o, i, bias, A.add, 0.0, A.max)
-            else:
-                ts(o, i, scale, A.mult, 0.0, A.max)
-
-        def consts():
-            ones_where(R("S0R"), [[-16, 8], [0, 16], [-1000, 2]], 1000, 1)
-            ones_where(R("E2", rows=16), [[0, 8], [-1, 16]], 0, 1)
-            ones_where(R("E3", rows=16), [[0, 8], [-1, 16], [0, 2]], 0, 1)
-            select(R("TRI"), R("ONE", 0, 128), [[-1, 128]], A.is_gt, 0.0, 0, 1)
-            fill("G", R("NEG"), -1)
-            iota(R("PD"), [[0, 1]], 2050, 2)
-            iota(R("PE"), [[0, 1]], 2306, 2)
-            iota(R("O32"), [[0, 16], [-1, 2]], 1, 0)
-            iota(R("K32"), [[0, 32]], 4096, 0)
-            ones_where(R("I1F"), [[-1, 128]], 0, 1)
+                mm(R("P4", 15 - i, 256, 16, rows=nl), R(src, nl * i, nl * i + nl), w, False, src == "FL" and i == 15)
 
         def totals(a, b):
             for i in range(a, b):
-                mm(R("P5", 0, 128), R("I1"), R("XG", 1 + i, S, 16) if i < 15 else R("X15"), i == 0, False)
+                mm(R("P5", 0, nl), R("I1"), R("XG", 1 + i, 16 * nl, 16) if i < 15 else R("X15", 0, nl), i == 0, False)
             if b == 16:
                 if not first:
                     mm(R("P5", B, 128), R("I1F"), R("D1F", 0, 512, 16), False, False)
                 mm(R("P5", 0, B), R("I1"), R("D1", 0, 1536, 16), False, True)
 
-        sl, so = "SB%d" % t, R("SO%d" % min(t, 1))
-
         def short():
             mm(R("P5", 0, 128), R("ONE", 0, 128, rows=1), R("RP", rows=1), True, False)
-            mm(R("P5", 0, 128), R("BKF"), R("RF"), False, True)
-
-        def unmet():
-            if ON["uu"] == "S":
-                act(R("UU"), R("P5", 0, 128), F.Sign, -1.0)
-            else:
-                ts(R("UU"), R("P5", 0, 128), 0.0, A.is_lt, 2.0, A.mult)
-
-        def number():
-            if ON["uu"] == "S":
-                scan(R("ZC", 128, 256), R("UU"), R("ONE", 0, 128), A.add, A.add)
-            else:
-                scan(R("ZC", 128, 256), R("UU"), R("UU"), A.add, A.max)
+            mm(R("P5", 0, 128), R("BKF"), R("RB"), False, True)
 
         def slots_turn():
             for x in range(2):
@@ -474,76 +453,64 @@ def rank_program(g, core, T, topo):
             for q in range(8):
                 d, p = R("DG", 128 * q, 128 * q + 128), R("P%d" % (2 + q // 4), 128 * (q % 4), 128 * (q % 4) + 128)
                 ts(d, R("I1"), R("SC", 16 * q + 15, 16 * q + 16), A.mult)
-                mm(p, R("TRI"), d, False, q % 4 == 3 and ON["eq"] == "V")
-                if ON["eq"] == "P":
-                    mm(p, d, R("NEG"), False, q % 4 == 3)
+                mm(p, R("TRI"), d)
 
         def choices():
             for q in range(8):
                 mm(R("P6", 32 * q, 32 * q + 32), R("DG", 128 * q, 128 * q + 128), R("O32"), False, False)
 
         def equal(k):
-            if ON["eq"] == "P":
-                ts(R("EQ", 512 * k, 512 * k + 512), R("P%d" % (2 + k)), 0.0, A.is_equal)
             for q in range(4 * k, 4 * k + 4):
-                if ON["eq"] == "V":
-                    ts(R("EQ", 128 * q, 128 * q + 128), R("P%d" % (2 + k), 128 * (q % 4), 128 * (q % 4) + 128), R("SC", 16 * q + 15, 16 * q + 16), A.is_equal)
+                ts(R("EQ", 128 * q, 128 * q + 128), R("P%d" % (2 + k), 128 * (q % 4), 128 * (q % 4) + 128), R("SC", 16 * q + 15, 16 * q + 16), A.is_equal)
                 mm(R("P6", 32 * q, 32 * q + 32), R("EQ", 128 * q, 128 * q + 128), R("K32"), False, q == 7)
 
         def winners(k):
             tt(R("FM", 128 * k, 128 * k + 128), R("P6", k, 256, 2), R("DM", k, 256, 2), A.min)
             mm(R("P%d" % k, 0, 8), R("FM", 128 * k, 128 * k + 128), R("B16"))
 
-        gs = TUNE["gs"]
-        every = {
-            "g0": lambda: cards("V", 0, 32), "g1": lambda: cards("S", 32, 64), "g2": lambda: cards("S", 64, 96),
-            "g3": lambda: cards("S", 96, gs), "g4": lambda: cards("V", gs, 128) if gs < 128 else None,
-            "s0": lambda: sums(0), "s1": lambda: sums(32), "s2": lambda: sums(64), "s3": lambda: sums(96),
-            "w0": lambda: wrap(0, 0, 32), "w1": lambda: wrap(1, 32, 96), "w2": lambda: wrap(0, 96, 128),
-            "l0": lambda: leave(0, 0, 32), "l1": lambda: leave(1, 32, 96), "l2": lambda: leave(0, 96, 128),
-            "L0": lambda: leavelist(0, 32), "L1": lambda: leavelist(32, 96), "L2": lambda: leavelist(96, 128),
-            "z0": lambda: zero(0, 32), "z1": lambda: zero(32, 64), "z2": lambda: zero(cut, 128),
-            "m1": lambda: mark(64, 96), "m2": lambda: mark(96, cut), "Z1": lambda: zero(64, 96), "Z2": lambda: zero(96, cut),
-            "th": lambda: relu("th", R("TH", 0, 128), x0, 1.0, -1.0 / 32), "bs": lambda: relu("bs", R("BS"), x0, -65536.0, 1.0),
-            "th2": lambda: copy("G", R("TH", 128, 256), R("TH", 0, 128)), "th4": lambda: copy("G", R("TH", 256, 512), R("TH", 0, 256)),
-            "knz": lambda: mm(R("P4", 0, 256), R("NZ", c0, c0 + 128), R("BK2"), False, False),
-            "kbs": lambda: mm(R("P4", 0, 256), R("BS"), R("BK2"), False, False),
-            "key": lambda: tt(R("KY"), R("P4", 0, 128), R("PT"), A.min),
-            "pick": lambda: scan(R("SC"), R("P4", 128, 256), R("KY"), A.min, A.max),
+        every = {"g%d" % k: lambda p=p: cards(*p) for k, p in TUNE["gath"][min(t, 1)].items()}
+        every.update({
+            "s0": lambda: sums(0), "s1": lambda: sums(32), "s2": lambda: sums(64),
+            "w0": lambda: wrap(*WRAPS[0]), "w1": lambda: wrap(*WRAPS[1]), "l0": lambda: leave(*WRAPS[0]), "l1": lambda: leave(*WRAPS[1]),
+            "z0": lambda: zero(0, 32), "z1": lambda: zero(32, ma), "m1": lambda: mark(ma, ma + 32), "m2": lambda: mark(ma + 32, cut),
+            "Z1": lambda: zero(ma, ma + 32), "Z2": lambda: zero(ma + 32, cut),
+            "th": lambda: relu(ON["th"], R("TH", 0, nl), x0, 1.0, -1.0 / 32),
+            "bs": lambda: ts(R("BS", 0, nl), x0, 0.0, A.is_equal, 9.5 / 16, A.add),
+            "th2": lambda: copy("G", R("TH", nl, 2 * nl), R("TH", 0, nl)), "th4": lambda: copy("G", R("TH", 2 * nl, 4 * nl), R("TH", 0, 2 * nl)),
+            "kbs": lambda: mm(R("P4", 0, 256, rows=nl), R("BS", 0, nl), R("BK2"), True, False),
+            "knz": lambda: mm(R("P4", 0, 256, rows=nl), R("NZ", c0, c0 + nl), R("BK2"), False, False),
+            "key": lambda: tt(R("KY", rows=nl), R("P4", 0, 128, rows=nl), R("PT", rows=nl), A.min),
+            "pick": lambda: scan(R("SC", rows=nl), R("P4", 128, 256, rows=nl), R("KY", rows=nl), A.min, A.max),
             "pairs": pairs, "choices": choices, "e0": lambda: equal(0), "e1": lambda: equal(1),
             "win0": lambda: winners(0), "win1": lambda: winners(1),
             "u0": lambda: copy("V", R("LU", 0, 8), R("P0", 0, 8), 1.0, -1.0), "u1": lambda: copy("V", R("LU", 8, 16), R("P1", 0, 8), 1.0, -1.0),
-            "take": lambda: gath(ON["take"], R("VV", 128, 256), R("W", 0, WN), R("LU", 0, 8)),
-            "move": lambda: scat("V", R("W", 0, WN), R("LU"), R("VV"))}
+            "take": lambda: gath("V", R("VV", 128, 256), R("W", 0, WN), R("LU", 0, 8)),
+            "move": lambda: scat("V", R("W", 0, WN), R("LU"), R("VV"))})
         for k in range(len(cov) - 1):
             every.update({"c%d" % k: lambda k=k: compare(k), "f%d" % k: lambda k=k: marked(k),
                           "nc%d" % k: lambda k=k: count("CM", k), "nf%d" % k: lambda k=k: count("FL", k)})
         if first:
-            every.update({
-                "ends0": lambda: ends(0, 1), "nz0": lambda: noneed(0), "nz1": lambda: noneed(1), "nz2": lambda: noneed(2), "consts": consts,
-                "cov0": lambda: covers(0), "vm0": lambda: vtr(R("MT"), R("MH")), "turn0": lambda: covers_turn("P6"), "ml0": coverlist,
-                "pt0": lambda: keys("P6"), "oc0": open_counts, "op0": open_pairs, "ol0": lambda: open_lists(0),
-                "ch": lambda: cards16(1, 3), "endt": lambda: ends_turn(1, 3), "ends": lambda: ends(1, 3), "cu": lambda: cardlist(1, 3),
-                "dmm": lambda: mm(R("P0", 0, 256), R("E2", rows=16), R("E3", rows=16)),
-                "dm0": lambda: act(R("DM", 0, 256, 2), R("P0", 0, 256, 2), F.Copy, R("PD")),
-                "dm1": lambda: act(R("DM", 1, 256, 2), R("P0", 1, 256, 2), F.Copy, R("PE")),
-                "b16": lambda: copy("S", R("B16"), R("BK", 0, 128, 16)),
-                "wz": lambda: fill("S", R("W", S + 1, WN), 0.0), "vz": lambda: fill("S", R("VV", 0, 128), 0.0)})
+            every.update(begin)
         else:
             every.update({
+                "s3": lambda: sums(96), "w2": lambda: wrap(*WRAPS[2]), "l2": lambda: leave(*WRAPS[2]), "z2": lambda: zero(cut, 128),
                 "arr": lambda: copy("G", R("D1F", 0, 512, 16), R("ARR%d" % (t - 1))), "ml": coverlist, "pt": lambda: keys("P5"),
-                "nzm": lambda: mm(R("P7", 0, U), R("BKF"), R("D1F", 0, 512, 16)),
-                "nz": lambda: relu("nz", R("NZ", c0 + B, c0 + 128), R("P7", 0, U), -1.0, 1.0)})
+                "arb": lambda: copy("G", R("AB"), R("ARR%d" % (t - 1))), "nzm": lambda: mm(R("P7", 0, U), R("BKF"), R("AB")),
+                "nz": lambda: relu(ON["nz"], R("NZ", c0 + B, c0 + 128), R("P7", 0, U), -1.0, 1.0)})
         if not last:
             every.update({
-                "x15": lambda: gath(ON["x15"], R("X15"), WG, SL(0, t)), "tot0": lambda: totals(0, 8), "tot1": lambda: totals(8, 16),
-                "rf": lambda: relu("rf", R("RF"), R("P5", 0, 128), -1.0, 0.0), "short": short, "uu": unmet,
-                "zc": lambda: relu("zc", R("ZC", 0, 128), R("P5", 0, 128), 1.0, 0.0),
-                "num": number, "vz2": lambda: vtr(R("ZT"), R("ZC")), "turnz": slots_turn,
+                "x15": lambda: gath(ON["x15"], R("X15"), WG, SL(0, t)),
+                "tot0": lambda: totals(0, 4), "tot1": lambda: totals(4, 8), "tot2": lambda: totals(8, 12), "tot3": lambda: totals(12, 16),
+                "rf": lambda: relu(ON["rf"], R("RF", 0, nl), R("P5", 0, nl), -1.0, 0.0), "rb": lambda: copy(ON["rb"], R("RB"), R("RF")),
+                "short": short, "uu": lambda: act(R("UU"), R("P5", 0, 128), F.Sign, -1.0),
+                "zc": lambda: relu(ON["zc"], R("ZC", 0, 128), R("P5", 0, 128), 1.0, 0.0),
+                "num": lambda: scan(R("ZC", 128, 256), R("UU"), R("ONE", 0, 128), A.add, A.add),
+                "vz2": lambda: vtr(R("ZT"), R("ZC")), "turnz": slots_turn,
                 "ol": lambda: copy("V", R("OL"), R("P5", 0, 8), 0.5, -1.0), "sb": lambda: fill("S", R(sl, 0, U), -MAGIC), "put": put,
                 "so": lambda: copy(ON["so"], so, R(sl, 0, U), 1.0, MAGIC), "send": send, "needs": lambda: needs("S", t + 1),
                 "cov": lambda: covers(t + 1), "vm": lambda: vtr(R("MT"), R("MH")), "turn": lambda: covers_turn("P5"),
-                "op": open_pairs, "oc": open_counts, "olist": lambda: open_lists(t + 1)})
+                "ow0": lambda: open_wrap(t + 1, *WRAPS[0]), "ow1": lambda: open_wrap(t + 1, *WRAPS[1]), "ow2": lambda: open_wrap(t + 1, *WRAPS[2]),
+                "olist": lambda: open_lists(t + 1)})
         for name in ORDER:
             if name in every:
                 every[name]()

from concourse.mybir import AluOpType as A, ActivationFunctionType as F

BF, FP, F16, I32, U16 = "bfloat16", "float32", "float16", "int32", "uint16"
S, L, B, U, RO = 2048, 128, 96, 32, 3
BIG = 4096.0
DUMP = 2064
WW, WN = 4128, 2560
KE = 8192.0
WC = 4096.0
MAGIC = 12582912.0
NENG = 4

SCRATCH = {}
for _n, _w, _d in [
        ("SK", S, BF), ("SKF", S, FP), ("OC", 128, I32), ("CD", 384, I32), ("ND", 288, BF), ("CV", S, I32),
        ("W", WW, FP), ("FW", WW, BF), ("XG", S + 16, BF), ("EE", S, BF), ("D1", 1536, BF), ("D1F", 512, FP), ("CM", S, BF), ("FL", S, BF),
        ("ZR", 512, FP), ("MK0", 512, BF), ("MK1", 512, BF), ("MK2", 512, BF), ("TH", 512, BF), ("RH", 1024, F16),
        ("OH", 128, F16), ("OT", 128, F16), ("OU", 128, U16), ("CU", 384, U16), ("CH", 384, F16), ("CT", 384, F16),
        ("SL", 48, U16), ("MH", 128, F16), ("MT", 128, F16), ("ML", 128, U16), ("PT", 128, FP), ("NZ", 384, BF), ("BS", 128, BF),
        ("LL", 128, U16), ("X15", 128, BF), ("KY", 128, FP), ("SC", 128, FP), ("DG", 1024, F16), ("EQ", 1024, BF),
        ("FM", 256, F16), ("LU", 16, U16), ("VV", 256, FP), ("RF", 128, FP), ("RB", 128, BF), ("ZC", 256, BF), ("ZT", 256, BF), ("UU", 128, BF),
        ("OL", 8, U16), ("SB0", 512, FP), ("SB1", 512, FP), ("SO0", U, FP), ("SO1", U, FP), ("RB0", U, FP), ("RB1", U, FP),
        ("ARR0", U, FP), ("ARR1", U, FP), ("AB", U, BF), ("YC", 128, FP), ("YI", 128, I32), ("YJ", 128, I32), ("YO", 128, FP),
        ("WX", 256, FP), ("BK2", 256, BF), ("S0R", 256, BF), ("DM", 256, FP), ("I1F", 128, FP), ("ONE", 256, BF), ("E3", 256, BF)]:
    SCRATCH[_n] = ("sbuf", [128, _w], _d)
PARTS = {}
for _b, _d, _l in [
        ("GI", I32, [("IP", 8), ("IA", 8), ("IB", 8)]),
        ("GF", FP, [("PX", 8), ("PY", 8), ("PM", 8), ("PN", 8), ("PD", 8), ("PE", 8)]),
        ("GB", BF, [("I1", 128), ("Z", 144), ("BK", 128), ("BKF", 128), ("SW", 48), ("RP", 128), ("PV", 128), ("TRI", 128), ("Q00", 128),
                    ("Q01", 128), ("Q10", 128), ("Q11", 128), ("B16", 16), ("O32", 32), ("K32", 32), ("C16", 128), ("E1", 128), ("E2", 128),
                    ("E4", 144), ("CK", 64)])]:
    _o = 0
    for _n, _w in _l:
        PARTS[_n] = (_b, _o, 1 if _b in ("GI", "GF") else {"B16": 8}.get(_n, _w))
        _o += _w
    SCRATCH[_b] = ("sbuf", [128, _o], _d)
for _k in range(8):
    SCRATCH["P%d" % _k] = ("psum", [128, 512], FP)
SEMAPHORES = ["cV", "cS", "cP", "cG"] + ["d%d" % k for k in range(12)] + ["arr0", "arr1", "rin0", "rin1", "out0", "out1"]

TUNE = {"state": [("S", 0, 72), ("V", 72, 100), ("V", 100, 128)],
        "gath": [{0: ("V", 0, 16), 1: ("S", 16, 32), 2: ("S", 32, 64), 3: ("S", 64, 76), 4: ("V", 76, 96)},
                 {0: ("V", 0, 16), 1: ("S", 16, 32), 2: ("S", 32, 64), 3: ("S", 64, 96), 4: ("V", 96, 128)}],
        "cov": [[0, 4, 8, 12, 16], [0, 4, 8, 12, 16], [0, 4, 8, 12, 15, 16]], "marks": [(58, 96), (64, 116), (64, 114)]}
ON = {"big": "V", "needs0": "V", "d10": "V", "d11": "V", "d12": "V", "x15": "V", "th": "V", "nz": "V", "rf": "S", "zc": "S", "so": "V",
      "rb": "G"}
ORDER = """wx zr one ip d10 rh0 ia E1 c16 rh1 wbig py E4 ramp0 rh2 E3 px d12 ramp2 E2 blocks q11 ib oh i1 q00 ot d1f sw1 pm ramp3 pv sw0
bk2b q10 bkf q01 ramp1 pn Z sk0 turno d11 xbig tab2 ou tab0 bk tab3 ck sk1 fw ch0 s0r bk2c bk2a tab1 mk b16 W0 W1 ow01 ow00 endt0 nd
needs0 arr W2 rff cu0
g1 g2 ends0 g3 g0 nz0 scf x15 s0 g4 pt w0 s1 l0 s2 w1 ml th arb z0 s3 cov0 sb l1 bs tot0 z1 th2 w2 vm0 m1 l2 rp tot2 turn0 th4 tot1
ml0 nzm tot3 nz kbs m2 z2 pt0
rf f1 ol0 f0 c1 dmm rb f2 c0 c2 c3 ch c4 short knz consts nf0 nf1 f3 nc0 nc2 uu nc1 f4 nf2 nz1 nc3 zc nf3 nz2 nc4 Z1 dm0 endt nf4
num wz key vz2 pick turnz cu pairs ol e0 ow0 choices e1 dm1 put win0 so ends win1 send cov olist needs u0 Z2 u1 take vm vz move ow1 ow2
turn""".split()


def rank_program(g, core, T, topo):
    cores = list(T.cores)
    n = len(cores)

    def relay_of(r):
        src, dst = cores[r], cores[(r + 1) % n]
        c = [x for x in topo.cores_of(src) if x != src and topo.may_write(x, dst)]
        c.sort(key=lambda x: (topo.die(x) != topo.die(src), x))
        return c[0]

    def emask(a, b):
        e = topo.engines(a, b)[:NENG]
        return sum(1 << x for x in e), len(e)

    rank = T.rank_of(core)
    if rank is None:
        for r in range(n):
            if relay_of(r) == core:
                dst = cores[(r + 1) % n]
                _, nin = emask(cores[r], core)
                m, k = emask(core, dst)
                rid, pid = topo.addr(dst, core)
                for t in range(RO - 1):
                    g.wait_ge(T.sem["rin%d" % t], nin)
                    g.remote_dma(T["ARR%d" % t][:, :], T["RB%d" % t][:, :], T.sem["arr%d" % t], T.sem["out%d" % t], pid, rid, m)
                for t in range(RO - 1):
                    g.wait_ge(T.sem["out%d" % t], k)
        return

    Q = {"V": g.vector, "S": g.scalar, "P": g.tensor, "G": g, "Y": g.sync}
    CS = {"V": "cV", "S": "cS", "P": "cP", "G": "cG"}
    acc, done, on = {}, [], []
    cnt, known, total, nd = {k: 0 for k in CS}, {k: {} for k in Q}, {}, [0]

    def R(name, lo=0, hi=None, st=1, rows=128):
        if name in PARTS:
            b, o, w = PARTS[name]
            return (b, o + lo, o + (w if hi is None else hi), st, rows)
        return (name, lo, SCRATCH[name][1][-1] if hi is None else hi, st, rows)

    def ap(r):
        return T[r[0]][0:r[4], r[1]:r[2]:r[3]] if r[3] != 1 else T[r[0]][0:r[4], r[1]:r[2]]

    def psum(name):
        return SCRATCH[name][0] == "psum"

    def width(r):
        return (r[2] - r[1] + r[3] - 1) // r[3]

    def apart(a, b):
        return a[1] >= b[2] or b[1] >= a[2] or (a[3] == b[3] and a[3] > 1 and (a[1] - b[1]) % a[3] != 0)

    def issue(q, fn, reads, writes, chain=False, sem=None):
        me, need = len(done), {}
        mine = [(r, "r") for r in reads] + [(r, "w") for r in writes]
        for rr, k in mine:
            for (o, ok, j) in acc.get(rr[0], []):
                same = on[j] == q
                if psum(rr[0]):
                    if same and ((k == "r" and ok == "r") or (q == "P" and (chain or apart(rr, o)))):
                        continue
                elif apart(rr, o) or (k == "r" and ok == "r"):
                    continue
                need[done[j][0]] = max(need.get(done[j][0], 0), done[j][1])
        for rr, k in mine:
            keep = []
            for e in acc.get(rr[0], []):
                o = e[0]
                cov = rr[1] <= o[1] and o[2] <= rr[2] and rr[4] >= o[4] and (rr[3] == 1 or (rr[3] == o[3] and (rr[1] - o[1]) % rr[3] == 0))
                if k == "w" and e[2] != me and (cov or (psum(rr[0]) and on[e[2]] != "P")):
                    continue
                keep.append(e)
            keep.append((rr, k, me))
            acc[rr[0]] = keep
        for s in sorted(need):
            if known[q].get(s, 0) < need[s]:
                Q[q].wait_ge(T.sem[s], need[s])
                known[q][s] = need[s]
        ins = fn(Q[q])
        if sem is None:
            cnt[q] += 1
            sem = (CS[q], cnt[q])
            ins.then_inc(T.sem[CS[q]], 1)
            on.append(q)
        elif sem == "dma":
            sem = ("d%d" % nd[0], 16)
            nd[0] += 1
            ins.then_inc(T.sem[sem[0]], 16)
            on.append("")
        else:
            on.append("")
        done.append(sem)
        total[sem[0]] = max(total.get(sem[0], 0), sem[1])

    def dma(q, out, in_, reads, writes):
        issue(q, lambda e: e.dma_start(out, in_), reads, writes, sem="dma")

    def copy(q, o, i, scale=1.0, bias=0.0):
        if q == "S":
            act(o, i, F.Copy if bias == 0.0 else F.Identity, scale, bias)
        elif q == "G":
            select(o, i, [[0, width(o)]], A.is_ge, 0.0, 0, 0)
        elif scale == 1.0 and bias == 0.0:
            issue(q, lambda e: e.tensor_copy(ap(o), ap(i)), [i], [o])
        else:
            ts(o, i, float(scale), A.mult, float(bias), A.add)

    def act(o, i, func, scale=1.0, bias=0.0):
        if isinstance(scale, tuple):
            issue("S", lambda e: e.activation(ap(o), ap(i), func, scale=ap(scale)), [i, scale], [o])
        else:
            issue("S", lambda e: e.activation(ap(o), ap(i), func, bias=float(bias), scale=float(scale)), [i], [o])

    def ts(o, i, s1, op0, s2=None, op1=None):
        rd = [i] + [s for s in (s1, s2) if isinstance(s, tuple)]
        a1, a2 = [ap(s) if isinstance(s, tuple) else s for s in (s1, s2)]
        if op1 is None:
            issue("V", lambda e: e.tensor_scalar(ap(o), ap(i), a1, None, op0), rd, [o])
        else:
            issue("V", lambda e: e.tensor_scalar(ap(o), ap(i), a1, a2, op0, op1), rd, [o])

    def tt(o, a, b, o_):
        issue("V", lambda e: e.tensor_tensor(ap(o), ap(a), ap(b), o_), [a, b], [o])

    def fill(q, o, v):
        if q == "V":
            issue(q, lambda e: e.memset(ap(o), v), [], [o])
        elif q == "S":
            copy(q, o, R("ZR", 0, width(o), rows=o[4]), 1.0, v)
        else:
            iota(o, [[0, width(o)]], int(v), 0)

    def relu(q, o, i, scale, bias):
        if q == "S":
            act(o, i, F.Relu, scale, bias)
        elif bias == 1.0:
            ts(o, i, 0.0, A.is_equal)
        elif scale == 1.0:
            ts(o, i, bias, A.add, 0.0, A.max)
        else:
            ts(o, i, scale, A.mult, 0.0, A.max)

    def scan(o, a, b, op0, op1):
        issue("V", lambda e: e.tensor_tensor_scan(ap(o), ap(a), ap(b), 0.0, op0, op1), [a, b], [o])

    def mm(o, l, r, start=True, stop=True):
        issue("P", lambda e: e.matmul(ap(o), ap(l), ap(r), start, stop), [l, r], [o], chain=not start)

    def gath(q, o, win, lst):
        issue(q, lambda e: e.tensor_copy(ap(o), ap(win).indirect(ap(lst))) if q == "V" else
              e.activation(ap(o), ap(win).indirect(ap(lst)), F.Copy), [win, lst], [o])

    def scat(q, win, lst, i):
        issue(q, lambda e: e.tensor_copy(ap(win).indirect(ap(lst)), ap(i)) if q == "V" else
              e.activation(ap(win).indirect(ap(lst)), ap(i), F.Silu), [lst, i], [win])

    def iota(o, pat, base, cm):
        if SCRATCH[o[0]][2] == I32:
            issue("G", lambda e: e.iota(ap(o), pat, base, cm), [], [o])
        else:
            issue("G", lambda e: e.iota(ap(o), pat, base, cm, allow_small_or_imprecise_dtypes=True), [], [o])

    def select(o, i, pat, op, other, base, cm):
        issue("G", lambda e: e.affine_select(ap(o), ap(i), pat, op, other, base, cm), [i], [o])

    def ones_where(o, pat, base, cm):
        select(o, R("ONE", 0, width(o), rows=o[4]), pat, A.is_equal, 0.0, base, cm)

    def vtr(o, i):
        issue("V", lambda e: e.transpose(ap(o), ap(i)), [i], [o])

    def Qm(x, y):
        return R("Q%d%d" % (x, y))

    def turn(bank, src, nb=4):
        for b in range(nb):
            for x in range(2):
                for y in range(2):
                    mm(R(bank, 2 * b + x, 32 * nb, 2 * nb), Qm(x, y), R(src, 32 * b + 16 * y, 32 * b + 16 * y + 16), y == 0, y == 1)

    def Z(i):
        return R("Z", 15 - i, 143 - i)

    WG, WS, D0 = R("W", 0, S + 1), R("W"), R("WX", 64, 192)
    WRAPS = ((2, 0, 32), (3, 32, 96), (1, 96, 128))

    dma("Y", T.OC[:, :], T.occ[:, :], [], [R("OC")])
    for q, a, b in (("S", 0, 1024), ("Y", 1024, 1536), ("Y", 1536, S)):
        dma(q, T.SK[:, a:b], T.skill[:, a:b], [], [R("SK", a, b)])
    dma("Y", T.CD[:, 0:128], T.cards[:, 0:128], [], [R("CD", 0, 128)])
    dma("Y", T.ND[:, :], T.need[:, :], [], [R("ND")])
    dma("Y", T.CV[:, :], T.cover[:, :], [], [R("CV")])
    dma("Y", T.CD[:, 128:384], T.cards[:, 128:384], [], [R("CD", 128, 384)])

    def cards16(a, b):
        copy("V", R("CH", 128 * a, 128 * b), R("CD", 128 * a, 128 * b), 1.0, 1.0)

    def cardlist(a, b):
        ts(R("CU", 128 * a, 128 * b), R("CH", 128 * a, 128 * b), R("PM"), A.mult, R("PN"), A.add)

    def ends_turn(a, b):
        vtr(R("CT", 128 * a, 128 * b), R("CH", 128 * a, 128 * b))
        w = 8 * (b - a)
        for u, i in enumerate((15, 0)):
            for x in range(2):
                for y in range(2):
                    mm(R("P7", w * u + x, w * u + w, 2), Qm(x, y), R("CT", 128 * a + 16 * y + i, 128 * b, 32), y == 0, y == 1)

    def ends(a, b):
        copy("V", R("SL", 16 * a, 16 * b), R("P7", 0, 16 * (b - a)), 1.0, -1.0)

    def SL(u, t):
        return R("SL", 8 * u, 8 * u + 8) if t == 0 else R("SL", 8 + 16 * u + 8 * t, 16 + 16 * u + 8 * t)

    def covers(t):
        issue("V", lambda e: e.tensor_scalar(ap(R("MH")), ap(R("CV")).indirect(ap(SL(1, t))), 1.0, None, A.add), [R("CV"), SL(1, t)], [R("MH")])

    def covers_turn(bank, nb=4):
        turn("P7", "MT", nb)
        mm(R(bank, 128, 256), R("MH"), R("PV"))

    def coverlist(nl=L):
        copy("V", R("ML", 0, nl), R("P7", 0, nl), 1.0, -1.0)

    def keys(bank):
        copy("S", R("PT"), R(bank, 128, 256))

    def needs(q, t):
        copy(q, R("D1", 0, 1536, 16), R("ND", B * t, B * t + B), -1.0)

    def noneed(t):
        act(R("NZ", 128 * t, 128 * t + B), R("P7", 128 + B * t, 128 + B * t + B), F.Relu, -1.0, 1.0)

    def open_wrap(t, k, a, b):
        p = R("P%d" % k, 0, b - a)
        mm(p, R("I1"), R("CH", 128 * t + a, 128 * t + b), True, False)
        mm(p, R("ONE", 0, 128, rows=1), R("CK", 0, b - a, rows=1), False, False)

    def open_lists(t):
        mm(R("P6", 0, 256), R("CH", 128 * t, 128 * t + 128), R("S0R"), True, False)

    bk = R("P6", 256, 384)

    def ramp(c):
        mm(R("P%d" % c), R("C16", rows=1), R("RH", 512 * (c % 2), 512 * (c % 2) + 512, rows=1), True, c > 1)

    def table(c):
        sk, o = R("SK", 512 * c, 512 * c + 512), R("SKF", 512 * c, 512 * c + 512)
        if c < 2:
            copy("S", o, R("P%d" % c), 1.0, 1.0 / 64)
        else:
            tt(o, sk, R("P%d" % c), A.add)

    def blocks():
        mm(R("P6", 0, 144), R("E1", rows=8), R("E4", rows=8))
        mm(bk, R("E1", rows=8), R("E1", rows=8))

    def signs(a, b):
        for k in range(a, b):
            copy("S", R("SW", 8 * k, 8 * k + 8), R("P6", 256, 384, 16), (-WC, WC, -WC, 0.0, WC, 0.0)[k])

    def sel(x, y):
        ts(Qm(x, y), D0, 16.0 * (y - x), A.is_equal, R("PX" if x else "PY"), A.mult)

    def consts():
        select(R("TRI"), R("ONE", 0, 128), [[-1, 128]], A.is_gt, -1.0, 0, 1)
        iota(R("PD"), [[0, 1]], 2050, 2)
        iota(R("PE"), [[0, 1]], 2306, 2)
        iota(R("O32"), [[0, 16], [-1, 2]], 1, 0)
        iota(R("K32"), [[0, 32]], 4096, 0)
        ones_where(R("I1F"), [[-1, 128]], 0, 1)

    begin = {
        "wx": lambda: iota(R("WX"), [[1, 256]], -64, -1),
        "ip": lambda: iota(R("IP"), [[0, 1]], 0, 1), "one": lambda: fill("V", R("ONE"), 1.0),
        "c16": lambda: fill("V", R("C16", rows=32), 2.0 ** -16), "zr": lambda: fill("V", R("ZR"), 0.0),
        "d1f": lambda: act(R("D1F"), R("ZR"), F.Silu),
        "E1": lambda: ones_where(R("E1", rows=8), [[-1, 8], [0, 16]], 0, 1), "E4": lambda: ones_where(R("E4", rows=8), [[1, 144]], -15, -16),
        "fw": lambda: fill("G", R("FW", 0, S), 0), "mk": lambda: fill("G", R("MK0"), 1),
        "rh0": lambda: copy("V", R("RH", 0, 256, rows=1), R("WX", rows=1), -1.0, 959.0),
        "rh1": lambda: copy("V", R("RH", 256, 512, rows=1), R("RH", 0, 256, rows=1), 1.0, -256.0),
        "rh2": lambda: copy("V", R("RH", 512, 1024, rows=1), R("RH", 0, 512, rows=1), 1.0, -512.0),
        "ia": lambda: ts(R("IA"), R("IP"), 4, A.arith_shift_right, 1, A.bitwise_and),
        "px": lambda: copy("V", R("PX"), R("IA")), "py": lambda: copy("V", R("PY"), R("IA"), -1.0, 1.0),
        "q11": lambda: sel(1, 1), "q10": lambda: sel(1, 0), "q00": lambda: sel(0, 0), "q01": lambda: sel(0, 1),
        "oh": lambda: copy("V", R("OH"), R("OC")), "i1": lambda: ts(R("I1"), D0, 0.0, A.is_equal), "ot": lambda: vtr(R("OT"), R("OH")),
        "blocks": blocks, "turno": lambda: turn("P7", "OT"), "ou": lambda: copy("V", R("OU"), R("P7", 0, 128)),
        "ib": lambda: ts(R("IB"), R("IP"), 15, A.bitwise_and), "pm": lambda: ts(R("PM"), R("IB"), 15.0, A.is_lt),
        "pn": lambda: copy("V", R("PN"), R("PM"), -float(S + 1), float(S)),
        "wbig": lambda: fill(ON["big"], R("W", S, S + 1), BIG), "xbig": lambda: fill(ON["big"], R("XG", 0, 1), BIG),
        "ck": lambda: fill(ON["big"], R("CK", rows=32), float(DUMP)),
        "Z": lambda: copy("S", R("Z"), R("P6", 0, 144), KE), "bk": lambda: copy("S", R("BK"), bk),
        "bkf": lambda: copy("S", R("BKF"), bk, -2048.0), "bk2a": lambda: copy("S", R("BK2", 0, 128), bk, -WC),
        "bk2b": lambda: copy("S", R("BK2", 128, 256), bk, WC), "bk2c": lambda: fill("S", R("BK2", 128, 256, 16), 0.0),
        "sw0": lambda: signs(0, 3), "sw1": lambda: signs(3, 6),
        "ch0": lambda: cards16(0, 1), "needs0": lambda: needs(ON["needs0"], 0), "cu0": lambda: cardlist(0, 1), "endt0": lambda: ends_turn(0, 1),
        "nd": lambda: mm(R("P7", 128, 416), R("BK"), R("ND")),
        "rp": lambda: iota(R("RP", rows=32), [[2, 128]], 258, 0), "pv": lambda: ones_where(R("PV"), [[-16, 8], [1, 16]], -15, 1),
        "s0r": lambda: ones_where(R("S0R"), [[-16, 8], [0, 16], [-1000, 2]], 1000, 1),
        "E2": lambda: ones_where(R("E2", rows=16), [[0, 8], [-1, 16]], 0, 1),
        "E3": lambda: ones_where(R("E3", rows=16), [[0, 8], [-1, 16], [0, 2]], 0, 1),
        "ends0": lambda: ends(0, 1), "nz0": lambda: noneed(0), "nz1": lambda: noneed(1), "nz2": lambda: noneed(2), "consts": consts,
        "cov0": lambda: covers(0), "vm0": lambda: vtr(R("MT"), R("MH")), "turn0": lambda: covers_turn("P6", 3), "ml0": lambda: coverlist(B),
        "scf": lambda: fill("S", R("SC"), 0.0), "rff": lambda: fill("S", R("RF", B, 128), 0.0),
        "pt0": lambda: keys("P6"), "ol0": lambda: open_lists(0),
        "ch": lambda: cards16(1, 3), "endt": lambda: ends_turn(1, 3), "ends": lambda: ends(1, 3), "cu": lambda: cardlist(1, 3),
        "dmm": lambda: mm(R("P0", 0, 256), R("E2", rows=16), R("E3", rows=16)),
        "dm0": lambda: act(R("DM", 0, 256, 2), R("P0", 0, 256, 2), F.Copy, R("PD")),
        "dm1": lambda: act(R("DM", 1, 256, 2), R("P0", 1, 256, 2), F.Copy, R("PE")),
        "b16": lambda: copy("S", R("B16"), R("BK", 0, 128, 16)),
        "wz": lambda: fill("S", R("W", S + 1, WN), 0.0), "vz": lambda: fill("S", R("VV", 0, 128), 0.0)}
    for c in range(4):
        begin.update({"ramp%d" % c: lambda c=c: ramp(c), "tab%d" % c: lambda c=c: table(c)})
    for c in range(3):
        begin.update({"d1%d" % c: lambda c=c: fill(ON["d1%d" % c], R("D1", 512 * c, 512 * c + 512), 0.0),
                      "W%d" % c: lambda p=TUNE["state"][c]: gath(p[0], R("W", 16 * p[1], 16 * p[2]), R("SKF"), R("OU", p[1], p[2]))})
    for c in range(2):
        begin["ow0%d" % c] = lambda c=c: open_wrap(0, *WRAPS[c])
        begin["sk%d" % c] = lambda c=c: mm(R("P%d" % c), R("I1"), R("SK", 512 * c, 512 * c + 512), False, True)

    for t in range(RO):
        first, last, c0, cov = t == 0, t == RO - 1, 128 * t, TUNE["cov"][t]
        nl = B if first else L
        ma, cut = TUNE["marks"][t]
        x0, sl, so = R("XG", 1, 16 * nl, 16), "SB%d" % t, R("SO%d" % min(t, 1))

        def cards(q, a, b):
            gath(q, R("XG", 1 + 16 * a, 1 + 16 * b), WG, R("CU", c0 + a, c0 + b))

        def sums(a):
            scan(R("EE", 16 * a, 16 * a + 512), R("XG", 16 * a, 16 * a + 512), R("D1", 16 * a, 16 * a + 512) if a < B else R("D1F"), A.add, A.min)

        def wrap(k, a, b):
            p = R("P%d" % k, 0, b - a)
            for i in range(16):
                mm(p, Z(i), R("EE", 16 * a + i, 16 * b, 16), False, i == 15)

        def leave(k, a, b):
            tt(R("LL", a, b), R("P%d" % k, 0, b - a), R("CD", c0 + a, c0 + b), A.max)

        def zero(a, b):
            scat("S", WS, R("LL", a, b), R("ZR", 0, 16 * (b - a)))

        def mark(a, b):
            scat("V", R("FW"), R("LL", a, b), R("MK%d" % t, 0, 16 * (b - a)))

        def compare(k):
            a, b = cov[k], cov[k + 1]
            m, th, p = R("CM", nl * a, nl * b), R("TH", 0, nl * (b - a)), R("ML", nl // 16 * a, nl // 16 * b)
            issue("V", lambda e: e.tensor_tensor(ap(m), ap(WG).indirect(ap(p)), ap(th), A.is_gt), [WG, p, th], [m])

        def marked(k):
            a, b = cov[k], cov[k + 1]
            f, w, p = R("FL", nl * a, nl * b), R("FW", 0, S), R("ML", nl // 16 * a, nl // 16 * b)
            issue("S", lambda e: e.activation(ap(f), ap(w).indirect(ap(p)), F.Relu, bias=-float(t)), [w, p], [f])

        def count(src, k):
            u = 8 if src == "CM" else 0
            for i in range(cov[k], cov[k + 1]):
                w = R("SW", u, u + 16) if i < 15 else R("SW", 16 + 2 * u, 32 + 2 * u)
                mm(R("P4", 15 - i, 256, 16, rows=nl), R(src, nl * i, nl * i + nl), w, False, src == "FL" and i == 15)

        def totals(a, b):
            for i in range(a, b):
                mm(R("P5", 0, nl), R("I1"), R("XG", 1 + i, 16 * nl, 16) if i < 15 else R("X15", 0, nl), i == 0, False)
            if b == 16:
                if not first:
                    mm(R("P5", B, 128), R("I1F"), R("D1F", 0, 512, 16), False, False)
                mm(R("P5", 0, B), R("I1"), R("D1", 0, 1536, 16), False, True)

        def short():
            mm(R("P5", 0, 128), R("ONE", 0, 128, rows=1), R("RP", rows=1), True, False)
            mm(R("P5", 0, 128), R("BKF"), R("RB"), False, True)

        def slots_turn():
            for x in range(2):
                for y in range(2):
                    for u in range(2):
                        mm(R("P5", x, 8, 2), Qm(x, y), R("ZT", 128 * u + 16 * y, 128 * u + 128, 32), y + u == 0, y + u == 2)

        def put():
            issue("V", lambda e: e.tensor_scalar(ap(R(sl)).indirect(ap(R("OL"))), ap(R("RF")), -(1.0 + 2.0 ** -14), -MAGIC, A.mult, A.add),
                  [R("OL"), R("RF")], [R(sl)])

        def send():
            rl = relay_of(rank)
            m, k = emask(core, rl)
            rid, pid = topo.addr(rl, core)
            _, ka = emask(relay_of((rank - 1) % n), core)
            issue("G", lambda e: e.remote_dma(T["RB%d" % t][:, :], ap(so), T.sem["rin%d" % t], T.sem["out%d" % t], pid, rid, m),
                  [so], [R("ARR%d" % t)], sem=("arr%d" % t, ka))
            total["out%d" % t] = k
            fill("G", R("MK%d" % (t + 1)), t + 2)

        def pairs():
            for q in range(8):
                d, p = R("DG", 128 * q, 128 * q + 128), R("P%d" % (2 + q // 4), 128 * (q % 4), 128 * (q % 4) + 128)
                ts(d, R("I1"), R("SC", 16 * q + 15, 16 * q + 16), A.mult)
                mm(p, R("TRI"), d)

        def choices():
            for q in range(8):
                mm(R("P6", 32 * q, 32 * q + 32), R("DG", 128 * q, 128 * q + 128), R("O32"), False, False)

        def equal(k):
            for q in range(4 * k, 4 * k + 4):
                ts(R("EQ", 128 * q, 128 * q + 128), R("P%d" % (2 + k), 128 * (q % 4), 128 * (q % 4) + 128), R("SC", 16 * q + 15, 16 * q + 16), A.is_equal)
                mm(R("P6", 32 * q, 32 * q + 32), R("EQ", 128 * q, 128 * q + 128), R("K32"), False, q == 7)

        def winners(k):
            tt(R("FM", 128 * k, 128 * k + 128), R("P6", k, 256, 2), R("DM", k, 256, 2), A.min)
            mm(R("P%d" % k, 0, 8), R("FM", 128 * k, 128 * k + 128), R("B16"))

        every = {"g%d" % k: lambda p=p: cards(*p) for k, p in TUNE["gath"][min(t, 1)].items()}
        every.update({
            "s0": lambda: sums(0), "s1": lambda: sums(32), "s2": lambda: sums(64),
            "w0": lambda: wrap(*WRAPS[0]), "w1": lambda: wrap(*WRAPS[1]), "l0": lambda: leave(*WRAPS[0]), "l1": lambda: leave(*WRAPS[1]),
            "z0": lambda: zero(0, 32), "z1": lambda: zero(32, ma), "m1": lambda: mark(ma, ma + 32), "m2": lambda: mark(ma + 32, cut),
            "Z1": lambda: zero(ma, ma + 32), "Z2": lambda: zero(ma + 32, cut),
            "th": lambda: relu(ON["th"], R("TH", 0, nl), x0, 1.0, -1.0 / 32),
            "bs": lambda: ts(R("BS", 0, nl), x0, 0.0, A.is_equal, 9.5 / 16, A.add),
            "th2": lambda: copy("G", R("TH", nl, 2 * nl), R("TH", 0, nl)), "th4": lambda: copy("G", R("TH", 2 * nl, 4 * nl), R("TH", 0, 2 * nl)),
            "kbs": lambda: mm(R("P4", 0, 256, rows=nl), R("BS", 0, nl), R("BK2"), True, False),
            "knz": lambda: mm(R("P4", 0, 256, rows=nl), R("NZ", c0, c0 + nl), R("BK2"), False, False),
            "key": lambda: tt(R("KY", rows=nl), R("P4", 0, 128, rows=nl), R("PT", rows=nl), A.min),
            "pick": lambda: scan(R("SC", rows=nl), R("P4", 128, 256, rows=nl), R("KY", rows=nl), A.min, A.max),
            "pairs": pairs, "choices": choices, "e0": lambda: equal(0), "e1": lambda: equal(1),
            "win0": lambda: winners(0), "win1": lambda: winners(1),
            "u0": lambda: copy("V", R("LU", 0, 8), R("P0", 0, 8), 1.0, -1.0), "u1": lambda: copy("V", R("LU", 8, 16), R("P1", 0, 8), 1.0, -1.0),
            "take": lambda: gath("V", R("VV", 128, 256), R("W", 0, WN), R("LU", 0, 8)),
            "move": lambda: scat("V", R("W", 0, WN), R("LU"), R("VV"))})
        for k in range(len(cov) - 1):
            every.update({"c%d" % k: lambda k=k: compare(k), "f%d" % k: lambda k=k: marked(k),
                          "nc%d" % k: lambda k=k: count("CM", k), "nf%d" % k: lambda k=k: count("FL", k)})
        if first:
            every.update(begin)
        else:
            every.update({
                "s3": lambda: sums(96), "w2": lambda: wrap(*WRAPS[2]), "l2": lambda: leave(*WRAPS[2]), "z2": lambda: zero(cut, 128),
                "arr": lambda: copy("G", R("D1F", 0, 512, 16), R("ARR%d" % (t - 1))), "ml": coverlist, "pt": lambda: keys("P5"),
                "arb": lambda: copy("G", R("AB"), R("ARR%d" % (t - 1))), "nzm": lambda: mm(R("P7", 0, U), R("BKF"), R("AB")),
                "nz": lambda: relu(ON["nz"], R("NZ", c0 + B, c0 + 128), R("P7", 0, U), -1.0, 1.0)})
        if not last:
            every.update({
                "x15": lambda: gath(ON["x15"], R("X15"), WG, SL(0, t)),
                "tot0": lambda: totals(0, 4), "tot1": lambda: totals(4, 8), "tot2": lambda: totals(8, 12), "tot3": lambda: totals(12, 16),
                "rf": lambda: relu(ON["rf"], R("RF", 0, nl), R("P5", 0, nl), -1.0, 0.0), "rb": lambda: copy(ON["rb"], R("RB"), R("RF")),
                "short": short, "uu": lambda: act(R("UU"), R("P5", 0, 128), F.Sign, -1.0),
                "zc": lambda: relu(ON["zc"], R("ZC", 0, 128), R("P5", 0, 128), 1.0, 0.0),
                "num": lambda: scan(R("ZC", 128, 256), R("UU"), R("ONE", 0, 128), A.add, A.add),
                "vz2": lambda: vtr(R("ZT"), R("ZC")), "turnz": slots_turn,
                "ol": lambda: copy("V", R("OL"), R("P5", 0, 8), 0.5, -1.0), "sb": lambda: fill("S", R(sl, 0, U), -MAGIC), "put": put,
                "so": lambda: copy(ON["so"], so, R(sl, 0, U), 1.0, MAGIC), "send": send, "needs": lambda: needs("S", t + 1),
                "cov": lambda: covers(t + 1), "vm": lambda: vtr(R("MT"), R("MH")), "turn": lambda: covers_turn("P5"),
                "ow0": lambda: open_wrap(t + 1, *WRAPS[0]), "ow1": lambda: open_wrap(t + 1, *WRAPS[1]), "ow2": lambda: open_wrap(t + 1, *WRAPS[2]),
                "olist": lambda: open_lists(t + 1)})
        for name in ORDER:
            if name in every:
                every[name]()

    dma("Y", T.YC[:, :], T.W[0:128:16, 0:S], [R("W", 0, S)], [R("YC")])
    copy("V", R("YI"), R("YC"), 65536.0)
    ts(R("YJ"), R("YI"), 2047, A.bitwise_and)
    copy("V", R("YO"), R("YJ"), -1.0, 2047.0)
    dma("Y", T.y[:, :], T.YO[:, :], [R("YO")], [])
    for s in sorted(total):
        if known["G"].get(s, 0) < total[s]:
            g.wait_ge(T.sem[s], total[s])
